import numpy as np, ml_dtypes
CORES = [10,34,74,98]
N = 4
BF = ml_dtypes.bfloat16
P, BK, W, SH, NB, EV = 256, 8192, 8, 3, 4096, 4
LV, AR, LIVE = 48, 64, 448
def group():
    return np.arange(8)[None, :, None]
def event(bm, cs, ls, e, sd, t):
    q = e >> 16; u = e & 65535; g = group()
    m = bm[q, g, u >> SH]; b = (m >> 5) + ((u & (W - 1)) >= (m & 31))
    c = cs.reshape(N, 8, 16, NB)[q, g, :, b]
    k = np.sum(c <= ((sd >> (4 * t)) & 4095)[..., None], axis=-1)
    return c, np.maximum(e - ls.reshape(N, 8, 16, NB)[q, g, k, b].astype(np.float32).astype(np.int64), 0)
def first(rng, key, on, cap):
    k = np.where(on, key, 9999); o = np.lexsort((rng.random(k.size), k)); s = k[o]; r = np.empty_like(o)
    r[o] = np.arange(s.size) - np.searchsorted(s, s); return on & (r < cap)
def plant(rng, d, u, sd):
    e = u + 65536 * np.arange(N)[:, None, None]; d["en"] = e.astype(np.int32); g = np.broadcast_to(group(), e.shape).ravel()
    for t in range(EV - 1):
        s = sd + (rng.integers(0, 16, sd.shape) << (8 + 4 * t)); v = event(d["bm"], d["cs"], d["ls"], e, s, t)[1]
        a = (e >> 16).ravel(); z = (v >> 16).ravel()
        ok = first(rng, z * 8 + g, first(rng, (a * N + z) * 8 + g, a != z, LV), AR)
        no = ((a != z) & ~ok).reshape(e.shape); sd = np.where(no, sd, s); e = np.where(no, e, v)
    d["sd"] = sd.astype(np.int32); return d
def sections(c):
    return c.reshape(N, 128, NB).astype(np.int32)
def losses(v):
    v[:, :, 0] = 0; return v.reshape(N, 128, NB).astype(np.float32).astype(BF)
def setup_inputs(rng):
    h = np.zeros((N, 8, BK), np.int64); h[:, :, -1] = 1
    np.put_along_axis(h[..., :-1], np.argsort(rng.random((N, 8, BK - 1)), axis=-1)[..., :NB - 2], 1, -1)
    bm = (np.cumsum(h, axis=-1) - h) * 32 + np.where(h == 1, rng.integers(0, W, h.shape), W)
    c = np.sort(rng.integers(256, 4097, (N, 8, 16, NB)), axis=2); c[:, :, 15] = rng.integers(4096, 8192, (N, 8, NB))
    v = rng.integers(0, 256, c.shape) << rng.integers(0, 10 + 1, c.shape)
    d = {"bm": bm.astype(np.int32), "cs": sections(c), "ls": losses(v), "en": None, "sd": None}
    return plant(rng, d, rng.integers(0, 65536, (N, 8, P)), rng.integers(0, 256, (N, 8, P)))
def setup_inputs_full(rng):
    d = setup_inputs(rng); v = losses(rng.integers(64, 256, (N, 8, 16, NB)) * 512); d["ls"][1:] = v[1:]
    return plant(rng, d, rng.integers(0, 65536, (N, 8, P)), rng.integers(0, 256, (N, 8, P)))
def setup_inputs_ends(rng):
    d = setup_inputs(rng); m = d["bm"]; n = (N, 8, P)
    d["bm"] = np.where((m & 31) < W, (m >> 5) * 32 + rng.choice(np.array([0, 1, W - 1]), m.shape), m).astype(np.int32)
    c = 256 * np.sort(rng.integers(1, 17, (N, 8, 16, NB)), axis=2); c[:, :, 15] = rng.choice(np.array([4096, 8191]), (N, 8, NB)); d["cs"] = sections(c)
    d["ls"] = losses(rng.choice(np.array([0, 1, 1, 2, 255, 32768, 65280, 65536, 131072, 65536 * N]), c.shape))
    u = W * rng.integers(0, BK, n) + rng.choice(np.array([0, 1, W - 1]), n)
    u = np.where(rng.random(n) < 0.25, rng.choice(np.array([0, 1, 65534, 65535]), n), u)
    return plant(rng, d, u, np.zeros(n, np.int64))
def setup_inputs_still(rng):
    d = setup_inputs(rng); w = (N, 8, 16, NB)
    c = np.sort(rng.integers(0, 4097, w), axis=2); c[:, :, 15] = rng.integers(4096, 8192, (N, 8, NB)); d["cs"] = sections(c)
    d["ls"] = rng.integers(1, 256, w).reshape(N, 128, NB).astype(np.float32).astype(BF)
    return plant(rng, d, rng.integers(4096, 65536, (N, 8, P)), rng.integers(0, 256, (N, 8, P)))
def setup_inputs_spread(rng):
    d = setup_inputs(rng); w = (N, 8, 16, NB)
    d["bm"] = ((rng.random((N, 8, BK)) ** 4 * (NB - 1)).astype(np.int64) * 32 + rng.integers(0, W + 1, (N, 8, BK))).astype(np.int32)
    c = 256 + (rng.random(w) ** 3 * 7936).astype(np.int64); c[:, :, 15] = np.maximum(c[:, :, 15], 4096); d["cs"] = sections(c)
    d["ls"] = losses((rng.random(w) ** 4 * 256).astype(np.int64) << rng.integers(0, 10 + 1, w))
    return plant(rng, d, (rng.random((N, 8, P)) ** 4 * 65536).astype(np.int64), rng.integers(0, 256, (N, 8, P)))
def check_inputs(d):
    bad = []; m = d["bm"]; c = d["cs"].reshape(N, 8, 16, NB); v = d["ls"].astype(np.float32); e = d["en"].astype(np.int64); s = d["sd"].astype(np.int64)
    if not ((m >= 0) & ((m >> 5) <= NB - 2) & ((m & 31) <= W)).all(): bad.append("buckets")
    if not ((c >= 0) & (c <= 8191)).all() or not (c[:, :, 15] >= 4096).all(): bad.append("sections")
    if not ((v >= 0) & (v <= 65536 * N) & (v == np.floor(v))).all(): bad.append("losses")
    if not ((e >> 16) == np.arange(N)[:, None, None]).all(): bad.append("energies")
    if not ((s >= 0) & (s < 16 ** (EV + 1))).all(): bad.append("seeds")
    if bad: return bad
    for t in range(EV - 1):
        a = e >> 16; e = event(m, d["cs"], d["ls"], e, s, t)[1]; z = e >> 16
        n = np.bincount(((a * N + z) * 8 + group()).ravel(), minlength=N * N * 8).reshape(N, N, 8)
        if (n[~np.eye(N, dtype=bool)] > LV).any(): bad.append("leavers")
        if (np.sum(n, axis=0) > LIVE).any(): bad.append("live")
    return sorted(set(bad))
def reference(bm, cs, ls, en, sd):
    e = en.astype(np.int64); s = sd.astype(np.int64); tally = np.zeros((N, 8, P, 16), np.int64)
    for t in range(EV):
        c, e = event(bm, cs, ls, e, s, t)
        tally += c
    return {"y": tally.transpose(0, 1, 3, 2).reshape(N, 128, P).astype(np.float32)}

@@ -1,0 +1,808 @@
+from concourse.bass import DstId, RemoteDMATransfer
+from concourse.mybir import AluOpType as A, ActivationFunctionType as AF
+
+N, CAP, EV, RES = 4, 48, 4, 16
+BIG = 131072.0
+LOW = -524288.0
+TRW = 1456
+ZF = "VVVSSSGG"
+LOOKS, ROUNDS = (0.4, 0.5, 0.55, 0.6, 0.65, 0.7, 0.8), 6
+C = dict(cyc=1.0e-3, same=0.10, cross=0.17, dissue=0.06, dlat=0.6, drate=300e3, rissue=0.7, rstart=0.6, rhop=0.6,
+         rrate=60e3, first=1.4, gg=1.5, sg=3.5)
+
+SCRATCH = {}
+for _n, _w, _t in (
+        ("bmr", 512, "int32"), ("bmh", 512, "int32"), ("kt", 512, "float32"), ("t5", 512, "float32"), ("hi", 512, "bfloat16"),
+        ("lo", 512, "bfloat16"), ("bmp", 1024, "bfloat16"), ("win", 8192, "bfloat16"), ("one", 128, "bfloat16"),
+        ("zz", 1024, "bfloat16"), ("nb", 128, "bfloat16"),
+        ("s89", 256, "bfloat16"), ("sel", 512, "bfloat16"), ("csb", 4112, "int32"), ("lsb", 4112, "bfloat16"),
+        ("mg4", 128, "bfloat16"), ("bk4", 128, "bfloat16"), ("lb4", 512, "bfloat16"), ("lb4f", 512, "float32"),
+        ("lid", 512, "bfloat16"), ("lbe", 512, "bfloat16"), ("bkf", 128, "float32"), ("fz", 256, "float32"),
+        ("s5", 8, "float32"), ("dg", 512, "int32"),
+        ("nm", 112, "bfloat16"), ("rq", 112, "float32"), ("m4", 112, "float32"),
+        ("nma", 144, "bfloat16"), ("jm", 256, "float32"), ("dm", 256, "float32"), ("r16", 144, "float32"),
+        ("enw", 16, "int32"), ("sdw", 16, "int32"), ("wi", 16, "int32"), ("iw", 80, "int32"),
+        ("ge", 256, "float32"), ("gv", 256, "float32"), ("gs", 256, "bfloat16"),
+        ("gm", 256, "float32"), ("ms", 256, "bfloat16"), ("pl", 256, "bfloat16"), ("ki", 256, "bfloat16"),
+        ("pi", 4, "int32"), ("ci", 16, "int32"), ("jcl", 16, "uint16"), ("prm", 16, "uint16"), ("j16", 16, "float32"),
+        ("oh", 16, "float32"), ("cc", 64, "float32"), ("mi", 128, "bfloat16"), ("idb", 128, "bfloat16"),
+        ("nu", 128, "bfloat16"), ("dp", 128, "bfloat16"), ("k48", 96, "bfloat16"), ("kx", 96, "bfloat16"),
+        ("nt", 128, "bfloat16"), ("bv", 384, "bfloat16"), ("br", 384, "bfloat16"), ("be", 128, "bfloat16"),
+        ("trn", 32, "float32"), ("trd", 32, "float32"), ("rm", 96, "float32"), ("th", 216, "bfloat16"), ("ft", 216, "bfloat16"),
+        ("sg", 1024, "float32"), ("gl", 768, "bfloat16"), ("z", 704, "bfloat16"), ("tal", 704, "float32"),
+        ("bl", 64, "float32"), ("le0", 192, "uint16"),
+        ("le1", 144, "uint16"), ("le2", 96, "uint16"), ("li0", 12, "uint16"), ("li1", 10, "uint16"), ("li2", 6, "uint16"),
+        ("ll0", 154, "uint16"), ("ll1", 102, "uint16"), ("ll2", 52, "uint16"), ("er", 288, "uint16"), ("il", 18, "uint16"),
+        ("lr", 154, "uint16"), ("ert", 64, "float32"), ("dqi", 112, "float32"), ("ye0", TRW, "float32"), ("ye1", TRW, "float32"),
+        ("ye2", TRW, "float32"), ("yl", TRW, "float32"), ("ac", 256, "float32"), ("yo", 256, "float32"),
+        ("sw0", 768, "bfloat16"), ("sw1", 768, "bfloat16"), ("sw2", 768, "bfloat16"), ("mk", 256, "bfloat16")):
+    SCRATCH[_n] = ("sbuf", [128, _w], _t)
+for _k in "EFA":
+    for _n, _w, _t in (("of", 64, "uint16"), ("bn", 32, "uint16"), ("yy", 288, "bfloat16"),
+                       ("in", 256, "bfloat16"), ("xx", 256, "bfloat16"), ("vr", 256, "float32"),
+                       ("tw", 544, "float32"), ("xf", 128, "bfloat16")):
+        SCRATCH[_n + _k] = ("sbuf", [128, _w], _t)
+PS = ("E0", "E1", "F0", "F1", "A0", "A1", "psZ", "psI")
+for _k in PS:
+    SCRATCH[_k] = ("psum", [128, 512], "float32")
+
+SEMAPHORES = (["cV", "cP", "cS", "cG", "snt", "rx0", "rx1", "rx2"] + [a + str(s) for a in ("ri", "re", "rl") for s in range(3)]
+              + ["d%d" % i for i in range(16)])
+
+
+def clean(regs):
+    return [(r[0], (0, 512, 1)) if r[0] in PS else (r[0], tuple(r[1:4])) for r in regs]
+
+
+def meet(a, b):
+    return a[0] < b[1] and b[0] < a[1] and (a[2] != b[2] or (a[0] - b[0]) % a[2] == 0)
+
+
+def within(a, b):
+    return b[0] <= a[0] and a[1] <= b[1] and (b[2] == 1 or (a[2] == b[2] and (a[0] - b[0]) % a[2] == 0))
+
+
+def tracker(g, T):
+    qs = {"V": g.vector, "P": g.tensor, "S": g.scalar, "Y": g.sync, "G": g}
+    cnt, acc, nd = {}, {}, [0]
+    know = {q: {} for q in qs}
+
+    def need(q, reads, writes):
+        out = []
+        for kind, regs in (("r", clean(reads)), ("w", clean(writes))):
+            for b, c in regs:
+                for e in acc.get(b, []):
+                    if meet(e[0], c):
+                        if b in PS:
+                            if e[2] != q or (q != "P" and "w" in (kind, e[1])):
+                                out.append(e)
+                        elif "w" in (kind, e[1]):
+                            out.append(e)
+        return out
+
+    def wait(q, deps):
+        k = know[q]
+        top, imp = {}, {}
+        for e in deps:
+            top[e[3]] = max(top.get(e[3], 0), e[4])
+            for s, v in e[5].items():
+                if s != e[3]:
+                    imp[s] = max(imp.get(s, 0), v)
+        for s, v in top.items():
+            if k.get(s, 0) >= v or imp.get(s, 0) >= v:
+                continue
+            qs[q].wait_ge(T.sem[s], v)
+        for e in deps:
+            k[e[3]] = max(k.get(e[3], 0), e[4])
+            for s, v in e[5].items():
+                k[s] = max(k.get(s, 0), v)
+
+    def note(q, reads, writes, sem, val, snap):
+        for kind, regs in (("r", clean(reads)), ("w", clean(writes))):
+            for b, c in regs:
+                l = acc.setdefault(b, [])
+                if kind == "w":
+                    l[:] = [e for e in l if not within(e[0], c)]
+                l.append((c, kind, q, sem, val, snap))
+
+    def issue(o):
+        q, reads, writes = o["q0"], o["r"], o["w"]
+        if o["k"] == "op":
+            wait(q, need(q, reads, writes))
+            for f in o["f"][:-1]:
+                f()
+            s = "c" + q
+            o["f"][-1]().then_inc(T.sem[s], 1)
+            cnt[s] = cnt.get(s, 0) + 1
+            note(q, reads, writes, s, cnt[s], dict(know[q]))
+        elif o["k"] == "dma":
+            s = "d%d" % nd[0]
+            nd[0] += 1
+            wait(q, need(q, reads, writes))
+            for f in o["f"]:
+                f().then_inc(T.sem[s], 16)
+            cnt[s] = 16 * len(o["f"])
+            note("D", reads, writes, s, cnt[s], dict(know[q]))
+        elif o["k"] == "land":
+            note("R", [], writes, o["sem"], o["val"], {})
+            cnt[o["sem"]] = o["val"]
+        else:
+            wait(q, need(q, reads, []))
+            o["f"][0]()
+            cnt["snt"] = cnt.get("snt", 0) + o["val"]
+
+    def finish():
+        for s, v in cnt.items():
+            g.wait_ge(T.sem[s], v)
+
+    return issue, finish
+
+
+def links(ops):
+    acc = {}
+    for i, o in enumerate(ops):
+        d, q = {}, o["q"]
+        for kind, regs in (("r", clean(o["r"])), ("w", clean(o["w"]))):
+            for b, c in regs:
+                for e in acc.get(b, []):
+                    if meet(e[0], c) and e[3] != i and not (o.get("com") == b and ops[e[3]].get("com") == b):
+                        same = e[2] == q and q != "D"
+                        if b in PS:
+                            lat = (C["same"] if q != "P" and "w" in (kind, e[1]) else 0.0) if same else C["cross"]
+                        elif "w" in (kind, e[1]):
+                            lat = C["same"] if same else C["cross"]
+                        else:
+                            continue
+                        d[e[3]] = max(d.get(e[3], 0.0), lat)
+        for kind, regs in (("r", clean(o["r"])), ("w", clean(o["w"]))):
+            for b, c in regs:
+                l = acc.setdefault(b, [])
+                if kind == "w" and o.get("com") != b:
+                    l[:] = [e for e in l if not within(e[0], c)]
+                l.append((c, kind, q, i))
+        o["d"] = d
+
+
+def schedule(progs):
+    ops, base = [], []
+    for p in progs:
+        links(p)
+        base.append(len(ops))
+        ops += p
+    n = len(ops)
+    rank = [r for r, p in enumerate(progs) for _ in p]
+    dep, sends = [], {}
+    for r, p in enumerate(progs):
+        for i, o in enumerate(p):
+            dep.append({base[r] + j: lat for j, lat in o["d"].items()})
+            if o["k"] == "send":
+                for d in o["to"]:
+                    sends.setdefault((d, o["sem"]), []).append((base[r] + i, C["rstart"] + o["by"] / C["rrate"] + C["rhop"]))
+    for i, o in enumerate(ops):
+        if o["k"] == "land":
+            for j, lat in sends[(rank[i], o["sem"])]:
+                dep[i][j] = lat
+    into = [list(d.items()) for d in dep]
+    out = [[] for _ in range(n)]
+    for i in range(n):
+        for j, lat in into[i]:
+            out[j].append((i, lat))
+    left, last, way = [len(l) for l in out], [i for i in range(n) if not out[i]], [0.0] * n
+    for i in last:
+        way[i] = ops[i]["t"] + max([way[j] + lat for j, lat in out[i]] + [0.0])
+        for j, _ in into[i]:
+            left[j] -= 1
+            if left[j] == 0:
+                last.append(j)
+    best = None
+    for look in LOOKS:
+        pri = way
+        for _ in range(ROUNDS):
+            end, seq, fin = arrange(ops, rank, into, out, pri, look)
+            if best is None or end < best[0]:
+                best = (end, seq)
+            pri = arrange(ops, rank, out, into, fin, look)[2]
+    return [[ops[i] for i in l] for l in best[1]]
+
+
+def arrange(ops, rank, into, out, pri, look):
+    n = len(ops)
+    deg, ready, fin = [len(l) for l in into], [0.0] * n, [0.0] * n
+    pool, free, dfree, first = {}, {}, [0.0] * N, set()
+    res = [[] for _ in range(N)]
+
+    def enter(j):
+        pool.setdefault((rank[j], ops[j]["q0"]), []).append(j)
+
+    def done(i, t):
+        st = [(i, t)]
+        while st:
+            i, t = st.pop()
+            fin[i] = t
+            for j, lat in out[i]:
+                ready[j] = max(ready[j], t + lat)
+                deg[j] -= 1
+                if deg[j] == 0:
+                    if ops[j]["k"] == "land":
+                        res[rank[j]].append(j)
+                        st.append((j, ready[j]))
+                    else:
+                        enter(j)
+
+    for i in range(n):
+        if not into[i]:
+            enter(i)
+    while True:
+        best = None
+        for key, l in pool.items():
+            if not l:
+                continue
+            f = free.get(key, 0.0)
+            t0 = max(f, min(ready[i] for i in l))
+            c = max((i for i in l if ready[i] <= t0), key=lambda i: (pri[i], -i))
+            lim = t0 + ops[c]["t"] * look
+            for i in l:
+                if t0 < ready[i] < lim and pri[i] > pri[c] + (ready[i] - t0):
+                    c, lim = i, ready[i]
+            s = max(f, ready[c])
+            if best is None or s < best[0]:
+                best = (s, key, c)
+        if best is None:
+            break
+        s, key, c = best
+        pool[key].remove(c)
+        o, r = ops[c], key[0]
+        e = s + o["t"]
+        if o["k"] == "send" and r not in first:
+            first.add(r)
+            e += C["first"]
+        free[key] = e
+        res[r].append(c)
+        if o["k"] == "dma":
+            dfree[r] = max(dfree[r], e + C["dlat"]) + o["by"] / C["drate"]
+            e = dfree[r] + C["dlat"]
+        done(c, e)
+    return max(fin), res, fin
+
+
+def program(g, q, T, topo):
+    ops, cols = [], {}
+    core = T.cores[q]
+    V, P, S = g.vector, g.tensor, g.scalar
+    NA = N - 1 - q
+    AC = 3 * NA
+    CT = RES + AC * 2
+    Q1 = q + 1
+    OFF = BIG - 8192.0 * q - 0.4375
+    if q == 0:
+        OFF = -0.4375
+    cy = C["cyc"]
+
+    def op(qq, fns, reads, writes, t, **kw):
+        o = dict(k="op", q=qq, q0=qq, f=fns, r=reads, w=writes, t=t)
+        o.update(kw)
+        ops.append(o)
+
+    def B(n, lo=0, hi=None, step=1):
+        return (n, lo, SCRATCH[n][1][1] if hi is None else hi, step)
+
+    def ap(r):
+        if not isinstance(r, tuple):
+            return r
+        return T[r[0]][:, r[1]:r[2]] if r[3] == 1 else T[r[0]][:, r[1]:r[2]:r[3]]
+
+    def wd(r):
+        return (r[2] - r[1] + r[3] - 1) // r[3]
+
+    def tv(n, f):
+        return cy * max(64, n * f)
+
+    def short(*rs):
+        return all(SCRATCH[r[0]][2] in ("bfloat16", "uint16") for r in rs)
+
+    def ts(o, i, s1, s2, op0, op1=None):
+        rd = [i] + [s for s in (s1, s2) if isinstance(s, tuple)]
+        t = tv(wd(o), 0.5 if short(o, i) else 1)
+        if op1 is None:
+            op("V", [lambda: V.tensor_scalar(ap(o), ap(i), ap(s1), None, op0)], rd, [o], t)
+        else:
+            op("V", [lambda: V.tensor_scalar(ap(o), ap(i), ap(s1), ap(s2), op0, op1)], rd, [o], t)
+
+    def tt(o, a, b, f):
+        op("V", [lambda: V.tensor_tensor(ap(o), ap(a), ap(b), f)], [a, b], [o], tv(wd(o), 1 if a[0] in PS or b[0] in PS else 2))
+
+    def ttg(o, w, l, b, f):
+        op("V", [lambda: V.tensor_tensor(ap(o), ap(w).indirect(ap(l)), ap(b), f)], [w, l, b], [o], 0.05 + cy * C["gg"] * wd(o))
+
+    def cp(o, i):
+        op("V", [lambda: V.tensor_copy(ap(o), ap(i))], [i], [o], tv(wd(o), 0.5 if short(o, i) else 1))
+
+    def cpg(o, w, l, eng="V"):
+        if eng == "V":
+            op("V", [lambda: V.tensor_copy(ap(o), ap(w).indirect(ap(l)))], [w, l], [o], 0.05 + cy * C["gg"] * wd(o))
+        else:
+            op("S", [lambda: S.activation(ap(o), ap(w).indirect(ap(l)), AF.Copy)], [w, l], [o], 0.065 + cy * C["gg"] * wd(o))
+
+    def sca(w, l, i):
+        op("V", [lambda: V.tensor_copy(ap(w).indirect(ap(l)), ap(i))], [l, i], [w], 0.05 + cy * C["sg"] * wd(i), com=w[0])
+
+    def scan(o, m, i, op0=A.add, op1=A.max, f=1):
+        op("V", [lambda: V.tensor_tensor_scan(ap(o), ap(m), ap(i), 0.0, op0, op1)], [m, i], [o], tv(wd(o), f))
+
+    def fill(o, c):
+        op("V", [lambda: V.memset(ap(o), c)], [], [o], tv(wd(o), 0.5 if short(o) else 1))
+
+    def act(o, i, scale=1.0, bias=None, func=AF.Identity):
+        t = 0.06 + cy * wd(o)
+        more = [x for x in (scale, bias) if isinstance(x, tuple)]
+        if bias:
+            op("S", [lambda: S.activation(ap(o), ap(i), func, bias=ap(bias), scale=ap(scale))], [i] + more, [o], t)
+        elif more:
+            op("S", [lambda: S.activation(ap(o), ap(i), func, scale=ap(scale))], [i] + more, [o], t)
+        else:
+            op("S", [lambda: S.activation(ap(o), ap(i), AF.Copy, scale=scale)], [i], [o], t)
+
+    def iota(o, pat, base, ch):
+        kw = {} if SCRATCH[o[0]][2] == "int32" else {"allow_small_or_imprecise_dtypes": True}
+        op("G", [lambda: g.iota(ap(o), pat, base, ch, **kw)], [], [o], 0.13 + 2 * cy * wd(o))
+
+    def aff(o, i, pat, cmp, base, ch, other=0.0):
+        op("G", [lambda: g.affine_select(ap(o), ap(i), pat, cmp, other, base, ch)], [i], [o], 0.17 + 2 * cy * wd(o))
+
+    def mm(o, lst, a=0, b=None):
+        n = len(lst)
+        part = list(enumerate(lst))[a:b]
+        fns = [lambda k=k, l=l, r=r: P.matmul(ap(o), ap(l), ap(r), k == 0, k == n - 1) for k, (l, r) in part]
+        t = sum(0.03 + cy * max(64, wd(r)) * (1 if short(r) else 4) for k, (l, r) in part)
+        op("P", fns, [x for _, p in part for x in p], [o], t)
+
+    def dma(qq, fns, reads, writes, by):
+        op(qq, fns, reads, writes, C["dissue"] * len(fns), k="dma", q="D", by=by)
+
+    def load(qq, dst, name):
+        dma(qq, [lambda: (g.sync if qq == "Y" else g.scalar).dma_start(T[dst[0]][:, dst[1]:dst[2]], T[name][:, :])], [], [dst],
+            128 * wd(dst) * (2 if short(dst) else 4))
+
+    def col(name):
+        if name not in cols:
+            cols[name] = len(cols)
+        k = cols[name]
+        return B("cc", k, k + 1)
+
+    def oh(k):
+        return B("oh", k, k + 1)
+
+    def M3(n, k):
+        return B(n, 128 * k, 128 * k + 128)
+
+    bk, idb = B("bk4"), B("idb")
+
+    def quad(lname, src, s0, s1):
+        return ([(idb, B("nm", 0, (s1 - s0) // 4))]
+                + [(M3(lname, r), (src, s0 + r, s1, 4)) for r in range(4)])
+
+    def unquad(ps, n, o):
+        scan(B(o, 0, 4 * n), B("rq", 0, 4 * n), B(ps, 0, 4 * n))
+        return B(o, 3, 4 * n, 4)
+
+    def low(n):
+        return (idb, B("nma", 0, n))
+
+    def diag(ps, n, o):
+        scan(B(o, 0, n), B("r16", 0, n), B(ps, 0, n))
+        return B(o, 15, n, 16)
+
+    load("Y", B("enw"), "en")
+    load("S", B("bmr"), "bm")
+    load("Y", B("sdw"), "sd")
+    load("Y", B("csb", 0, 4096), "cs")
+    load("Y", B("lsb", 0, 4096), "ls")
+    iota(B("pi", 0, 1), [[0, 1]], 0, 1)
+    iota(B("j16"), [[1, 16]], 0, 0)
+    iota(B("jm"), [[0, 16], [1, 16]], 0, 0)
+    iota(B("ci"), [[1, 16]], 0, 0)
+    iota(B("mg4"), [[16, 8], [0, 16]], 0, 0)
+    iota(B("mi"), [[1, 128]], 0, 0)
+    iota(B("m4"), [[0, 28], [1, 4]], 0, 0)
+    fill(B("one"), 1.0)
+    fill(B("zz"), 0.0)
+    for k, e in enumerate(ZF):
+        w = B("win", 1024 * k, 1024 * k + 1024)
+        if e == "V":
+            fill(w, 0.0)
+        elif e == "S":
+            act(w, B("zz"))
+        else:
+            iota(w, [[0, 1024]], 0, 0)
+    ts(B("pi", 1, 2), B("pi", 0, 1), 15, None, A.bitwise_and)
+    ts(B("pi", 2, 3), B("pi", 0, 1), 2, 3, A.arith_shift_right, A.bitwise_and)
+    cp(col("p"), B("pi", 0, 1))
+    cp(col("o"), B("pi", 1, 2))
+    cp(col("o4"), B("pi", 2, 3))
+    tt(col("g16"), col("p"), col("o"), A.subtract)
+    ts(B("oh"), B("j16"), col("o"), None, A.is_equal)
+    ts(B("dm"), B("jm"), col("o"), None, A.is_equal)
+    cp(B("jcl"), B("ci"))
+    ts(bk, B("mg4"), col("g16"), None, A.is_equal)
+    ts(idb, B("mi"), col("p"), None, A.is_equal)
+    tt(B("s5", 0, 5), B("oh", 0, 5), B("oh", 5, 10), A.add)
+    sc = B("s5", 4, 5)
+    for k in (3, 2, 1, 0):
+        act(col("s%d" % k), sc, 0.0625, B("s5", k, k + 1))
+        sc = col("s%d" % k)
+    ts(col("h9"), col("o"), 9.0, -0.5, A.is_le, A.mult)
+    act(col("bi"), sc, 0.5, col("h9"))
+    for t in range(3):
+        act(col("n%d" % t), oh(6 + t), 16.0, oh(5 + t))
+        act(col("m%d" % t), oh(7 + t), 256.0, col("n%d" % t))
+        act(M3("bv", t), bk, col("m%d" % t))
+    act(col("bA"), oh(15), float(q), oh(13))
+    ts(col("bb"), col("o"), -16384.0, 32.0, A.mult, A.add)
+    if q:
+        act(B("nb"), bk, -1.0)
+        aff(B("nt"), B("nb"), [[-1, 128]], A.is_gt, 0, 1)
+        aff(B("nu"), B("nt"), [[-1, 128]], A.not_equal, 0, 1, -2048.0)
+        ts(col("p1"), col("p"), 1.0, None, A.add)
+        act(B("dp"), idb, col("p1"))
+    act(B("lb4f"), B("zz", 0, 512))
+    act(B("lb4"), B("zz", 0, 512))
+    for r in range(4):
+        act(B("lb4f", 129 * r, 128 * r + 128, 4), B("bk4", r, 128, 4))
+        act(B("lb4", 129 * r, 128 * r + 128, 4), B("bk4", r, 128, 4))
+    act(B("bkf"), bk)
+    aff(M3("fz", 0), B("bkf"), [[0, 8], [-1, 16]], A.is_ge, 4, 0)
+    aff(M3("fz", 1), B("bkf"), [[0, 8], [1, 16]], A.is_ge, -5, 0)
+    iota(B("kt"), [[-32, 512]], 0, 0)
+    iota(B("pl"), [[1, 16], [16, 16]], 0, 0)
+    aff(M3("s89", 0), B("one"), [[0, 8], [-1, 16]], A.is_ge, 7, 0)
+    aff(M3("s89", 1), B("one"), [[0, 8], [1, 16]], A.is_ge, -8, 0)
+    for k in range(2):
+        aff(M3("sel", k), M3("s89", 0), [[-16, 8], [-2, 16]], A.is_equal, -k, 1)
+        aff(M3("sel", 2 + k), M3("s89", 1), [[-16, 8], [-2, 16]], A.is_equal, 16 - k, 1)
+    if q:
+        iota(B("k48", 0, Q1 * CT), [[0, CT], [CAP, Q1]], 0, 0)
+        iota(B("trn", 0, CT), [[16, CT]], CAP * q - 2048, 0)
+        act(B("k48", q, Q1 * CT, Q1), B("trn", 0, CT))
+        act(B("br"), B("zz", 0, 384))
+        for j in range(3):
+            act(B("br", 129 * j + 10, 128 * j + 128, 16), B("bk4", 10 + j, 128, 16))
+    if NA:
+        iota(B("trd"), [[16, 32]], -1024, 1)
+    ts(B("nm"), B("m4"), col("o4"), LOW, A.not_equal, A.mult)
+    ts(B("rq"), B("m4"), 0.0, 2 * LOW, A.is_equal, A.mult)
+    mi0, mi1, mh0, mb0, e7 = [B("iw", 16 * k, 16 * k + 16) for k in range(5)]
+    ts(B("wi"), B("enw"), 12, 15, A.arith_shift_right, A.bitwise_and)
+    ttg(B("gs"), B("wi"), B("jcl"), B("dm"), A.mult)
+    mm(B("A0", 0, 256), [(bk, B("gs"))])
+    ts(mi0, B("enw"), 3, 511, A.arith_shift_right, A.bitwise_and)
+    cp(B("ofE", 0, 16), mi0)
+    ts(e7, B("enw"), 7, None, A.bitwise_and)
+    ts(B("ms"), B("A0", 0, 256), col("o"), None, A.is_equal)
+    L = quad("lb4f", "gm", 0, 256)
+    mm(B("E0", 0, 64), L, 0, 1)
+    ttg(B("gm"), B("bmr"), B("ofE", 0, 16), B("ms"), A.mult)
+    mm(B("E0", 0, 64), L, 1)
+    ttg(B("ge"), B("enw"), B("jcl"), B("dm"), A.mult)
+    ttg(B("gv"), B("sdw"), B("jcl"), B("dm"), A.mult)
+    Z = [(M3("fz", 0), B("ge")), (M3("fz", 1), B("gv"))]
+    mm(B("F0", 0, 256), Z, 0, 1)
+    mm(B("F0", 0, 256), Z, 1, 2)
+    ts(B("dg", 0, 256), B("F0", 0, 256), sc, col("bi"), A.mult, A.add)
+    ts(B("dg", 256, 512), B("dg", 0, 256), 15, None, A.bitwise_and)
+    ts(B("ki"), B("pl"), oh(14), col("bA"), A.mult, A.add)
+    tt(B("z", 0, 256), B("dg", 256, 512), B("ki"), A.add)
+    cp(mi1, unquad("E0", 16, "twE"))
+    ts(mh0, mi1, 31, None, A.bitwise_and)
+    ts(mb0, mi1, 5, None, A.arith_shift_right)
+    tt(B("twE", 288, 304), mh0, e7, A.is_le)
+    tt(B("twE", 320, 336), mb0, B("twE", 288, 304), A.add)
+    cp(B("bnE", 0, 16), B("twE", 320, 336))
+    act(B("psZ"), B("kt"), bias=col("bb"))
+    ts(B("bmh"), B("bmr"), 31, None, A.bitwise_and)
+    tt(B("F1"), B("psZ"), B("bmr"), A.add)
+    act(B("t5"), B("bmh"), -5.0)
+    tt(B("psZ"), B("F1"), B("t5"), A.add)
+    act(B("hi"), B("psZ"))
+    fill(B("csb", 4096, 4112), 0)
+    fill(B("lsb", 4096, 4112), 0.0)
+    if q:
+        fill(B("rm", 0, Q1 * CT), 0.0)
+        fill(B("rm", 0, Q1 * CT, Q1), -2 * LOW)
+        fill(B("kx", 0, Q1 * CT), 0.0)
+        fill(B("kx", q, Q1 * CT, Q1), 1.0)
+        fill(B("ft"), 0.0)
+        for x in "EFA" if NA else "E":
+            fill(B("xf" + x), 0.0)
+        for t in range(3):
+            fill(B("sw%d" % t, 0, CAP * q), 0.0)
+    tt(B("lo"), B("psZ"), B("hi"), A.subtract)
+    mm(B("A1"), [(M3("sel", 0), B("hi")), (M3("sel", 2), B("lo"))])
+    act(B("bmp", 0, 512), B("A1"), 0.03125)
+    mm(B("psI"), [(M3("sel", 1), B("hi")), (M3("sel", 3), B("lo"))])
+    act(B("bmp", 512, 1024), B("psI"), 0.03125)
+    dma("Y", [lambda s=s: g.sync.dma_start(T.win[s::8, 1024 * s:1024 * s + 1024], T.bmp[s::8, :]) for s in range(8)],
+        [B("bmp"), B("win")], [B("win")], 262144)
+    wt = oh(4)
+    for k in (3, 2, 1, 0):
+        act(col("w%d" % k), wt, 16.0, oh(k))
+        wt = col("w%d" % k)
+    ts(col("f9"), col("o"), 10.0, None, A.is_ge)
+    ts(col("e9"), col("o"), 12.0, col("f9"), A.is_le, A.mult)
+    act(col("u1"), wt, 0.125, col("e9"))
+    if q:
+        act(col("cb"), oh(13), -BIG, col("u1"))
+    act(B("lbe"), B("lb4"), col("cb" if q else "u1"))
+    if NA:
+        ts(B("nma"), B("jm", 0, 144), col("o"), LOW, A.not_equal, A.mult)
+        ts(B("r16"), B("jm", 0, 144), 0.0, 2 * LOW, A.is_equal, A.mult)
+        act(B("be"), bk, col("cb" if q else "u1"))
+        act(col("u3"), oh(15), 256.0, oh(14))
+        act(col("cid"), oh(13), -2048.0, col("u3"))
+        act(B("lid"), B("lb4"), col("cid"))
+    ts(col("o16"), col("o"), 16.0, None, A.mult)
+    ts(B("prm"), B("ci"), col("o16"), None, A.add)
+    if q:
+        for n in ["ye%d" % s for s in range(q)] + ["yl"]:
+            iota(B(n, 256 * q, 256 * q + 256), [[0, 256]], 0, 0)
+
+    def tw(x, k, n):
+        return B("tw" + x, 288 + 32 * k, 288 + 32 * k + n)
+
+    def sg(t):
+        return B("sg", 256 * t, 256 * t + 256)
+
+    def vrep(x, t, s0, s1, copy):
+        o = B(x + "1", 256, 256 + s1 - s0)
+        mm(o, [(M3("bv", t), B("z", s0, s1))])
+        if copy:
+            act(B("vr" + x, 0, s1 - s0), o)
+
+    def buckets(x, src):
+        ts(B("of" + x, 0, wd(src)), src, 8191.0, 0.0, A.min, A.max)
+
+    def sums(x, row, c0, c1, fresh):
+        m = 16 * (c1 - c0)
+        if fresh:
+            return [low(m), (B("be"), B("z", 16 * c0, 16 * c1)), (bk, row)], m, 1
+        if m > 144:
+            return quad("lb4", row[0], 0, m), m // 4, 4
+        return [low(m), (bk, row)], m, 1
+
+    def wrapped(x, n, w):
+        return unquad(x + "0", n, "tw" + x) if w < 16 * n else diag(x + "0", w, "tw" + x)
+
+    def bins(x, c0, c1):
+        n = c1 - c0
+        m = 16 * n
+        yy, bn = B("yy" + x, 0, m), B("bn" + x, 0, n)
+        fresh = x == "A" and q
+        L, w, late = sums(x, yy, c0, c1, fresh)
+        mm(B(x + "0", 0, w), L, 0, len(L) - late)
+        cpg(yy, B("win"), B("of" + x, 0, n), "S" if m > 64 and x != "A" else "V")
+        mm(B(x + "0", 0, w), L, len(L) - late)
+        s = wrapped(x, n, w)
+        if fresh:
+            ts(bn, s, OFF, 4096.0, A.add, A.min)
+        else:
+            tt(tw(x, 0, n), s, B("bl", c0, c1), A.add)
+            ts(bn, tw(x, 0, n), 4096.0, 0.0, A.min, A.max)
+
+    def tally(x, t, c0, c1):
+        bn, o = B("bn" + x, 0, c1 - c0), B("tal", 16 * c0, 16 * c1)
+        if x == "E":
+            cpg(sg(t), B("csb"), bn, "S")
+        elif x == "A":
+            cpg(o, B("csb"), bn, "S")
+        else:
+            ttg(o, B("csb"), bn, o, A.add)
+
+    def event(x, t, c0, c1):
+        n, s0, s1 = c1 - c0, 16 * c0, 16 * c1
+        m = 16 * n
+        p0, p1, fresh = x + "0", x + "1", x == "A" or t == 0
+        row, zr, bn, hit = B("xx" + x, 0, m), B("z", s0, s1), B("bn" + x, 0, n), B("in" + x, 0, m)
+        ks, mp = B(p1, 0, m), B(p1, 256, 256 + m)
+        if x == "E" and t:
+            tally(x, t, c0, c1)
+            tt(hit, sg(t), mp, A.is_le)
+        else:
+            ttg(hit, B("csb"), bn, B("vr" + x, 0, m), A.is_le)
+        mm(ks, [(bk, hit)])
+        L, w, late = sums(x, row, c0, c1, x == "A")
+        if t == 0:
+            L[1:1] = [(M3("lbe", r), ("z", r, m, 4)) for r in range(4)]
+        mm(B(p0, 0, w), L, 0, len(L) - late)
+        if t == 0:
+            tally(x, t, c0, c1)
+            ts(B("mk", 0, m), ks, col("o"), -0.125, A.is_equal, A.mult)
+            ttg(row, B("lsb"), bn, B("mk", 0, m), A.mult)
+        else:
+            k = 256 * "EFA".index(x)
+            gl = B("gl", k, k + m)
+            cpg(gl, B("lsb"), bn, "S")
+            if x != "E":
+                tally(x, t, c0, c1)
+            ts(mp, ks, col("o"), -0.125, A.is_equal, A.mult)
+            tt(row, gl, mp, A.mult)
+        mm(B(p0, 0, w), L, len(L) - late)
+        en, off = wrapped(x, n, w), OFF
+        if t == 0:
+            ts(B("ofE", 0, RES), en, OFF, 8191.0, A.add, A.min)
+        if q == 0 and fresh:
+            ts(B("bl", c0, c1), en, OFF, -0.4375, A.add, A.max)
+            return
+        if not fresh:
+            tt(tw(x, 1, n), en, B("bl", c0, c1), A.add)
+            en, off = tw(x, 1, n), 0.0
+        if q == 0:
+            ts(B("bl", c0, c1), en, -0.4375, 0.0, A.max, A.add)
+            return
+        f0, a, b = 72 * t, c0 * Q1, c1 * Q1
+
+        def thr(s):
+            return 8192.0 * (s + 1 - q) - 0.5 - off
+
+        def to(s):
+            return B("ft", f0 + a + s, f0 + b, Q1)
+
+        def under(s, lo, hi):
+            return B("th", f0 + s * CT + lo, f0 + s * CT + hi) if s else B("ft", f0 + lo * Q1, f0 + hi * Q1, Q1)
+        for s in range(q):
+            ts(under(s, c0, c1), en, thr(s), None, A.is_lt)
+        pl = B(p0, 0, b - a)
+        L2 = [(idb, B("k48", a, b)), (B("dp"), B("kx", a, b)), (B("nu"), B("ft", f0 + a, f0 + b)), (bk, B("xf" + x, a, b))]
+        mm(pl, L2, 0, 2)
+        for s in range(q):
+            scan(B("xf" + x, s, b, Q1), under(s, 0, c1), under(s - 1, 0, c1) if s else B("zz", 0, c1), A.add, A.subtract, 0.5)
+        for s in range(1, q):
+            tt(to(s), under(s, c0, c1), under(s - 1, c0, c1), A.subtract)
+        mm(pl, L2, 2, 3)
+        mm(pl, L2, 3)
+        act(tw(x, 3, n), en, -16 * BIG, 16 * BIG * thr(q - 1), AF.Relu)
+        if fresh:
+            act(tw(x, 2, n), en, 1.0, off)
+            en = tw(x, 2, n)
+        tt(B("bl", c0, c1), en, tw(x, 3, n), A.add)
+        scan(B("tw" + x, 448, 448 + b - a), B("rm", 0, b - a), pl, A.add, A.min)
+        ts(B("of" + x, 32, 32 + n), B("tw" + x, 448 + q, 448 + b - a, Q1), 2047.0, None, A.add)
+        k = 8 if m > 144 else n
+        for i in range(0, n, k):
+            o, h = B("psZ", 16 * i, 16 * (i + k)), B("z", s0 + 16 * i, s0 + 16 * (i + k))
+            L3 = [(idb, h), (M3("br", t), B("xx" + x, 16 * i, 16 * (i + k)))]
+            mm(o, L3, 0, 1)
+            mm(o, L3, 1, 2)
+            act(h, o)
+        for i in range(0, n, k):
+            sca(B("sw%d" % t, 0, CAP * q + 16 * CT + 128), B("of" + x, 32 + i, 32 + i + k), B("z", s0 + 16 * i, s0 + 16 * (i + k)))
+
+    def split(s, kind):
+        d = list(range(s))[::-1] if kind == "rx" else list(range(s + 1, N))[::-1]
+        groups = {"rx": [[x] for x in d], "ri": [d]}.get(kind, [d[:2], d[2:]])
+        return [list(zip(x, {1: (8,), 2: (4, 4), 3: (4, 2, 2)}[len(x)])) for x in groups if x]
+
+    def width(s, d, kind):
+        return [w for x in split(s, kind) for y, w in x if y == d][0]
+
+    def send(src, dst, rsem):
+        for call in split(q, rsem[:2]):
+            sd = [(d, w, src(d, call[0][0]), dst(d, call[0][0])) for d, w in call]
+
+            def go(sd=sd):
+                e = topo.engines(core, T.cores[sd[0][0]])
+                tr, pos = [], 0
+                for d, w, a, b in sd:
+                    rid, pid, _ = topo.addr(T.cores[d])
+                    tr.append(RemoteDMATransfer(dst_ids=[DstId(rid=rid, pnc=pid)], remote_sem=T.sem[rsem], src=ap(a), dst=ap(b),
+                                                dma_engine_mask=sum(1 << k for k in e[pos:pos + w])))
+                    pos += w
+                g.remote_dma_fused(tr, local_sem=T.sem.snt)
+            op("G", [go], [x[2] for x in sd], [], C["rissue"], k="send", sem=rsem, to=[x[0] for x in sd],
+               by=256 * sum(wd(x[2]) for x in sd), val=sum(x[1] for x in sd))
+
+    def landed(sem, val, regs):
+        op("R", [], [], regs, 0.0, k="land", sem=sem, val=val)
+
+    def zcol(s, t, r):
+        return 16 * (RES + 3 * (N - 1 - s) * t) + CAP * (r - s - 1)
+
+    def places(n, out, k, ps, tmp):
+        er = B("ert", 32 * k, 32 * k + n)
+        tt(er, unquad(ps, n, tmp), B("trd", 0, n), A.min)
+        ts(B(out, 0, n), er, 2048.0, None, A.add)
+
+    for t in range(EV):
+        if t < 3:
+            if t == 2:
+                buckets("E", tw("E", 1, RES))
+            vrep("E", t, 0, 256, t == 0)
+            if t:
+                bins("E", 0, RES)
+            event("E", t, 0, RES)
+        if t == 2 and NA:
+            buckets("F", B("bl", RES, RES + AC))
+            vrep("F", t, 256, 256 + 16 * AC, True)
+            bins("F", RES, RES + AC)
+            event("F", t, RES, RES + AC)
+        if t == 3 and NA:
+            for a in (RES, RES + AC):
+                buckets("F", tw("F", 1, AC) if a == RES else B("bl", a, a + AC))
+                bins("F", a, a + AC)
+                tally("F", t, a, a + AC)
+                cp(B("er", 16 * (a - RES), 16 * (a - RES + AC)), B("tal", 16 * a, 16 * (a + AC)))
+            w = 16 * (AC + 3)
+            send(lambda d, m: B("er", CAP * (d - q - 1), CAP * (d - q - 1) + w), lambda d, m: B("le%d" % q, 0, w), "re%d" % q)
+        if t and NA:
+            c0 = RES + AC * (t - 1)
+            c1 = c0 + AC
+            zr = B("z", 16 * c0, 16 * c1)
+            n = 16 * AC
+            landed("rx%d" % (t - 1), sum(width(r, q, "rx") for r in range(q + 1, N)), [zr])
+            U = [low(n), (B("be"), zr)]
+            mm(B("A0", 0, n), U, 0, 1)
+            mm(B("A0", 0, n), U, 1)
+            if t < 3:
+                vrep("A", t, 16 * c0, 16 * c1, True)
+            ts(B("ofA", 0, AC), diag("A0", n, "twA"), OFF, 8191.0, A.add, A.min)
+            if q == 0:
+                ts(B("bl", c0, c1), B("twA", 15, n, 16), OFF, -0.4375, A.add, A.max)
+            bins("A", c0, c1)
+            if t < 3:
+                event("A", t, c0, c1)
+            else:
+                mm(B("A1", 0, 4 * AC), quad("lid", "z", 16 * c0, 16 * c1))
+                cpg(B("lr", AC, AC + n), B("csb"), B("bnA", 0, AC))
+                places(AC, "lr", 1, "A1", "dqi")
+                send(lambda d, m: B("lr", 0, AC + CAP * (m - q)), lambda d, m: B("ll%d" % q, 0, AC + CAP * (m - q)), "rl%d" % q)
+        if t < 3 and q:
+            send(lambda d, m: B("sw%d" % t, CAP * d, CAP * d + CAP), lambda d, m: B("z", zcol(d, t, q), zcol(d, t, q) + CAP), "rx%d" % t)
+        if NA and t == 2:
+            k = 2 * AC
+            mm(B("psI", 0, 4 * k), quad("lid", "z", 256, 256 + 16 * k))
+            places(k, "il", 0, "psI", "dqi")
+            send(lambda d, m: B("il", 3 * (d - q - 1), 3 * (d - q - 1) + AC + 3), lambda d, m: B("li%d" % q, 0, AC + 3), "ri%d" % q)
+
+    buckets("E", tw("E", 1, RES))
+    bins("E", 0, RES)
+    tally("E", 3, 0, RES)
+    own = 256 * q
+
+    def leave(h):
+        lo, hi = 128 * h, 128 * h + 128
+        dma("YS"[h], [lambda: (g.scalar if h else g.sync).dma_start(T.y[:, lo:hi], T.yo[:, lo:hi])], [B("yo", lo, hi)], [], 65536)
+
+    out = B("ac" if q else "yo")
+    cpg(out, sg(0), B("prm"), "S")
+    for t in range(1, EV):
+        ttg(out, sg(t), B("prm"), out, A.add)
+    if q == 0:
+        for h in range(2):
+            leave(h)
+    else:
+        sm = B("psI", 0, 256)
+        act(sm, out)
+        for s in range(q - 1, -1, -1):
+            n = 3 * (N - s)
+            landed("ri%d" % s, width(s, q, "ri"), [B("li%d" % s)])
+            landed("re%d" % s, width(s, q, "re"), [B("le%d" % s)])
+            sca(B("ye%d" % s), B("li%d" % s, 0, n), B("le%d" % s, 0, 16 * n))
+            tt(sm, sm, B("ye%d" % s, own, own + 256), A.add)
+        for s in range(q - 1, -1, -1):
+            a, n = 3 * (N - 1 - s), 3 * (q - s)
+            landed("rl%d" % s, width(s, q, "rl"), [B("ll%d" % s)])
+            sca(B("yl"), B("ll%d" % s, 0, n), B("ll%d" % s, a, a + 16 * n))
+        for h in range(2):
+            lo, hi = 128 * h, 128 * h + 128
+            tt(B("yo", lo, hi), B("psI", lo, hi), B("yl", own + lo, own + hi), A.add)
+            leave(h)
+    return ops
+
+
+def rank_program(g, core, T, topo):
+    q = T.rank_of(core)
+    if q is None:
+        return
+    order = schedule([program(g, r, T, topo) for r in range(N)])
+    issue, finish = tracker(g, T)
+    for o in order[q]:
+        issue(o)
+    finish()

@@ -1,52 +1,81 @@
+import numpy
 from concourse.bass import DstId, RemoteDMATransfer
 from concourse.mybir import AluOpType as A, ActivationFunctionType as AF
 
 N, CAP, EV, RES = 4, 48, 4, 16
-BIG = 131072.0
-LOW = -524288.0
-TRW = 1456
-ZF = "VVVSSSGG"
-LOOKS, ROUNDS = (0.4, 0.5, 0.55, 0.6, 0.65, 0.7, 0.8), 6
-C = dict(cyc=1.0e-3, same=0.10, cross=0.17, dissue=0.06, dlat=0.6, drate=300e3, rissue=0.7, rstart=0.6, rhop=0.6,
-         rrate=60e3, first=1.4, gg=1.5, sg=3.5)
+OFFS = 262144.0
+OUT = 65536.0
+EMPTY = 40960.0
+ZF = ("VVVVSSSS", "VVVVSSSS", "VVVVSSSS", "VVVVVSSS")
+QUAD = 192
+CASES = ((1, 0, 1, 0, 0, 1), (1.2, 0, 1.2, 0, 0, 1), (1, 0.03, 1.3, 0, 0, 0.9), (1, 0, 1, 0.3, 0.6, 1), (0.9, 0, 0.9, -0.2, -0.3, 1),
+         (1.25, 0, 1.25, 0.3, 0.6, 1.15))
+TRIES, ROUNDS, STEP, SOME = 800, 2, 1.0, 0.1
+C = dict(cyc=1.0e-3, same=0.10, cross=0.17, dissue=0.06, dlat=0.6, drate=300e3, rissue=0.8, rstart=0.4, rrow=0.02, rhop=0.6,
+         rrate=60e3, first=1.4, smin=64, gg=1.5, sg=3.5)
+
+BATCH = {
+    3: [],
+    2: [("A", 1, "302", "V"), ("B", 2, "302", "V"), ("C", 2, "312", "V"), ("D", 3, "302 312", "V"), ("A", 3, "322", "V")],
+    1: [("AB", 1, "301 201", "V"), ("CD", 2, "301 201", "V"), ("AB", 2, "302 311 211", "V"), ("C", 3, "301 201", "S"),
+        ("D", 3, "302 311 211 312", "V"), ("A", 3, "321 221", "V")],
+    0: [("AB", 1, "300 200 100", "VS"), ("CD", 2, "300 200 100", "S"), ("XY", 2, "302 301 310", "S"), ("AB", 2, "201 210 110", "S"),
+        ("C", 3, "300 200 100", "S"), ("D", 3, "301 310 201 210 110", "V"), ("X", 3, "312 320 220 120", "S"),
+        ("Y", 3, "302 311 211", "V")],
+}
+TALLY = {3: "", 2: "302 312", 1: "301 201 302 311 211 312", 0: "300 200 100 302 301 310 201 210 110"}
+DOWN = {
+    3: [[(2, 1, "302")], [(1, 1, "301"), (0, 1, "300")], [(1, 2, "311")], [(2, 2, "312"), (0, 2, "310")],
+        [(0, 3, "320")], [(2, 3, "322"), (1, 3, "321")]],
+    2: [[(1, 1, "201"), (0, 1, "200")], [(1, 2, "302"), (0, 2, "302")], [(1, 2, "211"), (0, 2, "210")],
+        [(1, 3, "302"), (0, 3, "302")], [(1, 3, "312"), (0, 3, "312")], [(1, 3, "221"), (0, 3, "220")]],
+    1: [[(0, 1, "100")], [(0, 2, "301 201")], [(0, 2, "110")], [(0, 3, "301 201")], [(0, 3, "302 311 211")], [(0, 3, "120")]],
+    0: [],
+}
+HOME = {
+    3: ("", []),
+    2: ("302 312 322!3", [[(3, 0, "003")]]),
+    1: ("301 201 302 311 312 321!3 221!3 211", [[(3, 0, "0"), (2, 1, "0")], [(3, 2, "1113")], [(2, 6, "30")]]),
+    0: ("300!1 200!1 100!1 300 302 301 310 312!3 320!3 302!3 311!3 100 110 120!3 200 201 210 220!3 211!3",
+        [[(3, 0, "0"), (2, 1, "0"), (1, 2, "0")], [(3, 3, "3233")], [(1, 11, "333"), (2, 14, "333")],
+         [(3, 7, "3333")], [(2, 17, "33")]]),
+}
+PARTS = {3: [[((2,), "X"), ((1, 0), "A")], [((2, 1), "C"), ((0,), "B")], [((2, 1), "A"), ((0,), "X")]],
+         2: [[((1, 0), "X")]] * 3, 1: [[((0,), "X")]] * 3}
+YW = 592
 
 SCRATCH = {}
 for _n, _w, _t in (
-        ("bmr", 512, "int32"), ("bmh", 512, "int32"), ("kt", 512, "float32"), ("t5", 512, "float32"), ("hi", 512, "bfloat16"),
-        ("lo", 512, "bfloat16"), ("bmp", 1024, "bfloat16"), ("win", 8192, "bfloat16"), ("one", 128, "bfloat16"),
-        ("zz", 1024, "bfloat16"), ("nb", 128, "bfloat16"),
-        ("s89", 256, "bfloat16"), ("sel", 512, "bfloat16"), ("csb", 4112, "int32"), ("lsb", 4112, "bfloat16"),
-        ("mg4", 128, "bfloat16"), ("bk4", 128, "bfloat16"), ("lb4", 512, "bfloat16"), ("lb4f", 512, "float32"),
-        ("lid", 512, "bfloat16"), ("lbe", 512, "bfloat16"), ("bkf", 128, "float32"), ("fz", 256, "float32"),
-        ("s5", 8, "float32"), ("dg", 512, "int32"),
-        ("nm", 112, "bfloat16"), ("rq", 112, "float32"), ("m4", 112, "float32"),
-        ("nma", 144, "bfloat16"), ("jm", 256, "float32"), ("dm", 256, "float32"), ("r16", 144, "float32"),
-        ("enw", 16, "int32"), ("sdw", 16, "int32"), ("wi", 16, "int32"), ("iw", 80, "int32"),
-        ("ge", 256, "float32"), ("gv", 256, "float32"), ("gs", 256, "bfloat16"),
-        ("gm", 256, "float32"), ("ms", 256, "bfloat16"), ("pl", 256, "bfloat16"), ("ki", 256, "bfloat16"),
-        ("pi", 4, "int32"), ("ci", 16, "int32"), ("jcl", 16, "uint16"), ("prm", 16, "uint16"), ("j16", 16, "float32"),
-        ("oh", 16, "float32"), ("cc", 64, "float32"), ("mi", 128, "bfloat16"), ("idb", 128, "bfloat16"),
-        ("nu", 128, "bfloat16"), ("dp", 128, "bfloat16"), ("k48", 96, "bfloat16"), ("kx", 96, "bfloat16"),
-        ("nt", 128, "bfloat16"), ("bv", 384, "bfloat16"), ("br", 384, "bfloat16"), ("be", 128, "bfloat16"),
-        ("trn", 32, "float32"), ("trd", 32, "float32"), ("rm", 96, "float32"), ("th", 216, "bfloat16"), ("ft", 216, "bfloat16"),
-        ("sg", 1024, "float32"), ("gl", 768, "bfloat16"), ("z", 704, "bfloat16"), ("tal", 704, "float32"),
-        ("bl", 64, "float32"), ("le0", 192, "uint16"),
-        ("le1", 144, "uint16"), ("le2", 96, "uint16"), ("li0", 12, "uint16"), ("li1", 10, "uint16"), ("li2", 6, "uint16"),
-        ("ll0", 154, "uint16"), ("ll1", 102, "uint16"), ("ll2", 52, "uint16"), ("er", 288, "uint16"), ("il", 18, "uint16"),
-        ("lr", 154, "uint16"), ("ert", 64, "float32"), ("dqi", 112, "float32"), ("ye0", TRW, "float32"), ("ye1", TRW, "float32"),
-        ("ye2", TRW, "float32"), ("yl", TRW, "float32"), ("ac", 256, "float32"), ("yo", 256, "float32"),
-        ("sw0", 768, "bfloat16"), ("sw1", 768, "bfloat16"), ("sw2", 768, "bfloat16"), ("mk", 256, "bfloat16")):
+        ("bmr", 512, "int32"), ("bmh", 512, "int32"), ("kt", 512, "float32"), ("hi", 512, "bfloat16"),
+        ("lo", 512, "bfloat16"), ("bmp", 1024, "bfloat16"), ("win", 8224, "bfloat16"), ("one", 128, "bfloat16"),
+        ("zz", 512, "bfloat16"), ("s89", 256, "bfloat16"), ("sel", 512, "bfloat16"), ("csb", 4112, "int32"),
+        ("lsb", 4112, "bfloat16"), ("mg4", 128, "bfloat16"), ("bk4", 128, "bfloat16"), ("lb4", 512, "bfloat16"),
+        ("lb4f", 512, "float32"), ("bkf", 128, "float32"), ("bk8", 128, "float32"), ("idf", 128, "float32"),
+        ("nm", 64, "bfloat16"), ("m4", 64, "bfloat16"), ("nma", 192, "bfloat16"),
+        ("jm", 256, "float32"), ("dm", 256, "float32"), ("es", 32, "int32"), ("ti", 64, "float32"), ("tr", 64, "float32"),
+        ("tl", 2, "uint16"), ("ew", 80, "int32"), ("iw", 80, "int32"), ("ge", 256, "bfloat16"), ("wi", 16, "int32"),
+        ("gv", 1024, "float32"), ("gm", 256, "float32"), ("cl", 256, "float32"), ("ms", 256, "bfloat16"),
+        ("srow", 1040, "int32"), ("v0", 256, "int32"), ("v1", 256, "int32"), ("v2", 256, "float32"),
+        ("pi", 6, "int32"), ("ci", 16, "int32"), ("jcl", 16, "uint16"), ("j16", 16, "float32"), ("oh", 16, "float32"), ("ohb", 8, "bfloat16"),
+        ("cc", 64, "float32"), ("mi", 160, "bfloat16"), ("idw", 160, "bfloat16"), ("sg", 1024, "float32"),
+        ("mk", 256, "bfloat16"), ("d0", 64, "float32"), ("jj", 36, "float32"),
+        ("nb", 128, "bfloat16"), ("nt", 128, "bfloat16"), ("nu", 128, "bfloat16"), ("bko", 128, "bfloat16"),
+        ("bke", 128, "bfloat16"), ("j0", 144, "float32"), ("j1", 144, "float32"), ("j2", 144, "float32"),
+        ("r16", 144, "bfloat16"), ("rm", 64, "float32"), ("de", 144, "float32"), ("pe", 432, "float32"),
+        ("xw", 240, "float32"), ("pw", 240, "float32"), ("lt", 144, "bfloat16"), ("ft", 192, "bfloat16"),
+        ("xf", 192, "bfloat16"), ("pos", 144, "float32"),
+        ("dn", 128, "float32"), ("ld", 128, "float32"), ("tal", 432, "float32"), ("hs", 960, "uint16"), ("hr", 960, "uint16"),
+        ("ac", 256, "float32"), ("ye0", YW, "float32"), ("ye1", YW, "float32"), ("ye2", YW, "float32"), ("ye3", YW, "float32"),
+        ("yo", 256, "float32"),
+        ("pb", 7168, "bfloat16"), ("pf", 4096, "float32"), ("pd", 1536, "float32"), ("pu", 512, "uint16"), ("pv", 256, "int32")):
     SCRATCH[_n] = ("sbuf", [128, _w], _t)
-for _k in "EFA":
-    for _n, _w, _t in (("of", 64, "uint16"), ("bn", 32, "uint16"), ("yy", 288, "bfloat16"),
-                       ("in", 256, "bfloat16"), ("xx", 256, "bfloat16"), ("vr", 256, "float32"),
-                       ("tw", 544, "float32"), ("xf", 128, "bfloat16")):
-        SCRATCH[_n + _k] = ("sbuf", [128, _w], _t)
-PS = ("E0", "E1", "F0", "F1", "A0", "A1", "psZ", "psI")
+PS = ("E", "X", "Y", "W", "A", "B", "C", "D")
 for _k in PS:
     SCRATCH[_k] = ("psum", [128, 512], "float32")
 
-SEMAPHORES = (["cV", "cP", "cS", "cG", "snt", "rx0", "rx1", "rx2"] + [a + str(s) for a in ("ri", "re", "rl") for s in range(3)]
+SEMAPHORES = (["cV", "cP", "cS", "cG", "snt"] + ["sd%d" % r for r in range(1, N)]
+              + ["dn%d_%d" % (r, i) for r in range(N) for i in range(len(DOWN[r]))]
+              + ["hm%d_%d" % (r, i) for r in range(N) for i in range(len(HOME[r][1]))]
               + ["d%d" % i for i in range(16)])
 
 
@@ -161,6 +190,13 @@ def links(ops):
                     l[:] = [e for e in l if not within(e[0], c)]
                 l.append((c, kind, q, i))
         o["d"] = d
+    sends = [i for i, o in enumerate(ops) if o["k"] == "send"]
+    ops[sends[0]]["t"] += C["first"]
+    for i in sends[1:]:
+        ops[i]["d"].setdefault(sends[0], 0.0)
+    loads = [i for i, o in enumerate(ops) if o["k"] == "dma" and o["w"] and o["q0"] == "Y"]
+    for i, j in zip(loads, loads[1:]):
+        ops[j]["d"][i] = -ops[i]["lag"]
 
 
 def schedule(progs):
@@ -176,8 +212,9 @@ def schedule(progs):
         for i, o in enumerate(p):
             dep.append({base[r] + j: lat for j, lat in o["d"].items()})
             if o["k"] == "send":
-                for d in o["to"]:
-                    sends.setdefault((d, o["sem"]), []).append((base[r] + i, C["rstart"] + o["by"] / C["rrate"] + C["rhop"]))
+                for d, rows in o["to"]:
+                    lat = C["rstart"] + rows * C["rrow"] + o["by"] / C["rrate"] + C["rhop"]
+                    sends.setdefault((d, o["sem"]), []).append((base[r] + i, lat))
     for i, o in enumerate(ops):
         if o["k"] == "land":
             for j, lat in sends[(rank[i], o["sem"])]:
@@ -194,97 +231,139 @@ def schedule(progs):
             left[j] -= 1
             if left[j] == 0:
                 last.append(j)
-    best = None
-    for look in LOOKS:
+    tags = sorted(set((rank[i], o["tag"]) for i, o in enumerate(ops)))
+    tag = [tags.index((rank[i], o["tag"])) for i, o in enumerate(ops)]
+    cases = []
+    for work, more, wait, issue, way2, load in CASES:
+        t = [(o["t"] + issue if o["k"] == "send" else o["t"] * work + (more if o["k"] == "op" else 0.0), o["lag"] * load) for o in ops]
+        cases.append((t, [[(j, lat + way2 if ops[j]["k"] == "send" and lat else lat * (wait if lat > 0 else load)) for j, lat in l]
+                          for l in into]))
+    rng, best = numpy.random.default_rng(1), None
+    for k in range(TRIES):
         pri = way
-        for _ in range(ROUNDS):
-            end, seq, fin = arrange(ops, rank, into, out, pri, look)
-            if best is None or end < best[0]:
-                best = (end, seq)
-            pri = arrange(ops, rank, out, into, fin, look)[2]
-    return [[ops[i] for i in l] for l in best[1]]
+        if best:
+            off = (rng.normal(size=len(tags)) * STEP * (rng.random(len(tags)) < SOME)).tolist()
+            pri = [p + off[k] for p, k in zip(best[2], tag)]
+        for _ in range(ROUNDS if best else 10 * ROUNDS):
+            end, fin = arrange(ops, rank, into, out, pri, True)
+            if best is None or end < best[3] + 1:
+                order = sorted(range(n), key=lambda i: (fin[i] - ops[i]["t"] - ops[i]["lag"], i))
+                mean = sum(replay(ops, rank, order, *c) for c in cases) / len(cases)
+                if best is None or mean <= best[0]:
+                    best = (mean, order, pri, end)
+            pri = arrange(ops, rank, out, into, fin, False)[1]
+    return [[i - base[r] for i in best[1] if rank[i] == r] for r in range(N)]
 
 
-def arrange(ops, rank, into, out, pri, look):
+def replay(ops, rank, order, t, into):
+    fin, free = [0.0] * len(ops), {}
+    for i in order:
+        o = ops[i]
+        s = max([0.0] + [fin[j] + lat for j, lat in into[i]])
+        if o["k"] != "land":
+            s = max(s, free.get((rank[i], o["q0"]), 0.0))
+            free[(rank[i], o["q0"])] = s + t[i][0]
+        fin[i] = s + t[i][0] + t[i][1]
+    return max(fin)
+
+
+def arrange(ops, rank, into, out, pri, forward):
     n = len(ops)
-    deg, ready, fin = [len(l) for l in into], [0.0] * n, [0.0] * n
-    pool, free, dfree, first = {}, {}, [0.0] * N, set()
-    res = [[] for _ in range(N)]
+    deg, ready, fin, line = [len(l) for l in into], [0.0] * n, [0.0] * n, {}
+    pool = sorted((pri[i], -i) for i in range(n) if not deg[i])
+    while pool:
+        i = -pool.pop()[1]
+        o = ops[i]
+        s, t = ready[i] + (0.0 if forward else o["lag"]), o["t"]
+        if o["k"] != "land":
+            l = line.setdefault((rank[i], o["q0"]), [])
+            k = len(l)
+            while k and l[k - 1][1] > s:
+                k -= 1
+            while k < len(l) and l[k][0] < s + t:
+                s = max(s, l[k][1])
+                k += 1
+            l.insert(k, (s, s + t))
+        fin[i] = s + t + (o["lag"] if forward else 0.0)
+        for j, lat in out[i]:
+            ready[j] = max(ready[j], fin[i] + lat)
+            deg[j] -= 1
+            if not deg[j]:
+                pool.append((pri[j], -j))
+                pool.sort()
+    return max(fin), fin
 
-    def enter(j):
-        pool.setdefault((rank[j], ops[j]["q0"]), []).append(j)
 
-    def done(i, t):
-        st = [(i, t)]
-        while st:
-            i, t = st.pop()
-            fin[i] = t
-            for j, lat in out[i]:
-                ready[j] = max(ready[j], t + lat)
-                deg[j] -= 1
-                if deg[j] == 0:
-                    if ops[j]["k"] == "land":
-                        res[rank[j]].append(j)
-                        st.append((j, ready[j]))
-                    else:
-                        enter(j)
+def shares(n):
+    return {1: (8,), 2: (4, 4), 3: (4, 2, 2)}[n]
 
-    for i in range(n):
-        if not into[i]:
-            enter(i)
-    while True:
-        best = None
-        for key, l in pool.items():
-            if not l:
-                continue
-            f = free.get(key, 0.0)
-            t0 = max(f, min(ready[i] for i in l))
-            c = max((i for i in l if ready[i] <= t0), key=lambda i: (pri[i], -i))
-            lim = t0 + ops[c]["t"] * look
-            for i in l:
-                if t0 < ready[i] < lim and pri[i] > pri[c] + (ready[i] - t0):
-                    c, lim = i, ready[i]
-            s = max(f, ready[c])
-            if best is None or s < best[0]:
-                best = (s, key, c)
-        if best is None:
-            break
-        s, key, c = best
-        pool[key].remove(c)
-        o, r = ops[c], key[0]
-        e = s + o["t"]
-        if o["k"] == "send" and r not in first:
-            first.add(r)
-            e += C["first"]
-        free[key] = e
-        res[r].append(c)
-        if o["k"] == "dma":
-            dfree[r] = max(dfree[r], e + C["dlat"]) + o["by"] / C["drate"]
-            e = dfree[r] + C["dlat"]
-        done(c, e)
-    return max(fin), res, fin
+
+def layout():
+    src, dst, home = {}, {}, {r: [] for r in range(N)}
+    for r in range(N):
+        k = 0
+        for call in DOWN[r]:
+            for d, u, bl in call:
+                for b in bl.split():
+                    if (r, u, b) not in src:
+                        src[(r, u, b)] = k
+                        k += 6
+    for q in range(N):
+        k = 0
+        for _, u, bl, _ in BATCH[q]:
+            for b in bl.split():
+                for r in range(N - 1, q, -1):
+                    for i, call in enumerate(DOWN[r]):
+                        for (d, v, bs), w in zip(call, shares(len(call))):
+                            if d == q and v == u and b in bs.split() and (q, r, u, b) not in dst:
+                                for x in bs.split():
+                                    dst[(q, r, u, x)] = (k, i, w)
+                                    k += 6
+    used = [0] * N
+    for r in range(N):
+        for i, call in enumerate(HOME[r][1]):
+            for (d, a, y), w in zip(call, shares(len(call))):
+                home[d].append((r, i, a, y, w, used[d]))
+                used[d] += CAP * len(y)
+    return src, dst, home
+
+
+def runs(items, joins):
+    out = []
+    for x in items:
+        if out and joins(out[-1][-1], x):
+            out[-1].append(x)
+        else:
+            out.append([x])
+    return out
 
 
 def program(g, q, T, topo):
-    ops, cols = [], {}
+    ops, cols, taken, tag, moved = [], {}, {}, ["numbers"], [0, 0]
     core = T.cores[q]
     V, P, S = g.vector, g.tensor, g.scalar
     NA = N - 1 - q
-    AC = 3 * NA
-    CT = RES + AC * 2
-    Q1 = q + 1
-    OFF = BIG - 8192.0 * q - 0.4375
-    if q == 0:
-        OFF = -0.4375
+    BASE = -8192.0 * q - 0.4375
+    SRC, DST, HOMES = layout()
+    WINDOWS = sorted(set(y for h in HOMES[q] for y in h[3]))
     cy = C["cyc"]
 
     def op(qq, fns, reads, writes, t, **kw):
-        o = dict(k="op", q=qq, q0=qq, f=fns, r=reads, w=writes, t=t)
+        o = dict(k="op", q=qq, q0=qq, f=fns, r=reads, w=writes, t=t, tag=tag[0], lag=0.0)
         o.update(kw)
         ops.append(o)
 
     def B(n, lo=0, hi=None, step=1):
         return (n, lo, SCRATCH[n][1][1] if hi is None else hi, step)
+
+    def new(n, w):
+        a = taken.get(n, 0)
+        taken[n] = a + (w + 15) // 16 * 16
+        assert taken[n] <= SCRATCH[n][1][1], n
+        return B(n, a, a + w)
+
+    def sub(r, lo, hi, step=1):
+        return (r[0], r[1] + lo * r[3], r[1] + (hi - 1) * r[3] + 1, r[3] * step)
 
     def ap(r):
         if not isinstance(r, tuple):
@@ -300,13 +379,11 @@ def program(g, q, T, topo):
     def short(*rs):
         return all(SCRATCH[r[0]][2] in ("bfloat16", "uint16") for r in rs)
 
-    def ts(o, i, s1, s2, op0, op1=None):
-        rd = [i] + [s for s in (s1, s2) if isinstance(s, tuple)]
-        t = tv(wd(o), 0.5 if short(o, i) else 1)
-        if op1 is None:
-            op("V", [lambda: V.tensor_scalar(ap(o), ap(i), ap(s1), None, op0)], rd, [o], t)
-        else:
-            op("V", [lambda: V.tensor_scalar(ap(o), ap(i), ap(s1), ap(s2), op0, op1)], rd, [o], t)
+    def ts(o, i, s1, s2, op0, op1=None, by=None):
+        rd = [i] + [s for s in (s1, s2, by) if isinstance(s, tuple)]
+        t = 0.05 + cy * C["gg"] * wd(o) if by else tv(wd(o), 0.5 if short(o, i) else 1)
+        tail = (op0,) if op1 is None else (op0, op1)
+        op("V", [lambda: V.tensor_scalar(ap(o), ap(i).indirect(ap(by)) if by else ap(i), ap(s1), ap(s2), *tail)], rd, [o], t)
 
     def tt(o, a, b, f):
         op("V", [lambda: V.tensor_tensor(ap(o), ap(a), ap(b), f)], [a, b], [o], tv(wd(o), 1 if a[0] in PS or b[0] in PS else 2))
@@ -317,27 +394,32 @@ def program(g, q, T, topo):
     def cp(o, i):
         op("V", [lambda: V.tensor_copy(ap(o), ap(i))], [i], [o], tv(wd(o), 0.5 if short(o, i) else 1))
 
-    def cpg(o, w, l, eng="V"):
+    def cpg(o, w, l, eng="V", scale=1.0):
         if eng == "V":
             op("V", [lambda: V.tensor_copy(ap(o), ap(w).indirect(ap(l)))], [w, l], [o], 0.05 + cy * C["gg"] * wd(o))
         else:
-            op("S", [lambda: S.activation(ap(o), ap(w).indirect(ap(l)), AF.Copy)], [w, l], [o], 0.065 + cy * C["gg"] * wd(o))
+            op("S", [lambda: S.activation(ap(o), ap(w).indirect(ap(l)), AF.Copy, scale=scale)], [w, l], [o],
+               0.065 + cy * C["gg"] * wd(o))
 
     def sca(w, l, i):
         op("V", [lambda: V.tensor_copy(ap(w).indirect(ap(l)), ap(i))], [l, i], [w], 0.05 + cy * C["sg"] * wd(i), com=w[0])
 
-    def scan(o, m, i, op0=A.add, op1=A.max, f=1):
-        op("V", [lambda: V.tensor_tensor_scan(ap(o), ap(m), ap(i), 0.0, op0, op1)], [m, i], [o], tv(wd(o), f))
+    def scan(o, a, b, op0, op1, init=0.0):
+        op("V", [lambda: V.tensor_tensor_scan(ap(o), ap(a), ap(b), init, op0, op1)], [a, b], [o],
+           tv(wd(o), 0.5 if short(o, a, b) else 1))
 
     def fill(o, c):
         op("V", [lambda: V.memset(ap(o), c)], [], [o], tv(wd(o), 0.5 if short(o) else 1))
 
-    def act(o, i, scale=1.0, bias=None, func=AF.Identity):
-        t = 0.06 + cy * wd(o)
+    def act(o, i, scale=1.0, bias=None, func=AF.Identity, acc=None):
+        t = 0.06 + cy * max(C["smin"], wd(o))
         more = [x for x in (scale, bias) if isinstance(x, tuple)]
-        if bias:
+        if acc:
+            op("S", [lambda: S.activation(ap(o), ap(i), func, bias=ap(bias), scale=scale, accum_out=ap(acc))], [i] + more,
+               [o, acc], t + 0.02)
+        elif bias:
             op("S", [lambda: S.activation(ap(o), ap(i), func, bias=ap(bias), scale=ap(scale))], [i] + more, [o], t)
-        elif more:
+        elif more or func != AF.Identity:
             op("S", [lambda: S.activation(ap(o), ap(i), func, scale=ap(scale))], [i] + more, [o], t)
         else:
             op("S", [lambda: S.activation(ap(o), ap(i), AF.Copy, scale=scale)], [i], [o], t)
@@ -346,18 +428,25 @@ def program(g, q, T, topo):
         kw = {} if SCRATCH[o[0]][2] == "int32" else {"allow_small_or_imprecise_dtypes": True}
         op("G", [lambda: g.iota(ap(o), pat, base, ch, **kw)], [], [o], 0.13 + 2 * cy * wd(o))
 
+    def const(o, c):
+        iota(o, [[0, wd(o)]], c, 0)
+
     def aff(o, i, pat, cmp, base, ch, other=0.0):
         op("G", [lambda: g.affine_select(ap(o), ap(i), pat, cmp, other, base, ch)], [i], [o], 0.17 + 2 * cy * wd(o))
 
-    def mm(o, lst, a=0, b=None):
+    def mm(o, lst, a=0, b=None, more=False, last=None):
         n = len(lst)
+        last = not more if last is None else last
         part = list(enumerate(lst))[a:b]
-        fns = [lambda k=k, l=l, r=r: P.matmul(ap(o), ap(l), ap(r), k == 0, k == n - 1) for k, (l, r) in part]
+        fns = [lambda k=k, l=l, r=r: P.matmul(ap(o), ap(l), ap(r), k == 0 and not more, k == n - 1 and last)
+               for k, (l, r) in part]
         t = sum(0.03 + cy * max(64, wd(r)) * (1 if short(r) else 4) for k, (l, r) in part)
         op("P", fns, [x for _, p in part for x in p], [o], t)
 
     def dma(qq, fns, reads, writes, by):
-        op(qq, fns, reads, writes, C["dissue"] * len(fns), k="dma", q="D", by=by)
+        moved[bool(reads)] += by
+        ahead = 0.0 if reads else C["dissue"] * len([o for o in ops if o["q0"] == qq])
+        op(qq, fns, reads, writes, C["dissue"], k="dma", q="D", lag=2 * C["dlat"] + moved[bool(reads)] / C["drate"] - ahead)
 
     def load(qq, dst, name):
         dma(qq, [lambda: (g.sync if qq == "Y" else g.scalar).dma_start(T[dst[0]][:, dst[1]:dst[2]], T[name][:, :])], [], [dst],
@@ -369,32 +458,49 @@ def program(g, q, T, topo):
         k = cols[name]
         return B("cc", k, k + 1)
 
-    def oh(k):
-        return B("oh", k, k + 1)
-
     def M3(n, k):
         return B(n, 128 * k, 128 * k + 128)
 
-    bk, idb = B("bk4"), B("idb")
+    def remote(sem, parts, shared=False, after=[]):
+        w = shares(1 if shared else len(parts))
 
-    def quad(lname, src, s0, s1):
-        return ([(idb, B("nm", 0, (s1 - s0) // 4))]
-                + [(M3(lname, r), (src, s0 + r, s1, 4)) for r in range(4)])
+        def go():
+            e = topo.engines(core, T.cores[parts[0][0]])
+            ids = [DstId(rid=topo.addr(T.cores[d])[0], pnc=topo.addr(T.cores[d])[1]) for d, _, _ in parts]
+            masks = [sum(1 << k for k in e[sum(w[:i]):sum(w[:i + 1])]) for i in range(len(w))]
+            if shared:
+                tr = [RemoteDMATransfer(dst_ids=ids, remote_sem=T.sem[sem], srcs=[ap(parts[0][1])],
+                                        dsts=[ap(b) for _, _, b in parts], dma_engine_mask=masks[0])]
+            else:
+                tr = [RemoteDMATransfer(dst_ids=[i], remote_sem=T.sem[sem], src=ap(a), dst=ap(b), dma_engine_mask=m)
+                      for i, m, (_, a, b) in zip(ids, masks, parts)]
+            g.remote_dma_fused(tr, local_sem=T.sem.snt)
+        op("G", [go], [x[1] for x in parts] + after, [], C["rissue"], k="send", sem=sem,
+           to=[(x[0], 16 * len(parts) if shared else 128 // w[i]) for i, x in enumerate(parts)],
+           by=sum(128 * wd(x[1]) * (2 if short(x[1]) else 4) for x in parts), val=sum(w))
 
-    def unquad(ps, n, o):
-        scan(B(o, 0, 4 * n), B("rq", 0, 4 * n), B(ps, 0, 4 * n))
-        return B(o, 3, 4 * n, 4)
+    def landed(sem, val, regs):
+        op("R", [], [], regs, 0.0, k="land", sem=sem, val=val)
 
-    def low(n):
-        return (idb, B("nma", 0, n))
+    bk, idb = B("bk4"), B("idw", 16, 144)
 
-    def diag(ps, n, o):
-        scan(B(o, 0, n), B("r16", 0, n), B(ps, 0, n))
-        return B(o, 15, n, 16)
+    def sums(row, lname="lb4"):
+        m = wd(row)
+        if m >= QUAD:
+            return [(M3(lname, r), sub(row, r, m, 4)) for r in range(4)], m // 4
+        return [(bk, row)], m
 
-    load("Y", B("enw"), "en")
-    load("S", B("bmr"), "bm")
-    load("Y", B("sdw"), "sd")
+    def lifted(ps, m, w):
+        mm(B(ps, 0, w), [(idb, B("nm" if m >= QUAD else "nma", 0, w))], last=False)
+
+    def picked(ps, w, d, n, o=None, lo=0):
+        o = o or new("pf", w)
+        scan(o, B(ps, lo, lo + w), d, A.max, A.add)
+        return sub(o, w // n - 1, w, w // n)
+
+    load("Y", B("es", 0, 16), "en")
+    load("S", B("es", 16, 32), "sd")
+    load("Y", B("bmr"), "bm")
     load("Y", B("csb", 0, 4096), "cs")
     load("Y", B("lsb", 0, 4096), "ls")
     iota(B("pi", 0, 1), [[0, 1]], 0, 1)
@@ -402,407 +508,426 @@ def program(g, q, T, topo):
     iota(B("jm"), [[0, 16], [1, 16]], 0, 0)
     iota(B("ci"), [[1, 16]], 0, 0)
     iota(B("mg4"), [[16, 8], [0, 16]], 0, 0)
-    iota(B("mi"), [[1, 128]], 0, 0)
-    iota(B("m4"), [[0, 28], [1, 4]], 0, 0)
-    fill(B("one"), 1.0)
+    iota(B("mi"), [[1, 160]], -16, 0)
+    iota(B("m4"), [[0, 16], [1, 4]], 0, 0)
     fill(B("zz"), 0.0)
-    for k, e in enumerate(ZF):
-        w = B("win", 1024 * k, 1024 * k + 1024)
-        if e == "V":
-            fill(w, 0.0)
-        elif e == "S":
-            act(w, B("zz"))
-        else:
-            iota(w, [[0, 1024]], 0, 0)
     ts(B("pi", 1, 2), B("pi", 0, 1), 15, None, A.bitwise_and)
     ts(B("pi", 2, 3), B("pi", 0, 1), 2, 3, A.arith_shift_right, A.bitwise_and)
-    cp(col("p"), B("pi", 0, 1))
-    cp(col("o"), B("pi", 1, 2))
-    cp(col("o4"), B("pi", 2, 3))
+    ts(B("pi", 3, 4), B("pi", 0, 1), 4, 1, A.arith_shift_right, A.bitwise_and)
+    ts(B("pi", 4, 5), B("pi", 0, 1), 1, 7, A.arith_shift_right, A.bitwise_and)
+    ts(B("pi", 5, 6), B("pi", 0, 1), 1, None, A.bitwise_and)
+    for k, x in enumerate(("p", "o", "o4", "odd", "o8", "o1")):
+        assert col(x)[1] == k
+    cp(B("cc", 0, 6), B("pi"))
     tt(col("g16"), col("p"), col("o"), A.subtract)
-    ts(B("oh"), B("j16"), col("o"), None, A.is_equal)
     ts(B("dm"), B("jm"), col("o"), None, A.is_equal)
     cp(B("jcl"), B("ci"))
     ts(bk, B("mg4"), col("g16"), None, A.is_equal)
-    ts(idb, B("mi"), col("p"), None, A.is_equal)
-    tt(B("s5", 0, 5), B("oh", 0, 5), B("oh", 5, 10), A.add)
-    sc = B("s5", 4, 5)
-    for k in (3, 2, 1, 0):
-        act(col("s%d" % k), sc, 0.0625, B("s5", k, k + 1))
-        sc = col("s%d" % k)
-    ts(col("h9"), col("o"), 9.0, -0.5, A.is_le, A.mult)
-    act(col("bi"), sc, 0.5, col("h9"))
-    for t in range(3):
-        act(col("n%d" % t), oh(6 + t), 16.0, oh(5 + t))
-        act(col("m%d" % t), oh(7 + t), 256.0, col("n%d" % t))
-        act(M3("bv", t), bk, col("m%d" % t))
-    act(col("bA"), oh(15), float(q), oh(13))
+    ts(B("idw"), B("mi"), col("p"), None, A.is_equal)
+    act(col("o32"), col("o"), 1.0, 32.0)
+    ts(B("tl", 0, 1), col("odd"), 48.0, col("o"), A.mult, A.add)
+    ts(B("tl", 1, 2), col("odd"), -16.0, col("o32"), A.mult, A.add)
+    cp(B("ti", 0, 32), B("es"))
+    act(B("ti", 32, 48), B("es", 16, 32))
+    act(B("ti", 48, 64), B("es", 0, 16))
+    op("V", [lambda: V.transpose(ap(B("tr")), ap(B("ti")))], [B("ti")], [B("tr")], tv(64, 1))
+    cpg(B("ew", 0, 32), B("tr"), B("tl"))
+    enw, sdw = B("ew", 0, 16), B("ew", 16, 32)
+    if q:
+        pass
+    if NA:
+        landed("sd%d" % (q + 1), 8, [B("ew", 32, 32 + 16 * NA)])
+    if q:
+        remote("sd%d" % q, [(q - 1, B("ew", 16, 32 + 16 * NA), B("ew", 32, 48 + 16 * NA))])
+    fill(B("lb4"), 0.0)
+    for r in range(4):
+        cp(B("lb4", 129 * r, 128 * r + 128, 4), B("bk4", r, 128, 4))
+    act(B("lb4f"), B("lb4"))
+    act(B("bkf"), bk)
+    iota(B("kt"), [[-32, 512]], 0, 0)
+    ts(col("even"), col("o1"), -1.0, 1.0, A.mult, A.add)
+    for k in range(2):
+        for j in range(2):
+            ts(M3("sel", k + 2 * j), B("idw", 16 + k - j, 144 + k - j), col(("even", "o1")[k]), None, A.mult)
+    ts(B("nm"), B("m4"), col("o4"), OFFS, A.is_equal, A.mult)
+    act(B("nma"), B("dm", 0, 192), OFFS)
+    tag[0] = "first bins"
+    mi0, mi1, mh0, mb0, e7 = [B("iw", 16 * k, 16 * k + 16) for k in range(5)]
+    ts(B("wi"), enw, 12, 15, A.arith_shift_right, A.bitwise_and)
+    ttg(B("ge"), B("wi"), B("jcl"), B("dm"), A.mult)
+    mm(B("X", 0, 256), [(bk, B("ge"))])
+    of0, bn = new("pu", 16), new("pu", 16)
+    ts(mi0, enw, 3, 511, A.arith_shift_right, A.bitwise_and)
+    cp(of0, mi0)
+    ts(e7, enw, 7, None, A.bitwise_and)
+    ts(B("ms"), B("X", 0, 256), col("o"), None, A.is_equal)
+    ts(B("d0"), B("m4", 0, 64), 3.0, -OFFS, A.is_equal, A.mult)
+    L, w = sums(B("gm"), "lb4f")
+    lifted("E", 256, w)
+    ttg(B("gm"), B("bmr"), of0, B("ms"), A.mult)
+    mm(B("E", 0, w), L, more=True, last=True)
+    cp(mi1, picked("E", w, B("d0"), RES))
+    ts(mh0, mi1, 31, None, A.bitwise_and)
+    ts(mb0, mi1, 5, None, A.arith_shift_right)
+    h1, h2 = new("pf", 16), new("pf", 16)
+    tt(h1, mh0, e7, A.is_le)
+    tt(h2, mb0, h1, A.add)
+    cp(bn, h2)
+
+    def seeds(k, w, ps):
+        gv = B("gv", 256 * k, 256 * k + 256)
+        ttg(gv, w, B("jcl"), B("dm"), A.mult)
+        mm(B(ps, 0, 256), [(B("bkf"), gv)])
+        act(B("srow", 256 * k, 256 * k + 256), B(ps, 0, 256))
+
+    tag[0] = "seeds"
+    seeds(0, sdw, "W")
+    ts(B("v0"), B("srow", 0, 256), 4095, None, A.bitwise_and)
+    ts(B("v1"), B("srow", 0, 256), 4, 4095, A.arith_shift_right, A.bitwise_and)
+    act(B("v2"), B("srow", 0, 256), 1.0 / 256)
+    tag[0] = "table"
     ts(col("bb"), col("o"), -16384.0, 32.0, A.mult, A.add)
+    ts(B("bmh"), B("bmr"), 31, None, A.bitwise_and)
+    act(B("A"), B("bmh"), -5.0, col("bb"))
+    tt(B("A"), B("A"), B("bmr"), A.add)
+    tt(B("A"), B("A"), B("kt"), A.add)
+    act(B("hi"), B("A"))
+    fill(B("csb", 4096, 4112), 0)
+    fill(B("lsb", 4096, 4112), 0.0)
+    tt(B("lo"), B("A"), B("hi"), A.subtract)
+    for k, ps in enumerate("BC"):
+        L = [(M3("sel", k), B("hi")), (M3("sel", 2 + k), B("lo"))]
+        mm(B(ps), L, 0, 1)
+        mm(B(ps), L, 1)
+        act(B("bmp", 512 * k, 512 * k + 512), B(ps), 0.03125)
+    ts(B("oh", 0, 8), B("j16", 0, 8), col("o8"), None, A.is_equal)
+    ts(B("ohb"), B("j16", 0, 8), col("o8"), None, A.is_equal)
+    for k, e in enumerate(ZF[q]):
+        w = B("win", 16 + 1024 * k, 16 + 1024 * k + 1024)
+        if e == "V":
+            ts(w, B("bmp"), B("ohb", k, k + 1), None, A.mult)
+        else:
+            act(w, B("bmp"), B("oh", k, k + 1))
+    for a in (0, 8208):
+        fill(B("win", a, a + 16), OUT / 16)
+    const(new("pd", 64), 0)
+    tag[0] = "guests' seeds"
+    for r in range(q + 1, N):
+        k = r - q
+        seeds(k, B("ew", 16 * k + 16, 16 * k + 32), "DYX"[k - 1])
+    SW = B("srow", 0, 256 * (NA + 1) + 16)
+    if NA:
+        const(B("srow", SW[2] - 16, SW[2]), 0)
+    tag[0] = "more numbers"
     if q:
         act(B("nb"), bk, -1.0)
         aff(B("nt"), B("nb"), [[-1, 128]], A.is_gt, 0, 1)
         aff(B("nu"), B("nt"), [[-1, 128]], A.not_equal, 0, 1, -2048.0)
-        ts(col("p1"), col("p"), 1.0, None, A.add)
-        act(B("dp"), idb, col("p1"))
-    act(B("lb4f"), B("zz", 0, 512))
-    act(B("lb4"), B("zz", 0, 512))
-    for r in range(4):
-        act(B("lb4f", 129 * r, 128 * r + 128, 4), B("bk4", r, 128, 4))
-        act(B("lb4", 129 * r, 128 * r + 128, 4), B("bk4", r, 128, 4))
-    act(B("bkf"), bk)
-    aff(M3("fz", 0), B("bkf"), [[0, 8], [-1, 16]], A.is_ge, 4, 0)
-    aff(M3("fz", 1), B("bkf"), [[0, 8], [1, 16]], A.is_ge, -5, 0)
-    iota(B("kt"), [[-32, 512]], 0, 0)
-    iota(B("pl"), [[1, 16], [16, 16]], 0, 0)
-    aff(M3("s89", 0), B("one"), [[0, 8], [-1, 16]], A.is_ge, 7, 0)
-    aff(M3("s89", 1), B("one"), [[0, 8], [1, 16]], A.is_ge, -8, 0)
-    for k in range(2):
-        aff(M3("sel", k), M3("s89", 0), [[-16, 8], [-2, 16]], A.is_equal, -k, 1)
-        aff(M3("sel", 2 + k), M3("s89", 1), [[-16, 8], [-2, 16]], A.is_equal, 16 - k, 1)
-    if q:
-        iota(B("k48", 0, Q1 * CT), [[0, CT], [CAP, Q1]], 0, 0)
-        iota(B("trn", 0, CT), [[16, CT]], CAP * q - 2048, 0)
-        act(B("k48", q, Q1 * CT, Q1), B("trn", 0, CT))
-        act(B("br"), B("zz", 0, 384))
-        for j in range(3):
-            act(B("br", 129 * j + 10, 128 * j + 128, 16), B("bk4", 10 + j, 128, 16))
-    if NA:
-        iota(B("trd"), [[16, 32]], -1024, 1)
-    ts(B("nm"), B("m4"), col("o4"), LOW, A.not_equal, A.mult)
-    ts(B("rq"), B("m4"), 0.0, 2 * LOW, A.is_equal, A.mult)
-    mi0, mi1, mh0, mb0, e7 = [B("iw", 16 * k, 16 * k + 16) for k in range(5)]
-    ts(B("wi"), B("enw"), 12, 15, A.arith_shift_right, A.bitwise_and)
-    ttg(B("gs"), B("wi"), B("jcl"), B("dm"), A.mult)
-    mm(B("A0", 0, 256), [(bk, B("gs"))])
-    ts(mi0, B("enw"), 3, 511, A.arith_shift_right, A.bitwise_and)
-    cp(B("ofE", 0, 16), mi0)
-    ts(e7, B("enw"), 7, None, A.bitwise_and)
-    ts(B("ms"), B("A0", 0, 256), col("o"), None, A.is_equal)
-    L = quad("lb4f", "gm", 0, 256)
-    mm(B("E0", 0, 64), L, 0, 1)
-    ttg(B("gm"), B("bmr"), B("ofE", 0, 16), B("ms"), A.mult)
-    mm(B("E0", 0, 64), L, 1)
-    ttg(B("ge"), B("enw"), B("jcl"), B("dm"), A.mult)
-    ttg(B("gv"), B("sdw"), B("jcl"), B("dm"), A.mult)
-    Z = [(M3("fz", 0), B("ge")), (M3("fz", 1), B("gv"))]
-    mm(B("F0", 0, 256), Z, 0, 1)
-    mm(B("F0", 0, 256), Z, 1, 2)
-    ts(B("dg", 0, 256), B("F0", 0, 256), sc, col("bi"), A.mult, A.add)
-    ts(B("dg", 256, 512), B("dg", 0, 256), 15, None, A.bitwise_and)
-    ts(B("ki"), B("pl"), oh(14), col("bA"), A.mult, A.add)
-    tt(B("z", 0, 256), B("dg", 256, 512), B("ki"), A.add)
-    cp(mi1, unquad("E0", 16, "twE"))
-    ts(mh0, mi1, 31, None, A.bitwise_and)
-    ts(mb0, mi1, 5, None, A.arith_shift_right)
-    tt(B("twE", 288, 304), mh0, e7, A.is_le)
-    tt(B("twE", 320, 336), mb0, B("twE", 288, 304), A.add)
-    cp(B("bnE", 0, 16), B("twE", 320, 336))
-    act(B("psZ"), B("kt"), bias=col("bb"))
-    ts(B("bmh"), B("bmr"), 31, None, A.bitwise_and)
-    tt(B("F1"), B("psZ"), B("bmr"), A.add)
-    act(B("t5"), B("bmh"), -5.0)
-    tt(B("psZ"), B("F1"), B("t5"), A.add)
-    act(B("hi"), B("psZ"))
-    fill(B("csb", 4096, 4112), 0)
-    fill(B("lsb", 4096, 4112), 0.0)
-    if q:
-        fill(B("rm", 0, Q1 * CT), 0.0)
-        fill(B("rm", 0, Q1 * CT, Q1), -2 * LOW)
-        fill(B("kx", 0, Q1 * CT), 0.0)
-        fill(B("kx", q, Q1 * CT, Q1), 1.0)
+        act(B("bko"), bk, col("o"))
+        iota(B("j0"), [[-64, 3], [16, 3], [0, 16]], 128, 1)
+        act(col("ng"), col("g16"), -1.0)
+        act(B("j1"), B("j0"), 1.0, col("ng"))
+        iota(B("j2"), [[-64, 3], [1, CAP]], 129 - 2048, 0)
+        act(B("r16"), B("jm", 0, 144), func=AF.Sign)
+        ts(B("rm"), B("m4", 0, 64), 0.0, 4096.0, A.is_equal, A.mult)
+        ts(B("de"), B("jm", 0, 144), 15.0, EMPTY - OFFS, A.is_equal, A.mult)
+        const(B("dn"), 0)
+        for t in range(2):
+            const(B("pe", 48 * q * t, 48 * q * (t + 1)), 0)
         fill(B("ft"), 0.0)
-        for x in "EFA" if NA else "E":
-            fill(B("xf" + x), 0.0)
-        for t in range(3):
-            fill(B("sw%d" % t, 0, CAP * q), 0.0)
-    tt(B("lo"), B("psZ"), B("hi"), A.subtract)
-    mm(B("A1"), [(M3("sel", 0), B("hi")), (M3("sel", 2), B("lo"))])
-    act(B("bmp", 0, 512), B("A1"), 0.03125)
-    mm(B("psI"), [(M3("sel", 1), B("hi")), (M3("sel", 3), B("lo"))])
-    act(B("bmp", 512, 1024), B("psI"), 0.03125)
-    dma("Y", [lambda s=s: g.sync.dma_start(T.win[s::8, 1024 * s:1024 * s + 1024], T.bmp[s::8, :]) for s in range(8)],
-        [B("bmp"), B("win")], [B("win")], 262144)
-    wt = oh(4)
-    for k in (3, 2, 1, 0):
-        act(col("w%d" % k), wt, 16.0, oh(k))
-        wt = col("w%d" % k)
-    ts(col("f9"), col("o"), 10.0, None, A.is_ge)
-    ts(col("e9"), col("o"), 12.0, col("f9"), A.is_le, A.mult)
-    act(col("u1"), wt, 0.125, col("e9"))
-    if q:
-        act(col("cb"), oh(13), -BIG, col("u1"))
-    act(B("lbe"), B("lb4"), col("cb" if q else "u1"))
-    if NA:
-        ts(B("nma"), B("jm", 0, 144), col("o"), LOW, A.not_equal, A.mult)
-        ts(B("r16"), B("jm", 0, 144), 0.0, 2 * LOW, A.is_equal, A.mult)
-        act(B("be"), bk, col("cb" if q else "u1"))
-        act(col("u3"), oh(15), 256.0, oh(14))
-        act(col("cid"), oh(13), -2048.0, col("u3"))
-        act(B("lid"), B("lb4"), col("cid"))
-    ts(col("o16"), col("o"), 16.0, None, A.mult)
-    ts(B("prm"), B("ci"), col("o16"), None, A.add)
-    if q:
-        for n in ["ye%d" % s for s in range(q)] + ["yl"]:
-            iota(B(n, 256 * q, 256 * q + 256), [[0, 256]], 0, 0)
+        fill(B("xf"), 0.0)
 
-    def tw(x, k, n):
-        return B("tw" + x, 288 + 32 * k, 288 + 32 * k + n)
+    def lift(o, x):
+        if q == 0 and x[0] != "ld":
+            y = new("pf", wd(x))
+            act(y, x, func=AF.Relu)
+            x = y
+        act(o, x, 1.0, -OFFS)
 
-    def sg(t):
-        return B("sg", 256 * t, 256 * t + 256)
-
-    def vrep(x, t, s0, s1, copy):
-        o = B(x + "1", 256, 256 + s1 - s0)
-        mm(o, [(M3("bv", t), B("z", s0, s1))])
-        if copy:
-            act(B("vr" + x, 0, s1 - s0), o)
-
-    def buckets(x, src):
-        ts(B("of" + x, 0, wd(src)), src, 8191.0, 0.0, A.min, A.max)
-
-    def sums(x, row, c0, c1, fresh):
-        m = 16 * (c1 - c0)
-        if fresh:
-            return [low(m), (B("be"), B("z", 16 * c0, 16 * c1)), (bk, row)], m, 1
-        if m > 144:
-            return quad("lb4", row[0], 0, m), m // 4, 4
-        return [low(m), (bk, row)], m, 1
-
-    def wrapped(x, n, w):
-        return unquad(x + "0", n, "tw" + x) if w < 16 * n else diag(x + "0", w, "tw" + x)
-
-    def bins(x, c0, c1):
-        n = c1 - c0
+    def bins(x, pieces, eng, left=None, parts=None):
+        n = sum(wd(p) for p in pieces)
         m = 16 * n
-        yy, bn = B("yy" + x, 0, m), B("bn" + x, 0, n)
-        fresh = x == "A" and q
-        L, w, late = sums(x, yy, c0, c1, fresh)
-        mm(B(x + "0", 0, w), L, 0, len(L) - late)
-        cpg(yy, B("win"), B("of" + x, 0, n), "S" if m > 64 and x != "A" else "V")
-        mm(B(x + "0", 0, w), L, len(L) - late)
-        s = wrapped(x, n, w)
-        if fresh:
-            ts(bn, s, OFF, 4096.0, A.add, A.min)
-        else:
-            tt(tw(x, 0, n), s, B("bl", c0, c1), A.add)
-            ts(bn, tw(x, 0, n), 4096.0, 0.0, A.min, A.max)
-
-    def tally(x, t, c0, c1):
-        bn, o = B("bn" + x, 0, c1 - c0), B("tal", 16 * c0, 16 * c1)
-        if x == "E":
-            cpg(sg(t), B("csb"), bn, "S")
-        elif x == "A":
-            cpg(o, B("csb"), bn, "S")
-        else:
-            ttg(o, B("csb"), bn, o, A.add)
-
-    def event(x, t, c0, c1):
-        n, s0, s1 = c1 - c0, 16 * c0, 16 * c1
-        m = 16 * n
-        p0, p1, fresh = x + "0", x + "1", x == "A" or t == 0
-        row, zr, bn, hit = B("xx" + x, 0, m), B("z", s0, s1), B("bn" + x, 0, n), B("in" + x, 0, m)
-        ks, mp = B(p1, 0, m), B(p1, 256, 256 + m)
-        if x == "E" and t:
-            tally(x, t, c0, c1)
-            tt(hit, sg(t), mp, A.is_le)
-        else:
-            ttg(hit, B("csb"), bn, B("vr" + x, 0, m), A.is_le)
-        mm(ks, [(bk, hit)])
-        L, w, late = sums(x, row, c0, c1, x == "A")
-        if t == 0:
-            L[1:1] = [(M3("lbe", r), ("z", r, m, 4)) for r in range(4)]
-        mm(B(p0, 0, w), L, 0, len(L) - late)
-        if t == 0:
-            tally(x, t, c0, c1)
-            ts(B("mk", 0, m), ks, col("o"), -0.125, A.is_equal, A.mult)
-            ttg(row, B("lsb"), bn, B("mk", 0, m), A.mult)
-        else:
-            k = 256 * "EFA".index(x)
-            gl = B("gl", k, k + m)
-            cpg(gl, B("lsb"), bn, "S")
-            if x != "E":
-                tally(x, t, c0, c1)
-            ts(mp, ks, col("o"), -0.125, A.is_equal, A.mult)
-            tt(row, gl, mp, A.mult)
-        mm(B(p0, 0, w), L, len(L) - late)
-        en, off = wrapped(x, n, w), OFF
-        if t == 0:
-            ts(B("ofE", 0, RES), en, OFF, 8191.0, A.add, A.min)
-        if q == 0 and fresh:
-            ts(B("bl", c0, c1), en, OFF, -0.4375, A.add, A.max)
-            return
-        if not fresh:
-            tt(tw(x, 1, n), en, B("bl", c0, c1), A.add)
-            en, off = tw(x, 1, n), 0.0
-        if q == 0:
-            ts(B("bl", c0, c1), en, -0.4375, 0.0, A.max, A.add)
-            return
-        f0, a, b = 72 * t, c0 * Q1, c1 * Q1
-
-        def thr(s):
-            return 8192.0 * (s + 1 - q) - 0.5 - off
-
-        def to(s):
-            return B("ft", f0 + a + s, f0 + b, Q1)
-
-        def under(s, lo, hi):
-            return B("th", f0 + s * CT + lo, f0 + s * CT + hi) if s else B("ft", f0 + lo * Q1, f0 + hi * Q1, Q1)
-        for s in range(q):
-            ts(under(s, c0, c1), en, thr(s), None, A.is_lt)
-        pl = B(p0, 0, b - a)
-        L2 = [(idb, B("k48", a, b)), (B("dp"), B("kx", a, b)), (B("nu"), B("ft", f0 + a, f0 + b)), (bk, B("xf" + x, a, b))]
-        mm(pl, L2, 0, 2)
-        for s in range(q):
-            scan(B("xf" + x, s, b, Q1), under(s, 0, c1), under(s - 1, 0, c1) if s else B("zz", 0, c1), A.add, A.subtract, 0.5)
-        for s in range(1, q):
-            tt(to(s), under(s, c0, c1), under(s - 1, c0, c1), A.subtract)
-        mm(pl, L2, 2, 3)
-        mm(pl, L2, 3)
-        act(tw(x, 3, n), en, -16 * BIG, 16 * BIG * thr(q - 1), AF.Relu)
-        if fresh:
-            act(tw(x, 2, n), en, 1.0, off)
-            en = tw(x, 2, n)
-        tt(B("bl", c0, c1), en, tw(x, 3, n), A.add)
-        scan(B("tw" + x, 448, 448 + b - a), B("rm", 0, b - a), pl, A.add, A.min)
-        ts(B("of" + x, 32, 32 + n), B("tw" + x, 448 + q, 448 + b - a, Q1), 2047.0, None, A.add)
-        k = 8 if m > 144 else n
-        for i in range(0, n, k):
-            o, h = B("psZ", 16 * i, 16 * (i + k)), B("z", s0 + 16 * i, s0 + 16 * (i + k))
-            L3 = [(idb, h), (M3("br", t), B("xx" + x, 16 * i, 16 * (i + k)))]
-            mm(o, L3, 0, 1)
-            mm(o, L3, 1, 2)
-            act(h, o)
-        for i in range(0, n, k):
-            sca(B("sw%d" % t, 0, CAP * q + 16 * CT + 128), B("of" + x, 32 + i, 32 + i + k), B("z", s0 + 16 * i, s0 + 16 * (i + k)))
-
-    def split(s, kind):
-        d = list(range(s))[::-1] if kind == "rx" else list(range(s + 1, N))[::-1]
-        groups = {"rx": [[x] for x in d], "ri": [d]}.get(kind, [d[:2], d[2:]])
-        return [list(zip(x, {1: (8,), 2: (4, 4), 3: (4, 2, 2)}[len(x)])) for x in groups if x]
-
-    def width(s, d, kind):
-        return [w for x in split(s, kind) for y, w in x if y == d][0]
-
-    def send(src, dst, rsem):
-        for call in split(q, rsem[:2]):
-            sd = [(d, w, src(d, call[0][0]), dst(d, call[0][0])) for d, w in call]
-
-            def go(sd=sd):
-                e = topo.engines(core, T.cores[sd[0][0]])
-                tr, pos = [], 0
-                for d, w, a, b in sd:
-                    rid, pid, _ = topo.addr(T.cores[d])
-                    tr.append(RemoteDMATransfer(dst_ids=[DstId(rid=rid, pnc=pid)], remote_sem=T.sem[rsem], src=ap(a), dst=ap(b),
-                                                dma_engine_mask=sum(1 << k for k in e[pos:pos + w])))
-                    pos += w
-                g.remote_dma_fused(tr, local_sem=T.sem.snt)
-            op("G", [go], [x[2] for x in sd], [], C["rissue"], k="send", sem=rsem, to=[x[0] for x in sd],
-               by=256 * sum(wd(x[2]) for x in sd), val=sum(x[1] for x in sd))
-
-    def landed(sem, val, regs):
-        op("R", [], [], regs, 0.0, k="land", sem=sem, val=val)
-
-    def zcol(s, t, r):
-        return 16 * (RES + 3 * (N - 1 - s) * t) + CAP * (r - s - 1)
-
-    def places(n, out, k, ps, tmp):
-        er = B("ert", 32 * k, 32 * k + n)
-        tt(er, unquad(ps, n, tmp), B("trd", 0, n), A.min)
-        ts(B(out, 0, n), er, 2048.0, None, A.add)
-
-    for t in range(EV):
-        if t < 3:
-            if t == 2:
-                buckets("E", tw("E", 1, RES))
-            vrep("E", t, 0, 256, t == 0)
-            if t:
-                bins("E", 0, RES)
-            event("E", t, 0, RES)
-        if t == 2 and NA:
-            buckets("F", B("bl", RES, RES + AC))
-            vrep("F", t, 256, 256 + 16 * AC, True)
-            bins("F", RES, RES + AC)
-            event("F", t, RES, RES + AC)
-        if t == 3 and NA:
-            for a in (RES, RES + AC):
-                buckets("F", tw("F", 1, AC) if a == RES else B("bl", a, a + AC))
-                bins("F", a, a + AC)
-                tally("F", t, a, a + AC)
-                cp(B("er", 16 * (a - RES), 16 * (a - RES + AC)), B("tal", 16 * a, 16 * (a + AC)))
-            w = 16 * (AC + 3)
-            send(lambda d, m: B("er", CAP * (d - q - 1), CAP * (d - q - 1) + w), lambda d, m: B("le%d" % q, 0, w), "re%d" % q)
-        if t and NA:
-            c0 = RES + AC * (t - 1)
-            c1 = c0 + AC
-            zr = B("z", 16 * c0, 16 * c1)
-            n = 16 * AC
-            landed("rx%d" % (t - 1), sum(width(r, q, "rx") for r in range(q + 1, N)), [zr])
-            U = [low(n), (B("be"), zr)]
-            mm(B("A0", 0, n), U, 0, 1)
-            mm(B("A0", 0, n), U, 1)
-            if t < 3:
-                vrep("A", t, 16 * c0, 16 * c1, True)
-            ts(B("ofA", 0, AC), diag("A0", n, "twA"), OFF, 8191.0, A.add, A.min)
-            if q == 0:
-                ts(B("bl", c0, c1), B("twA", 15, n, 16), OFF, -0.4375, A.add, A.max)
-            bins("A", c0, c1)
-            if t < 3:
-                event("A", t, c0, c1)
+        of, yy = new("pu", n), new("pb", m)
+        L, w = sums(yy)
+        d = B("pd", 0, 64) if x == "E" else new("pd", w)
+        if x != "E":
+            const(d, 0)
+        last, k = sub(d, w // n - 1, w, w // n), 0
+        base = BASE + (EMPTY if x == "E" and q else 0)
+        for p in pieces:
+            if q:
+                ts(sub(of, k, k + wd(p)), p, base + 16, 8208.0, A.add, A.min)
             else:
-                mm(B("A1", 0, 4 * AC), quad("lid", "z", 16 * c0, 16 * c1))
-                cpg(B("lr", AC, AC + n), B("csb"), B("bnA", 0, AC))
-                places(AC, "lr", 1, "A1", "dqi")
-                send(lambda d, m: B("lr", 0, AC + CAP * (m - q)), lambda d, m: B("ll%d" % q, 0, AC + CAP * (m - q)), "rl%d" % q)
-        if t < 3 and q:
-            send(lambda d, m: B("sw%d" % t, CAP * d, CAP * d + CAP), lambda d, m: B("z", zcol(d, t, q), zcol(d, t, q) + CAP), "rx%d" % t)
-        if NA and t == 2:
-            k = 2 * AC
-            mm(B("psI", 0, 4 * k), quad("lid", "z", 256, 256 + 16 * k))
-            places(k, "il", 0, "psI", "dqi")
-            send(lambda d, m: B("il", 3 * (d - q - 1), 3 * (d - q - 1) + AC + 3), lambda d, m: B("li%d" % q, 0, AC + 3), "ri%d" % q)
+                ts(sub(of, k, k + wd(p)), p, BASE, 8192.0, A.add, A.min)
+            if left:
+                up = new("pf", n)
+                act(up, left, OUT, -OFFS)
+                tt(last, p, up, A.add)
+            else:
+                lift(sub(last, k, k + wd(p)), p)
+            k += wd(p)
+        lifted(x, m, w)
+        cpg(yy, B("win") if q else B("win", 16), of, eng)
+        mm(B(x, 0, w), L, more=True, last=True)
+        s, out = picked(x, w, d, n), []
+        for lo, hi in parts or [(0, n)]:
+            out.append(new("pu", hi - lo))
+            ts(out[-1], sub(s, lo, hi), base, 4096.0, A.add, A.min)
+        return out, d
 
-    buckets("E", tw("E", 1, RES))
-    bins("E", 0, RES)
-    tally("E", 3, 0, RES)
-    own = 256 * q
+    def event(x, bn, d, v, first=False, out=None):
+        n = wd(bn)
+        m = 16 * n
+        hit, row = new("pb", m), new("pb", m)
+        L, w = sums(row)
+        ks = B(x[-1], 256, 256 + m)
+        ttg(hit, B("csb"), bn, v, A.is_le)
+        mm(ks, [(bk, hit)])
+        mk = ks if len(x) > 1 and not first else new("pb", m)
+        ts(mk, ks, col("o"), -0.125, A.is_equal, A.mult)
+        lifted(x[0], m, w)
+        if first:
+            ttg(row, B("lsb"), bn, mk, A.mult)
+        else:
+            gl = new("pb", m)
+            cpg(gl, B("lsb"), bn, "S")
+            tt(row, gl, mk, A.mult)
+        mm(B(x[0], 0, w), L, more=True, last=True)
+        return picked(x[0], w, d, n, out)
+
+    def down(u, b):
+        ready.add((u, b))
+        for i, call in enumerate(DOWN[q]):
+            if i not in sent and all((v, x) in ready for _, v, bs in call for x in bs.split()):
+                sent.add(i)
+                parts = []
+                for d, v, bs in call:
+                    x = bs.split()
+                    a, z = SRC[(q, v, x[0])], DST[(d, q, v, x[0])][0]
+                    parts.append((d, B("dn", a, a + 6 * len(x)), B("ld", z, z + 6 * len(x))))
+                remote("dn%d_%d" % (q, i), parts)
+
+    def leavers(t, en):
+        def ft(s):
+            return B("ft", 64 * t + s, 64 * t + 64, 4)
+
+        def xf(s):
+            return B("xf", 64 * t + s, 64 * t + 64, 4)
+
+        def lt(s):
+            return B("lt", 48 * t + 16 * s, 48 * t + 16 * s + 16) if s > 0 else ft(0) if s == 0 else B("zz", 0, 16)
+        tag[0] = "flags %d" % t
+        for s in range(q - 1, -1, -1):
+            ts(lt(s), en, 8192.0 * (s + 1) - EMPTY, None, A.is_lt)
+        for s in range(q - 1, -1, -1):
+            scan(xf(s), lt(s), lt(s - 1), A.add, A.subtract, 4.0 * s)
+        for s in range(1, q):
+            tt(ft(s), lt(s), lt(s - 1), A.subtract)
+        pl, pw, cs = B("Y", 0, 64), B("pw", 80 * t + 8, 80 * t + 69), "D" if q == N - 1 else "X"
+        for c in range(3):
+            mm(B(cs, 64 * c, 64 + 64 * c), [(bk, B("xf", 64 * t, 64 * t + 64))])
+        mm(pl, [(B("nu"), B("ft", 64 * t, 64 * t + 64)), (bk, B("xf", 64 * t, 64 * t + 64))])
+        le = new("pb", CAP * q)
+        for s in range(q - 1, -1, -1):
+            tt(sub(le, CAP * (q - 1 - s), CAP * (q - s)), B(cs, s, 192, 4), B("j1", CAP * (N - 2 - s), CAP * (N - 1 - s)), A.is_le)
+        scan(B("pw", 80 * t + 5, 80 * t + 69), B("rm"), pl, A.add, A.min)
+        for ds, ps in PARTS[q][t]:
+            m, n, lo = CAP * len(ds), 3 * len(ds), CAP * (N - 2 - ds[0])
+            tag[0] = "list %d %d" % (t, ds[0])
+            cb, by, sel, gx, d = new("pb", m), new("pu", n), new("pb", m), new("pf", m), new("pe", m)
+            lifted(ps, 0, 2 * m if t < 2 else m)
+            scan(cb, B("r16", 0, m), sub(le, CAP * (q - 1 - ds[0]), CAP * (q - ds[-1])), A.mult, A.add)
+            cb = sub(cb, 15, m, 16)
+            ts(by, cb, 15.0, 4.0, A.min, A.mult)
+            ttg(sel, pw, by, B("j2", lo, lo + m), A.is_equal)
+            ttg(gx, B("xw", 80 * t + 8, 80 * t + 69), by, sel, A.mult)
+            if t < 2:
+                act(sub(d, 15, m, 16), cb, 16.0, -OFFS)
+                mm(B(ps, m, 2 * m), [(B("bko"), sel)], more=True)
+            mm(B(ps, 0, m), [(B("bkf"), gx)], more=True, last=True)
+            x = picked(ps, m, B("de", 0, m), n)
+            ix = picked(ps, m, d, n, lo=m) if t < 2 else None
+            for r in runs(range(len(ds)), lambda i, j: SRC[(q, t + 1, "%d%d%d" % (q, t, ds[j]))] == SRC[(q, t + 1, "%d%d%d" % (q, t, ds[i]))] + 6):
+                a, i, k = SRC[(q, t + 1, "%d%d%d" % (q, t, ds[r[0]]))], 3 * r[0], 3 * len(r)
+                ts(B("dn", a, a + 2 * k - 1, 2), sub(x, i, i + k), 0.0, None, A.max)
+                if t < 2:
+                    act(B("dn", a + 1, a + 2 * k, 2), sub(ix, i, i + k), 1.0, 256.0 * q)
+            for s in ds:
+                down(t + 1, "%d%d%d" % (q, t, s))
+        tag[0] = "windows"
+        for y in WINDOWS[t::2] if t < 2 else []:
+            for a in (0, YW // 2):
+                op("S", [lambda y=y, a=a: S.activation(ap(B("ye" + y, a, a + YW // 2)), ap(B("zz", 0, YW // 2)), AF.Copy)],
+                   [B("zz"), B("pw", 80 * t + 5, 80 * t + 69)], [B("ye" + y, a, a + YW // 2)], 0.06 + cy * YW / 2)
+        return lt(q - 1)
+
+    ready, sent, seen, local, place, lists, count = set(), set(), set(), {}, {}, {}, [0]
+    Y = B("W", 0, 256)
+
+    def add(t):
+        tag[0] = "sum"
+        if t == 0:
+            act(Y, B("sg", 0, 256))
+        elif t < EV - 1 or q:
+            tt(Y if t < EV - 1 else B("ac"), Y, B("sg", 256 * t, 256 * t + 256), A.add)
+
+    def own(t, bn, d):
+        cpg(B("sg", 256 * t, 256 * t + 256), B("csb"), bn, "S")
+        en = event("EW", bn, d, B("v%d" % t), t == 0, B("xw", 80 * t + 5, 80 * t + 69)) if t < 3 else None
+        left = leavers(t, en) if t < 3 and q else None
+        for k in range(EV):
+            if k == t == 3 or k <= t == 2:
+                add(k)
+        return en, left
+
+    def energies(u, b):
+        vs = [local[(u, b)]] if (u, b) in local else []
+        for r in range(N - 1, q, -1):
+            if (q, r, u, b) in DST:
+                a, i, w = DST[(q, r, u, b)]
+                if (r, i) not in seen:
+                    seen.add((r, i))
+                    bs = [x for d, _, x in DOWN[r][i] if d == q][0].split()
+                    z = DST[(q, r, u, bs[0])][0]
+                    landed("dn%d_%d" % (r, i), w, [B("ld", z, z + 6 * len(bs))])
+                vs.append(B("ld", a, a + 5, 2))
+                place.setdefault(b, B("ld", a + 1, a + 6, 2))
+        while len(vs) > 1:
+            o = new("pf", 3)
+            tt(o, vs[0], vs[1], A.min)
+            vs = [o] + vs[2:]
+        return vs[0]
+
+    def joined(regs):
+        rs = runs(regs, lambda a, b: a[0] == b[0] and a[3] == b[3] and b[1] == a[1] + wd(a) * a[3])
+        return [(r[0][0], r[0][1], r[-1][2], r[0][3]) for r in rs]
+
+    tal = TALLY[q].split()
+
+    def batch(x, u, bl, eng):
+        bs = bl.split()
+        n, m = 3 * len(bs), CAP * len(bs)
+        tag[0] = "batch %d %s" % (u, bl)
+        one = "!%d" % u
+        straight = bs[0] + one in hb
+        rs = runs(bs, lambda a, b: hb.index(b + one) == hb.index(a + one) + 1) if straight else [bs]
+        bns, d = bins(x[0], joined([energies(u, b) for b in bs]), eng[0], None,
+                      [(3 * bs.index(r[0]), 3 * bs.index(r[-1]) + 3) for r in rs])
+        bn = bns[0]
+        if u < 3:
+            if bl not in lists:
+                lists[bl], k = new("pu", n), 0
+                for p in joined([place[b] for b in bs]):
+                    act(sub(lists[bl], k, k + wd(p)), p, 1.0, -256.0 * q)
+                    k += wd(p)
+            if u == 1:
+                v = new("pv", m)
+                ts(v, SW, 4, 4095, A.arith_shift_right, A.bitwise_and, lists[bl])
+            else:
+                v = new("pf", m)
+                cpg(v, SW, lists[bl], "S", 1.0 / 256)
+            en = event(x, bn, d, v)
+            for i, b in enumerate(bs):
+                local[(u + 1, b)] = sub(en, 3 * i, 3 * i + 3)
+            on = [b for b in bs if (q, u + 1, b) in SRC]
+            for r in runs(on, lambda a, b: SRC[(q, u + 1, b)] == SRC[(q, u + 1, a)] + 6 and bs.index(b) == bs.index(a) + 1):
+                a, i = SRC[(q, u + 1, r[0])], bs.index(r[0])
+                ts(B("dn", a, a + 6 * len(r) - 1, 2), sub(en, 3 * i, 3 * (i + len(r))), 0.0, None, A.max)
+                if u == 1:
+                    for j, b in enumerate(r):
+                        act(B("dn", a + 6 * j + 1, a + 6 * j + 6, 2), place[b])
+            for b in on:
+                down(u + 1, b)
+        if straight:
+            for r, l in zip(rs, bns):
+                a = CAP * hb.index(r[0] + one)
+                cpg(B("hs", a, a + CAP * len(r)), B("csb"), l, eng[-1])
+            done.update((b + one, u) for b in bs)
+        else:
+            a = CAP * tal.index(bs[0])
+            o = B("tal", a, a + m)
+            if any(b in began for b in bs):
+                for b in set(bs) - began:
+                    const(B("tal", CAP * tal.index(b), CAP * tal.index(b) + CAP), 0)
+                ttg(o, B("csb"), bn, o, A.add)
+            else:
+                cpg(o, B("csb"), bn, "S")
+            began.update(bs)
+            done.update((b, u) for b in bs)
+            full = [b for b in hb if b in bs and end[b] == u]
+            for r in runs(full, lambda a, b: hb.index(b) == hb.index(a) + 1 and tal.index(b) == tal.index(a) + 1):
+                k, j = CAP * hb.index(r[0]), CAP * tal.index(r[0])
+                act(B("hs", k, k + CAP * len(r)), B("tal", j, j + CAP * len(r)))
+        for i, call in enumerate(HOME[q][1]):
+            if i not in gone and all((b, end[b]) in done for _, f, c in call for b in hb[f:f + len(c)]):
+                gone.add(i)
+                parts = []
+                for h, f, c in call:
+                    z = [e[5] for e in HOMES[h] if e[:2] == (q, i)][0]
+                    parts.append((h, B("hs", CAP * f, CAP * (f + len(c))), B("hr", z, z + CAP * len(c))))
+                remote("hm%d_%d" % (q, i), parts)
+
+    began, done, gone, end, hb = set(), set(), set(), {}, HOME[q][0].split()
+    for _, u, bl, _ in BATCH[q]:
+        for b in bl.split():
+            end["%s!%d" % (b, u) if "%s!%d" % (b, u) in hb else b] = u
+    d = B("pd", 0, 64)
+    act(sub(d, 3, 64, 4), enw, 0.125, -OFFS - (EMPTY if q else 0))
+    for t in range(EV):
+        tag[0] = "own %d" % t
+        if t:
+            (bn,), d = bins("E", [en], "S", left if t < 3 else None)
+        en, left = own(t, bn, d)
+        for x, u, bl, eng in BATCH[q]:
+            if u == t + 1:
+                batch(x, u, bl, eng)
 
     def leave(h):
         lo, hi = 128 * h, 128 * h + 128
         dma("YS"[h], [lambda: (g.scalar if h else g.sync).dma_start(T.y[:, lo:hi], T.yo[:, lo:hi])], [B("yo", lo, hi)], [], 65536)
 
-    out = B("ac" if q else "yo")
-    cpg(out, sg(0), B("prm"), "S")
-    for t in range(1, EV):
-        ttg(out, sg(t), B("prm"), out, A.add)
-    if q == 0:
-        for h in range(2):
-            leave(h)
-    else:
-        sm = B("psI", 0, 256)
-        act(sm, out)
-        for s in range(q - 1, -1, -1):
-            n = 3 * (N - s)
-            landed("ri%d" % s, width(s, q, "ri"), [B("li%d" % s)])
-            landed("re%d" % s, width(s, q, "re"), [B("le%d" % s)])
-            sca(B("ye%d" % s), B("li%d" % s, 0, n), B("le%d" % s, 0, 16 * n))
-            tt(sm, sm, B("ye%d" % s, own, own + 256), A.add)
-        for s in range(q - 1, -1, -1):
-            a, n = 3 * (N - 1 - s), 3 * (q - s)
-            landed("rl%d" % s, width(s, q, "rl"), [B("ll%d" % s)])
-            sca(B("yl"), B("ll%d" % s, 0, n), B("ll%d" % s, a, a + 16 * n))
-        for h in range(2):
-            lo, hi = 128 * h, 128 * h + 128
-            tt(B("yo", lo, hi), B("psI", lo, hi), B("yl", own + lo, own + hi), A.add)
-            leave(h)
+    tag[0] = "home"
+    if q:
+        at, where = B("pw", 8, 69, 4), new("pu", 16)
+        for t in (1, 2):
+            a, b = new("pf", 16), new("pf", 16)
+            act(a, B("pw", 80 * t + 8, 80 * t + 69, 4), 1.0, 192.0 * t)
+            tt(b, at, a, A.min)
+            at = b
+        ts(where, at, 2047.0, YW - 16.0, A.add, A.min)
+        for r, i, a, ys, val, z in HOMES[q]:
+            landed("hm%d_%d" % (r, i), val, [B("hr", z, z + CAP * len(ys))])
+            for j, b in enumerate(HOME[r][0].split()[a:a + len(ys)]):
+                if ys[j] != "-":
+                    k = 192 * int(b[1]) + 64 * int(b[2])
+                    o, i = B("ye" + ys[j], k, k + CAP), B("hr", z + CAP * j, z + CAP * j + CAP)
+                    if (j + len(ys)) % 2:
+                        cp(o, i)
+                    else:
+                        act(o, i)
+        for y in WINDOWS[:-1]:
+            ttg(B("ac"), B("ye" + y), where, B("ac"), A.add)
+    for h in range(2):
+        lo, hi = 128 * h, 128 * h + 128
+        if q:
+            ttg(B("yo", lo, hi), B("ye3"), sub(where, 8 * h, 8 * h + 8), B("ac", lo, hi), A.add)
+        else:
+            tt(B("yo", lo, hi), sub(Y, lo, hi), B("sg", 768 + lo, 768 + hi), A.add)
+        leave(h)
     return ops
+
+
+ORDER = []
 
 
 def rank_program(g, core, T, topo):
     q = T.rank_of(core)
     if q is None:
         return
-    order = schedule([program(g, r, T, topo) for r in range(N)])
+    if not ORDER:
+        ORDER.extend(schedule([program(g, r, T, topo) for r in range(N)]))
+    ops = program(g, q, T, topo)
     issue, finish = tracker(g, T)
-    for o in order[q]:
-        issue(o)
+    for i in ORDER[q]:
+        issue(ops[i])
     finish()

@@ -6,11 +6,13 @@ N, CAP, EV, RES = 4, 48, 4, 16
 OFFS = 262144.0
 OUT = 65536.0
 EMPTY = 40960.0
-ZF = ("VVVVSSSS", "VVVVSSSS", "VVVVSSSS", "VVVVVSSS")
+ZF = ("SVSVSVSVSVSVSVVV",) * 4
 QUAD = 192
-CASES = ((1, 0, 1, 0, 0, 1), (1.2, 0, 1.2, 0, 0, 1), (1, 0.03, 1.3, 0, 0, 0.9), (1, 0, 1, 0.3, 0.6, 1), (0.9, 0, 0.9, -0.2, -0.3, 1),
-         (1.25, 0, 1.25, 0.3, 0.6, 1.15))
-TRIES, ROUNDS, STEP, SOME = 800, 2, 1.0, 0.1
+CASES = ((1, 0, 1, 0, 0, 0.8), (1.2, 0, 1.2, 0, 0, 0.8), (1, 0.02, 1.2, 0, 0, 0.7), (1, 0, 1, 0.3, 0.6, 1), (0.9, 0, 0.9, -0.2, -0.3, 0.9),
+         (1.25, 0, 1.25, 0.3, 0.6, 1))
+PLAN = (1.1, 0, 1.1, 0.1, 0.2, 0.8)
+SWAPS, SLACK = 25000, 0.07
+TRIES, ROUNDS, STEP, SOME = 40, 2, 1.0, 0.1
 C = dict(cyc=1.0e-3, same=0.10, cross=0.17, dissue=0.06, dlat=0.6, drate=300e3, rissue=0.8, rstart=0.4, rrow=0.02, rhop=0.6,
          rrate=60e3, first=1.4, smin=64, gg=1.5, sg=3.5)
 
@@ -18,12 +20,12 @@ BATCH = {
     3: [],
     2: [("A", 1, "302", "V"), ("B", 2, "302", "V"), ("C", 2, "312", "V"), ("D", 3, "302 312", "V"), ("A", 3, "322", "V")],
     1: [("AB", 1, "301 201", "V"), ("CD", 2, "301 201", "V"), ("AB", 2, "302 311 211", "V"), ("C", 3, "301 201", "S"),
-        ("D", 3, "302 311 211 312", "V"), ("A", 3, "321 221", "V")],
+        ("D", 3, "302 311 211", "V"), ("A", 3, "312 321 221", "V")],
     0: [("AB", 1, "300 200 100", "VS"), ("CD", 2, "300 200 100", "S"), ("XY", 2, "302 301 310", "S"), ("AB", 2, "201 210 110", "S"),
-        ("C", 3, "300 200 100", "S"), ("D", 3, "301 310 201 210 110", "V"), ("X", 3, "312 320 220 120", "S"),
+        ("C", 3, "300 200 100", "S"), ("D", 3, "301 310", "V"), ("B", 3, "201 210 110", "V"), ("X", 3, "312 320 220 120", "S"),
         ("Y", 3, "302 311 211", "V")],
 }
-TALLY = {3: "", 2: "302 312", 1: "301 201 302 311 211 312", 0: "300 200 100 302 301 310 201 210 110"}
+TALLY = {3: "", 2: "302 312", 1: "301 201 302 311 211", 0: "300 200 100 302 301 310 201 210 110"}
 DOWN = {
     3: [[(2, 1, "302")], [(1, 1, "301"), (0, 1, "300")], [(1, 2, "311")], [(2, 2, "312"), (0, 2, "310")],
         [(0, 3, "320")], [(2, 3, "322"), (1, 3, "321")]],
@@ -35,26 +37,28 @@ DOWN = {
 HOME = {
     3: ("", []),
     2: ("302 312 322!3", [[(3, 0, "003")]]),
-    1: ("301 201 302 311 312 321!3 221!3 211", [[(3, 0, "0"), (2, 1, "0")], [(3, 2, "1113")], [(2, 6, "30")]]),
+    1: ("301 201 302 311 312!3 321!3 221!3 211", [[(3, 0, "0"), (2, 1, "0")], [(3, 2, "1113")], [(2, 6, "30")]]),
     0: ("300!1 200!1 100!1 300 302 301 310 312!3 320!3 302!3 311!3 100 110 120!3 200 201 210 220!3 211!3",
         [[(3, 0, "0"), (2, 1, "0"), (1, 2, "0")], [(3, 3, "3233")], [(1, 11, "333"), (2, 14, "333")],
          [(3, 7, "3333")], [(2, 17, "33")]]),
 }
 PARTS = {3: [[((2,), "X"), ((1, 0), "A")], [((2, 1), "C"), ((0,), "B")], [((2, 1), "A"), ((0,), "X")]],
          2: [[((1, 0), "X")]] * 3, 1: [[((0,), "X")]] * 3}
+OWN = {0: "SSS", 1: "SSS", 2: "SSS", 3: "SSS"}
+SMALL = {0: "SS", 1: "SS", 2: "SS", 3: "SS"}
 YW = 592
 
 SCRATCH = {}
 for _n, _w, _t in (
         ("bmr", 512, "int32"), ("bmh", 512, "int32"), ("kt", 512, "float32"), ("hi", 512, "bfloat16"),
         ("lo", 512, "bfloat16"), ("bmp", 1024, "bfloat16"), ("win", 8224, "bfloat16"), ("one", 128, "bfloat16"),
-        ("zz", 512, "bfloat16"), ("s89", 256, "bfloat16"), ("sel", 512, "bfloat16"), ("csb", 4112, "int32"),
+        ("zz", 16, "bfloat16"), ("tn", 512, "float32"), ("sel", 512, "bfloat16"), ("csb", 4112, "int32"),
         ("lsb", 4112, "bfloat16"), ("mg4", 128, "bfloat16"), ("bk4", 128, "bfloat16"), ("lb4", 512, "bfloat16"),
         ("lb4f", 512, "float32"), ("bkf", 128, "float32"), ("bk8", 128, "float32"), ("idf", 128, "float32"),
-        ("nm", 64, "bfloat16"), ("m4", 64, "bfloat16"), ("nma", 192, "bfloat16"),
+        ("nm", 64, "bfloat16"), ("m4", 64, "bfloat16"), ("nma", 144, "bfloat16"),
         ("jm", 256, "float32"), ("dm", 256, "float32"), ("es", 32, "int32"), ("ti", 64, "float32"), ("tr", 64, "float32"),
-        ("tl", 2, "uint16"), ("ew", 80, "int32"), ("iw", 80, "int32"), ("ge", 256, "bfloat16"), ("wi", 16, "int32"),
-        ("gv", 1024, "float32"), ("gm", 256, "float32"), ("cl", 256, "float32"), ("ms", 256, "bfloat16"),
+        ("tl", 2, "uint16"), ("ew", 80, "int32"), ("iw", 16, "int32"), ("ge", 256, "bfloat16"), ("wi", 16, "int32"),
+        ("gv", 1024, "float32"), ("gm", 512, "bfloat16"), ("cl", 256, "float32"), ("ms", 256, "bfloat16"),
         ("srow", 1040, "int32"), ("v0", 256, "int32"), ("v1", 256, "int32"), ("v2", 256, "float32"),
         ("pi", 6, "int32"), ("ci", 16, "int32"), ("jcl", 16, "uint16"), ("j16", 16, "float32"), ("oh", 16, "float32"), ("ohb", 8, "bfloat16"),
         ("cc", 64, "float32"), ("mi", 160, "bfloat16"), ("idw", 160, "bfloat16"), ("sg", 1024, "float32"),
@@ -62,12 +66,11 @@ for _n, _w, _t in (
         ("nb", 128, "bfloat16"), ("nt", 128, "bfloat16"), ("nu", 128, "bfloat16"), ("bko", 128, "bfloat16"),
         ("bke", 128, "bfloat16"), ("j0", 144, "float32"), ("j1", 144, "float32"), ("j2", 144, "float32"),
         ("r16", 144, "bfloat16"), ("rm", 64, "float32"), ("de", 144, "float32"), ("pe", 432, "float32"),
-        ("xw", 240, "float32"), ("pw", 240, "float32"), ("lt", 144, "bfloat16"), ("ft", 192, "bfloat16"),
-        ("xf", 192, "bfloat16"), ("pos", 144, "float32"),
+        ("xw", 240, "float32"), ("pw", 240, "float32"), ("lt", 144, "bfloat16"), ("fx", 384, "bfloat16"), ("pos", 144, "float32"),
         ("dn", 128, "float32"), ("ld", 128, "float32"), ("tal", 432, "float32"), ("hs", 960, "uint16"), ("hr", 960, "uint16"),
         ("ac", 256, "float32"), ("ye0", YW, "float32"), ("ye1", YW, "float32"), ("ye2", YW, "float32"), ("ye3", YW, "float32"),
         ("yo", 256, "float32"),
-        ("pb", 7168, "bfloat16"), ("pf", 4096, "float32"), ("pd", 1536, "float32"), ("pu", 512, "uint16"), ("pv", 256, "int32")):
+        ("pb", 7168, "bfloat16"), ("pf", 4096, "float32"), ("pd", 1536, "float32"), ("pu", 640, "uint16"), ("pv", 256, "int32")):
     SCRATCH[_n] = ("sbuf", [128, _w], _t)
 PS = ("E", "X", "Y", "W", "A", "B", "C", "D")
 for _k in PS:
@@ -234,10 +237,17 @@ def schedule(progs):
     tags = sorted(set((rank[i], o["tag"]) for i, o in enumerate(ops)))
     tag = [tags.index((rank[i], o["tag"])) for i, o in enumerate(ops)]
     cases = []
-    for work, more, wait, issue, way2, load in CASES:
+    for work, more, wait, issue, way2, load in CASES + (PLAN,):
         t = [(o["t"] + issue if o["k"] == "send" else o["t"] * work + (more if o["k"] == "op" else 0.0), o["lag"] * load) for o in ops]
         cases.append((t, [[(j, lat + way2 if ops[j]["k"] == "send" and lat else lat * (wait if lat > 0 else load)) for j, lat in l]
                           for l in into]))
+    t, into = cases.pop()
+    ops = [dict(o, t=a, lag=b) for o, (a, b) in zip(ops, t)]
+    out = [[] for _ in range(n)]
+    for i in range(n):
+        for j, lat in into[i]:
+            out[j].append((i, lat))
+    queue = [None if o["k"] == "land" else (rank[i], o["q0"]) for i, o in enumerate(ops)]
     rng, best = numpy.random.default_rng(1), None
     for k in range(TRIES):
         pri = way
@@ -248,23 +258,75 @@ def schedule(progs):
             end, fin = arrange(ops, rank, into, out, pri, True)
             if best is None or end < best[3] + 1:
                 order = sorted(range(n), key=lambda i: (fin[i] - ops[i]["t"] - ops[i]["lag"], i))
-                mean = sum(replay(ops, rank, order, *c) for c in cases) / len(cases)
+                before = ahead(queue, order)
+                mean = sum(max(replay(order, before, *c)) for c in cases) / len(cases)
                 if best is None or mean <= best[0]:
                     best = (mean, order, pri, end)
             pri = arrange(ops, rank, out, into, fin, False)[1]
-    return [[i - base[r] for i in best[1] if rank[i] == r] for r in range(N)]
+    mean, order = best[:2]
+    now, tried, before = order, set(), ahead(queue, order)
+    fins, ends = [replay(order, before, *c) for c in cases], [i for i in range(n) if not out[i]]
+    cur = mean
+    for k in range(SWAPS):
+        c = int(rng.integers(len(cases)))
+        (t, ins), fin = cases[c], fins[c]
+        i, pairs = fin.index(max(fin)), []
+        while i is not None:
+            j, a = None, 0.0
+            for x, lat in ins[i]:
+                if fin[x] + lat > a:
+                    j, a = x, fin[x] + lat
+            b = before[i]
+            if b is not None and fin[b] - t[b][1] > a + 1e-9:
+                j = b
+                pairs.append((b, i))
+            i = j
+        pairs = [p for p in pairs if p not in tried]
+        if not pairs:
+            tried.clear()
+            continue
+        b, i = pairs[int(rng.integers(len(pairs)))]
+        tried.add((b, i))
+        while rng.random() < 0.4 and before[b] is not None:
+            b = before[b]
+        lo, hi = now.index(b), now.index(i)
+        move = {i} | set(x for x, _ in into[i])
+        for x in now[hi - 1:lo:-1]:
+            if x in move:
+                move |= set(y for y, _ in into[x]) | {before[x]}
+        if b in move:
+            continue
+        seg = now[lo:hi + 1]
+        new = now[:lo] + [x for x in seg if x in move] + [x for x in seg if x not in move] + now[hi + 1:]
+        nb = ahead(queue, new)
+        nf = [replay(new[lo:], nb, *c, list(f)) for c, f in zip(cases, fins)]
+        m = sum(max(f[x] for x in ends) for f in nf) / len(cases)
+        if m < cur + SLACK * (1 - k / SWAPS) * rng.exponential():
+            now, before, fins, cur, tried = new, nb, nf, m, {(i, b)}
+            if m < mean:
+                mean, order = m, new
+    return [[i - base[r] for i in order if rank[i] == r] for r in range(N)]
 
 
-def replay(ops, rank, order, t, into):
-    fin, free = [0.0] * len(ops), {}
+def ahead(queue, order):
+    before, last = [None] * len(queue), {}
     for i in order:
-        o = ops[i]
-        s = max([0.0] + [fin[j] + lat for j, lat in into[i]])
-        if o["k"] != "land":
-            s = max(s, free.get((rank[i], o["q0"]), 0.0))
-            free[(rank[i], o["q0"])] = s + t[i][0]
+        if queue[i]:
+            before[i] = last.get(queue[i])
+            last[queue[i]] = i
+    return before
+
+
+def replay(order, before, t, into, fin=None):
+    fin = fin or [0.0] * len(t)
+    for i in order:
+        b = before[i]
+        s = 0.0 if b is None else fin[b] - t[b][1]
+        for j, lat in into[i]:
+            if fin[j] + lat > s:
+                s = fin[j] + lat
         fin[i] = s + t[i][0] + t[i][1]
-    return max(fin)
+    return fin
 
 
 def arrange(ops, rank, into, out, pri, forward):
@@ -345,7 +407,7 @@ def program(g, q, T, topo):
     NA = N - 1 - q
     BASE = -8192.0 * q - 0.4375
     SRC, DST, HOMES = layout()
-    WINDOWS = sorted(set(y for h in HOMES[q] for y in h[3]))
+    WINDOWS = sorted(set(y for h in HOMES[q] for y in h[3]) - {"-"})
     cy = C["cyc"]
 
     def op(qq, fns, reads, writes, t, **kw):
@@ -506,7 +568,6 @@ def program(g, q, T, topo):
     iota(B("pi", 0, 1), [[0, 1]], 0, 1)
     iota(B("j16"), [[1, 16]], 0, 0)
     iota(B("jm"), [[0, 16], [1, 16]], 0, 0)
-    iota(B("ci"), [[1, 16]], 0, 0)
     iota(B("mg4"), [[16, 8], [0, 16]], 0, 0)
     iota(B("mi"), [[1, 160]], -16, 0)
     iota(B("m4"), [[0, 16], [1, 4]], 0, 0)
@@ -521,7 +582,7 @@ def program(g, q, T, topo):
     cp(B("cc", 0, 6), B("pi"))
     tt(col("g16"), col("p"), col("o"), A.subtract)
     ts(B("dm"), B("jm"), col("o"), None, A.is_equal)
-    cp(B("jcl"), B("ci"))
+    cp(B("jcl"), B("j16"))
     ts(bk, B("mg4"), col("g16"), None, A.is_equal)
     ts(B("idw"), B("mi"), col("p"), None, A.is_equal)
     act(col("o32"), col("o"), 1.0, 32.0)
@@ -533,8 +594,6 @@ def program(g, q, T, topo):
     op("V", [lambda: V.transpose(ap(B("tr")), ap(B("ti")))], [B("ti")], [B("tr")], tv(64, 1))
     cpg(B("ew", 0, 32), B("tr"), B("tl"))
     enw, sdw = B("ew", 0, 16), B("ew", 16, 32)
-    if q:
-        pass
     if NA:
         landed("sd%d" % (q + 1), 8, [B("ew", 32, 32 + 16 * NA)])
     if q:
@@ -542,37 +601,22 @@ def program(g, q, T, topo):
     fill(B("lb4"), 0.0)
     for r in range(4):
         cp(B("lb4", 129 * r, 128 * r + 128, 4), B("bk4", r, 128, 4))
-    act(B("lb4f"), B("lb4"))
     act(B("bkf"), bk)
-    iota(B("kt"), [[-32, 512]], 0, 0)
-    ts(col("even"), col("o1"), -1.0, 1.0, A.mult, A.add)
+    iota(B("kt"), [[8, 512]], 0, 0)
+    act(col("even"), col("o1"), -1.0, 1.0)
     for k in range(2):
         for j in range(2):
-            ts(M3("sel", k + 2 * j), B("idw", 16 + k - j, 144 + k - j), col(("even", "o1")[k]), None, A.mult)
+            act(M3("sel", k + 2 * j), B("idw", 16 + k - j, 144 + k - j), col(("even", "o1")[k]))
     ts(B("nm"), B("m4"), col("o4"), OFFS, A.is_equal, A.mult)
-    act(B("nma"), B("dm", 0, 192), OFFS)
+    act(B("nma"), B("dm", 0, 144), OFFS)
     tag[0] = "first bins"
-    mi0, mi1, mh0, mb0, e7 = [B("iw", 16 * k, 16 * k + 16) for k in range(5)]
     ts(B("wi"), enw, 12, 15, A.arith_shift_right, A.bitwise_and)
     ttg(B("ge"), B("wi"), B("jcl"), B("dm"), A.mult)
     mm(B("X", 0, 256), [(bk, B("ge"))])
     of0, bn = new("pu", 16), new("pu", 16)
-    ts(mi0, enw, 3, 511, A.arith_shift_right, A.bitwise_and)
-    cp(of0, mi0)
-    ts(e7, enw, 7, None, A.bitwise_and)
-    ts(B("ms"), B("X", 0, 256), col("o"), None, A.is_equal)
-    ts(B("d0"), B("m4", 0, 64), 3.0, -OFFS, A.is_equal, A.mult)
-    L, w = sums(B("gm"), "lb4f")
-    lifted("E", 256, w)
-    ttg(B("gm"), B("bmr"), of0, B("ms"), A.mult)
-    mm(B("E", 0, w), L, more=True, last=True)
-    cp(mi1, picked("E", w, B("d0"), RES))
-    ts(mh0, mi1, 31, None, A.bitwise_and)
-    ts(mb0, mi1, 5, None, A.arith_shift_right)
-    h1, h2 = new("pf", 16), new("pf", 16)
-    tt(h1, mh0, e7, A.is_le)
-    tt(h2, mb0, h1, A.add)
-    cp(bn, h2)
+    ts(B("iw"), enw, 3, 511, A.arith_shift_right, A.bitwise_and)
+    act(of0, B("iw"))
+    ts(B("ms"), B("X", 0, 256), col("o"), -0.125, A.is_equal, A.mult)
 
     def seeds(k, w, ps):
         gv = B("gv", 256 * k, 256 * k + 256)
@@ -586,31 +630,42 @@ def program(g, q, T, topo):
     ts(B("v1"), B("srow", 0, 256), 4, 4095, A.arith_shift_right, A.bitwise_and)
     act(B("v2"), B("srow", 0, 256), 1.0 / 256)
     tag[0] = "table"
-    ts(col("bb"), col("o"), -16384.0, 32.0, A.mult, A.add)
-    ts(B("bmh"), B("bmr"), 31, None, A.bitwise_and)
-    act(B("A"), B("bmh"), -5.0, col("bb"))
+    act(col("bb"), col("o"), 4096.0, -8.0)
+    act(B("bmh"), B("bmr"), 0.03125)
+    act(B("A"), B("bmh"), -40.0, col("bb"))
     tt(B("A"), B("A"), B("bmr"), A.add)
     tt(B("A"), B("A"), B("kt"), A.add)
     act(B("hi"), B("A"))
-    fill(B("csb", 4096, 4112), 0)
-    fill(B("lsb", 4096, 4112), 0.0)
+    const(B("csb", 4096, 4112), 0)
+    const(B("lsb", 4096, 4112), 0)
     tt(B("lo"), B("A"), B("hi"), A.subtract)
+    tag[0] = "first bins"
+    d = new("pd", 64)
+    const(d, 0)
+    act(sub(d, 3, 64, 4), enw, 0.125, -OFFS - (EMPTY if q else 0))
+    w = 64
+    lifted("E", 256, w)
+    for k, x in enumerate(("hi", "lo")):
+        gm = B("gm", 256 * k, 256 * k + 256)
+        ttg(gm, B(x), of0, B("ms"), A.mult)
+        mm(B("E", 0, w), sums(gm)[0], more=True, last=k == 1)
+    ts(bn, picked("E", w, d, RES), BASE + (EMPTY if q else 0), None, A.add)
+    tag[0] = "table"
     for k, ps in enumerate("BC"):
         L = [(M3("sel", k), B("hi")), (M3("sel", 2 + k), B("lo"))]
         mm(B(ps), L, 0, 1)
         mm(B(ps), L, 1)
-        act(B("bmp", 512 * k, 512 * k + 512), B(ps), 0.03125)
+        act(B("bmp", 512 * k, 512 * k + 512), B(ps), -0.125)
     ts(B("oh", 0, 8), B("j16", 0, 8), col("o8"), None, A.is_equal)
-    ts(B("ohb"), B("j16", 0, 8), col("o8"), None, A.is_equal)
+    act(B("ohb"), B("oh", 0, 8))
     for k, e in enumerate(ZF[q]):
-        w = B("win", 16 + 1024 * k, 16 + 1024 * k + 1024)
+        w, h = B("win", 16 + 512 * k, 528 + 512 * k), B("bmp", 512 * (k % 2), 512 * (k % 2) + 512)
         if e == "V":
-            ts(w, B("bmp"), B("ohb", k, k + 1), None, A.mult)
+            ts(w, h, B("ohb", k // 2, k // 2 + 1), None, A.mult)
         else:
-            act(w, B("bmp"), B("oh", k, k + 1))
+            act(w, h, B("oh", k // 2, k // 2 + 1))
     for a in (0, 8208):
-        fill(B("win", a, a + 16), OUT / 16)
-    const(new("pd", 64), 0)
+        const(B("win", a, a + 16), int(OUT) // 16)
     tag[0] = "guests' seeds"
     for r in range(q + 1, N):
         k = r - q
@@ -634,15 +689,20 @@ def program(g, q, T, topo):
         const(B("dn"), 0)
         for t in range(2):
             const(B("pe", 48 * q * t, 48 * q * (t + 1)), 0)
-        fill(B("ft"), 0.0)
-        fill(B("xf"), 0.0)
+        for s in range(q, 4):
+            act(B("fx", s, 384, 4), B("dm", 0, 96), 0.0)
 
     def lift(o, x):
         if q == 0 and x[0] != "ld":
-            y = new("pf", wd(x))
-            act(y, x, func=AF.Relu)
-            x = y
-        act(o, x, 1.0, -OFFS)
+            ts(o, x, 0.0, -OFFS, A.max, A.add)
+        else:
+            plus(o, x, -OFFS, SMALL[q][1])
+
+    def plus(o, x, c, eng):
+        if eng == "V":
+            ts(o, x, c, None, A.add)
+        else:
+            act(o, x, 1.0, c)
 
     def bins(x, pieces, eng, left=None, parts=None):
         n = sum(wd(p) for p in pieces)
@@ -709,10 +769,10 @@ def program(g, q, T, topo):
 
     def leavers(t, en):
         def ft(s):
-            return B("ft", 64 * t + s, 64 * t + 64, 4)
+            return B("fx", 128 * t + s, 128 * t + 64, 4)
 
         def xf(s):
-            return B("xf", 64 * t + s, 64 * t + 64, 4)
+            return B("fx", 128 * t + 64 + s, 128 * t + 128, 4)
 
         def lt(s):
             return B("lt", 48 * t + 16 * s, 48 * t + 16 * s + 16) if s > 0 else ft(0) if s == 0 else B("zz", 0, 16)
@@ -725,8 +785,8 @@ def program(g, q, T, topo):
             tt(ft(s), lt(s), lt(s - 1), A.subtract)
         pl, pw, cs = B("Y", 0, 64), B("pw", 80 * t + 8, 80 * t + 69), "D" if q == N - 1 else "X"
         for c in range(3):
-            mm(B(cs, 64 * c, 64 + 64 * c), [(bk, B("xf", 64 * t, 64 * t + 64))])
-        mm(pl, [(B("nu"), B("ft", 64 * t, 64 * t + 64)), (bk, B("xf", 64 * t, 64 * t + 64))])
+            mm(B(cs, 64 * c, 64 + 64 * c), [(bk, B("fx", 128 * t + 64, 128 * t + 128))])
+        mm(pl, [(B("nu"), B("fx", 128 * t, 128 * t + 64)), (bk, B("fx", 128 * t + 64, 128 * t + 128))])
         le = new("pb", CAP * q)
         for s in range(q - 1, -1, -1):
             tt(sub(le, CAP * (q - 1 - s), CAP * (q - s)), B(cs, s, 192, 4), B("j1", CAP * (N - 2 - s), CAP * (N - 1 - s)), A.is_le)
@@ -735,7 +795,7 @@ def program(g, q, T, topo):
             m, n, lo = CAP * len(ds), 3 * len(ds), CAP * (N - 2 - ds[0])
             tag[0] = "list %d %d" % (t, ds[0])
             cb, by, sel, gx, d = new("pb", m), new("pu", n), new("pb", m), new("pf", m), new("pe", m)
-            lifted(ps, 0, 2 * m if t < 2 else m)
+            lifted(ps, 0, m)
             scan(cb, B("r16", 0, m), sub(le, CAP * (q - 1 - ds[0]), CAP * (q - ds[-1])), A.mult, A.add)
             cb = sub(cb, 15, m, 16)
             ts(by, cb, 15.0, 4.0, A.min, A.mult)
@@ -743,10 +803,11 @@ def program(g, q, T, topo):
             ttg(gx, B("xw", 80 * t + 8, 80 * t + 69), by, sel, A.mult)
             if t < 2:
                 act(sub(d, 15, m, 16), cb, 16.0, -OFFS)
-                mm(B(ps, m, 2 * m), [(B("bko"), sel)], more=True)
+                lifted("Y", 0, m)
+                mm(B("Y", 0, m), [(B("bko"), sel)], more=True, last=True)
+                ix = picked("Y", m, d, n)
             mm(B(ps, 0, m), [(B("bkf"), gx)], more=True, last=True)
             x = picked(ps, m, B("de", 0, m), n)
-            ix = picked(ps, m, d, n, lo=m) if t < 2 else None
             for r in runs(range(len(ds)), lambda i, j: SRC[(q, t + 1, "%d%d%d" % (q, t, ds[j]))] == SRC[(q, t + 1, "%d%d%d" % (q, t, ds[i]))] + 6):
                 a, i, k = SRC[(q, t + 1, "%d%d%d" % (q, t, ds[r[0]]))], 3 * r[0], 3 * len(r)
                 ts(B("dn", a, a + 2 * k - 1, 2), sub(x, i, i + k), 0.0, None, A.max)
@@ -757,8 +818,8 @@ def program(g, q, T, topo):
         tag[0] = "windows"
         for y in WINDOWS[t::2] if t < 2 else []:
             for a in (0, YW // 2):
-                op("S", [lambda y=y, a=a: S.activation(ap(B("ye" + y, a, a + YW // 2)), ap(B("zz", 0, YW // 2)), AF.Copy)],
-                   [B("zz"), B("pw", 80 * t + 5, 80 * t + 69)], [B("ye" + y, a, a + YW // 2)], 0.06 + cy * YW / 2)
+                act(B("ye" + y, a, a + YW // 2), B("bmp", 0, YW // 2), 0.0)
+                ops[-1]["r"].append(pw)
         return lt(q - 1)
 
     ready, sent, seen, local, place, lists, count = set(), set(), set(), {}, {}, {}, [0]
@@ -818,7 +879,7 @@ def program(g, q, T, topo):
             if bl not in lists:
                 lists[bl], k = new("pu", n), 0
                 for p in joined([place[b] for b in bs]):
-                    act(sub(lists[bl], k, k + wd(p)), p, 1.0, -256.0 * q)
+                    plus(sub(lists[bl], k, k + wd(p)), p, -256.0 * q, SMALL[q][0])
                     k += wd(p)
             if u == 1:
                 v = new("pv", m)
@@ -871,12 +932,10 @@ def program(g, q, T, topo):
     for _, u, bl, _ in BATCH[q]:
         for b in bl.split():
             end["%s!%d" % (b, u) if "%s!%d" % (b, u) in hb else b] = u
-    d = B("pd", 0, 64)
-    act(sub(d, 3, 64, 4), enw, 0.125, -OFFS - (EMPTY if q else 0))
     for t in range(EV):
         tag[0] = "own %d" % t
         if t:
-            (bn,), d = bins("E", [en], "S", left if t < 3 else None)
+            (bn,), d = bins("E", [en], OWN[q][t - 1], left if t < 3 else None)
         en, left = own(t, bn, d)
         for x, u, bl, eng in BATCH[q]:
             if u == t + 1:
@@ -901,7 +960,7 @@ def program(g, q, T, topo):
                 if ys[j] != "-":
                     k = 192 * int(b[1]) + 64 * int(b[2])
                     o, i = B("ye" + ys[j], k, k + CAP), B("hr", z + CAP * j, z + CAP * j + CAP)
-                    if (j + len(ys)) % 2:
+                    if ys[j] == "3" and len(ys) <= 2 or (j + len(ys)) % 2:
                         cp(o, i)
                     else:
                         act(o, i)

import numpy
from concourse.bass import DstId, RemoteDMATransfer
from concourse.mybir import AluOpType as A, ActivationFunctionType as AF

N, CAP, EV, RES = 4, 48, 4, 16
OFFS = 262144.0
OUT = 65536.0
EMPTY = 40960.0
ZF = ("SVSVSVSVSVSVSVVV",) * 4
QUAD = 192
CASES = ((1, 0, 1, 0, 0, 0.8), (1.2, 0, 1.2, 0, 0, 0.8), (1, 0.02, 1.2, 0, 0, 0.7), (1, 0, 1, 0.3, 0.6, 1), (0.9, 0, 0.9, -0.2, -0.3, 0.9),
         (1.25, 0, 1.25, 0.3, 0.6, 1))
PLAN = (1.1, 0, 1.1, 0.1, 0.2, 0.8)
SWAPS, SLACK = 25000, 0.07
TRIES, ROUNDS, STEP, SOME = 40, 2, 1.0, 0.1
C = dict(cyc=1.0e-3, same=0.10, cross=0.17, dissue=0.06, dlat=0.6, drate=300e3, rissue=0.8, rstart=0.4, rrow=0.02, rhop=0.6,
         rrate=60e3, first=1.4, smin=64, gg=1.5, sg=3.5)

BATCH = {
    3: [],
    2: [("A", 1, "302", "V"), ("B", 2, "302", "V"), ("C", 2, "312", "V"), ("D", 3, "302 312", "V"), ("A", 3, "322", "V")],
    1: [("AB", 1, "301 201", "V"), ("CD", 2, "301 201", "V"), ("AB", 2, "302 311 211", "V"), ("C", 3, "301 201", "S"),
        ("D", 3, "302 311 211", "V"), ("A", 3, "312 321 221", "V")],
    0: [("AB", 1, "300 200 100", "VS"), ("CD", 2, "300 200 100", "S"), ("XY", 2, "302 301 310", "S"), ("AB", 2, "201 210 110", "S"),
        ("C", 3, "300 200 100", "S"), ("D", 3, "301 310", "V"), ("B", 3, "201 210 110", "V"), ("X", 3, "312 320 220 120", "S"),
        ("Y", 3, "302 311 211", "V")],
}
TALLY = {3: "", 2: "302 312", 1: "301 201 302 311 211", 0: "300 200 100 302 301 310 201 210 110"}
DOWN = {
    3: [[(2, 1, "302")], [(1, 1, "301"), (0, 1, "300")], [(1, 2, "311")], [(2, 2, "312"), (0, 2, "310")],
        [(0, 3, "320")], [(2, 3, "322"), (1, 3, "321")]],
    2: [[(1, 1, "201"), (0, 1, "200")], [(1, 2, "302"), (0, 2, "302")], [(1, 2, "211"), (0, 2, "210")],
        [(1, 3, "302"), (0, 3, "302")], [(1, 3, "312"), (0, 3, "312")], [(1, 3, "221"), (0, 3, "220")]],
    1: [[(0, 1, "100")], [(0, 2, "301 201")], [(0, 2, "110")], [(0, 3, "301 201")], [(0, 3, "302 311 211")], [(0, 3, "120")]],
    0: [],
}
HOME = {
    3: ("", []),
    2: ("302 312 322!3", [[(3, 0, "003")]]),
    1: ("301 201 302 311 312!3 321!3 221!3 211", [[(3, 0, "0"), (2, 1, "0")], [(3, 2, "1113")], [(2, 6, "30")]]),
    0: ("300!1 200!1 100!1 300 302 301 310 312!3 320!3 302!3 311!3 100 110 120!3 200 201 210 220!3 211!3",
        [[(3, 0, "0"), (2, 1, "0"), (1, 2, "0")], [(3, 3, "3233")], [(1, 11, "333"), (2, 14, "333")],
         [(3, 7, "3333")], [(2, 17, "33")]]),
}
PARTS = {3: [[((2,), "X"), ((1, 0), "A")], [((2, 1), "C"), ((0,), "B")], [((2, 1), "A"), ((0,), "X")]],
         2: [[((1, 0), "X")]] * 3, 1: [[((0,), "X")]] * 3}
OWN = {0: "SSS", 1: "SSS", 2: "SSS", 3: "SSS"}
SMALL = {0: "SS", 1: "SS", 2: "SS", 3: "SS"}
YW = 592

SCRATCH = {}
for _n, _w, _t in (
        ("bmr", 512, "int32"), ("bmh", 512, "int32"), ("kt", 512, "float32"), ("hi", 512, "bfloat16"),
        ("lo", 512, "bfloat16"), ("bmp", 1024, "bfloat16"), ("win", 8224, "bfloat16"), ("one", 128, "bfloat16"),
        ("zz", 16, "bfloat16"), ("tn", 512, "float32"), ("sel", 512, "bfloat16"), ("csb", 4112, "int32"),
        ("lsb", 4112, "bfloat16"), ("mg4", 128, "bfloat16"), ("bk4", 128, "bfloat16"), ("lb4", 512, "bfloat16"),
        ("lb4f", 512, "float32"), ("bkf", 128, "float32"), ("bk8", 128, "float32"), ("idf", 128, "float32"),
        ("nm", 64, "bfloat16"), ("m4", 64, "bfloat16"), ("nma", 144, "bfloat16"),
        ("jm", 256, "float32"), ("dm", 256, "float32"), ("es", 32, "int32"), ("ti", 64, "float32"), ("tr", 64, "float32"),
        ("tl", 2, "uint16"), ("ew", 80, "int32"), ("iw", 16, "int32"), ("ge", 256, "bfloat16"), ("wi", 16, "int32"),
        ("gv", 1024, "float32"), ("gm", 512, "bfloat16"), ("cl", 256, "float32"), ("ms", 256, "bfloat16"),
        ("srow", 1040, "int32"), ("v0", 256, "int32"), ("v1", 256, "int32"), ("v2", 256, "float32"),
        ("pi", 6, "int32"), ("ci", 16, "int32"), ("jcl", 16, "uint16"), ("j16", 16, "float32"), ("oh", 16, "float32"), ("ohb", 8, "bfloat16"),
        ("cc", 64, "float32"), ("mi", 160, "bfloat16"), ("idw", 160, "bfloat16"), ("sg", 1024, "float32"),
        ("mk", 256, "bfloat16"), ("d0", 64, "float32"), ("jj", 36, "float32"),
        ("nb", 128, "bfloat16"), ("nt", 128, "bfloat16"), ("nu", 128, "bfloat16"), ("bko", 128, "bfloat16"),
        ("bke", 128, "bfloat16"), ("j0", 144, "float32"), ("j1", 144, "float32"), ("j2", 144, "float32"),
        ("r16", 144, "bfloat16"), ("rm", 64, "float32"), ("de", 144, "float32"), ("pe", 432, "float32"),
        ("xw", 240, "float32"), ("pw", 240, "float32"), ("lt", 144, "bfloat16"), ("fx", 384, "bfloat16"), ("pos", 144, "float32"),
        ("dn", 128, "float32"), ("ld", 128, "float32"), ("tal", 432, "float32"), ("hs", 960, "uint16"), ("hr", 960, "uint16"),
        ("ac", 256, "float32"), ("ye0", YW, "float32"), ("ye1", YW, "float32"), ("ye2", YW, "float32"), ("ye3", YW, "float32"),
        ("yo", 256, "float32"),
        ("pb", 7168, "bfloat16"), ("pf", 4096, "float32"), ("pd", 1536, "float32"), ("pu", 640, "uint16"), ("pv", 256, "int32")):
    SCRATCH[_n] = ("sbuf", [128, _w], _t)
PS = ("E", "X", "Y", "W", "A", "B", "C", "D")
for _k in PS:
    SCRATCH[_k] = ("psum", [128, 512], "float32")

SEMAPHORES = (["cV", "cP", "cS", "cG", "snt"] + ["sd%d" % r for r in range(1, N)]
              + ["dn%d_%d" % (r, i) for r in range(N) for i in range(len(DOWN[r]))]
              + ["hm%d_%d" % (r, i) for r in range(N) for i in range(len(HOME[r][1]))]
              + ["d%d" % i for i in range(16)])


def clean(regs):
    return [(r[0], (0, 512, 1)) if r[0] in PS else (r[0], tuple(r[1:4])) for r in regs]


def meet(a, b):
    return a[0] < b[1] and b[0] < a[1] and (a[2] != b[2] or (a[0] - b[0]) % a[2] == 0)


def within(a, b):
    return b[0] <= a[0] and a[1] <= b[1] and (b[2] == 1 or (a[2] == b[2] and (a[0] - b[0]) % a[2] == 0))


def tracker(g, T):
    qs = {"V": g.vector, "P": g.tensor, "S": g.scalar, "Y": g.sync, "G": g}
    cnt, acc, nd = {}, {}, [0]
    know = {q: {} for q in qs}

    def need(q, reads, writes):
        out = []
        for kind, regs in (("r", clean(reads)), ("w", clean(writes))):
            for b, c in regs:
                for e in acc.get(b, []):
                    if meet(e[0], c):
                        if b in PS:
                            if e[2] != q or (q != "P" and "w" in (kind, e[1])):
                                out.append(e)
                        elif "w" in (kind, e[1]):
                            out.append(e)
        return out

    def wait(q, deps):
        k = know[q]
        top, imp = {}, {}
        for e in deps:
            top[e[3]] = max(top.get(e[3], 0), e[4])
            for s, v in e[5].items():
                if s != e[3]:
                    imp[s] = max(imp.get(s, 0), v)
        for s, v in top.items():
            if k.get(s, 0) >= v or imp.get(s, 0) >= v:
                continue
            qs[q].wait_ge(T.sem[s], v)
        for e in deps:
            k[e[3]] = max(k.get(e[3], 0), e[4])
            for s, v in e[5].items():
                k[s] = max(k.get(s, 0), v)

    def note(q, reads, writes, sem, val, snap):
        for kind, regs in (("r", clean(reads)), ("w", clean(writes))):
            for b, c in regs:
                l = acc.setdefault(b, [])
                if kind == "w":
                    l[:] = [e for e in l if not within(e[0], c)]
                l.append((c, kind, q, sem, val, snap))

    def issue(o):
        q, reads, writes = o["q0"], o["r"], o["w"]
        if o["k"] == "op":
            wait(q, need(q, reads, writes))
            for f in o["f"][:-1]:
                f()
            s = "c" + q
            o["f"][-1]().then_inc(T.sem[s], 1)
            cnt[s] = cnt.get(s, 0) + 1
            note(q, reads, writes, s, cnt[s], dict(know[q]))
        elif o["k"] == "dma":
            s = "d%d" % nd[0]
            nd[0] += 1
            wait(q, need(q, reads, writes))
            for f in o["f"]:
                f().then_inc(T.sem[s], 16)
            cnt[s] = 16 * len(o["f"])
            note("D", reads, writes, s, cnt[s], dict(know[q]))
        elif o["k"] == "land":
            note("R", [], writes, o["sem"], o["val"], {})
            cnt[o["sem"]] = o["val"]
        else:
            wait(q, need(q, reads, []))
            o["f"][0]()
            cnt["snt"] = cnt.get("snt", 0) + o["val"]

    def finish():
        for s, v in cnt.items():
            g.wait_ge(T.sem[s], v)

    return issue, finish


def links(ops):
    acc = {}
    for i, o in enumerate(ops):
        d, q = {}, o["q"]
        for kind, regs in (("r", clean(o["r"])), ("w", clean(o["w"]))):
            for b, c in regs:
                for e in acc.get(b, []):
                    if meet(e[0], c) and e[3] != i and not (o.get("com") == b and ops[e[3]].get("com") == b):
                        same = e[2] == q and q != "D"
                        if b in PS:
                            lat = (C["same"] if q != "P" and "w" in (kind, e[1]) else 0.0) if same else C["cross"]
                        elif "w" in (kind, e[1]):
                            lat = C["same"] if same else C["cross"]
                        else:
                            continue
                        d[e[3]] = max(d.get(e[3], 0.0), lat)
        for kind, regs in (("r", clean(o["r"])), ("w", clean(o["w"]))):
            for b, c in regs:
                l = acc.setdefault(b, [])
                if kind == "w" and o.get("com") != b:
                    l[:] = [e for e in l if not within(e[0], c)]
                l.append((c, kind, q, i))
        o["d"] = d
    sends = [i for i, o in enumerate(ops) if o["k"] == "send"]
    ops[sends[0]]["t"] += C["first"]
    for i in sends[1:]:
        ops[i]["d"].setdefault(sends[0], 0.0)
    loads = [i for i, o in enumerate(ops) if o["k"] == "dma" and o["w"] and o["q0"] == "Y"]
    for i, j in zip(loads, loads[1:]):
        ops[j]["d"][i] = -ops[i]["lag"]


def schedule(progs):
    ops, base = [], []
    for p in progs:
        links(p)
        base.append(len(ops))
        ops += p
    n = len(ops)
    rank = [r for r, p in enumerate(progs) for _ in p]
    dep, sends = [], {}
    for r, p in enumerate(progs):
        for i, o in enumerate(p):
            dep.append({base[r] + j: lat for j, lat in o["d"].items()})
            if o["k"] == "send":
                for d, rows in o["to"]:
                    lat = C["rstart"] + rows * C["rrow"] + o["by"] / C["rrate"] + C["rhop"]
                    sends.setdefault((d, o["sem"]), []).append((base[r] + i, lat))
    for i, o in enumerate(ops):
        if o["k"] == "land":
            for j, lat in sends[(rank[i], o["sem"])]:
                dep[i][j] = lat
    into = [list(d.items()) for d in dep]
    out = [[] for _ in range(n)]
    for i in range(n):
        for j, lat in into[i]:
            out[j].append((i, lat))
    left, last, way = [len(l) for l in out], [i for i in range(n) if not out[i]], [0.0] * n
    for i in last:
        way[i] = ops[i]["t"] + max([way[j] + lat for j, lat in out[i]] + [0.0])
        for j, _ in into[i]:
            left[j] -= 1
            if left[j] == 0:
                last.append(j)
    tags = sorted(set((rank[i], o["tag"]) for i, o in enumerate(ops)))
    tag = [tags.index((rank[i], o["tag"])) for i, o in enumerate(ops)]
    cases = []
    for work, more, wait, issue, way2, load in CASES + (PLAN,):
        t = [(o["t"] + issue if o["k"] == "send" else o["t"] * work + (more if o["k"] == "op" else 0.0), o["lag"] * load) for o in ops]
        cases.append((t, [[(j, lat + way2 if ops[j]["k"] == "send" and lat else lat * (wait if lat > 0 else load)) for j, lat in l]
                          for l in into]))
    t, into = cases.pop()
    ops = [dict(o, t=a, lag=b) for o, (a, b) in zip(ops, t)]
    out = [[] for _ in range(n)]
    for i in range(n):
        for j, lat in into[i]:
            out[j].append((i, lat))
    queue = [None if o["k"] == "land" else (rank[i], o["q0"]) for i, o in enumerate(ops)]
    rng, best = numpy.random.default_rng(1), None
    for k in range(TRIES):
        pri = way
        if best:
            off = (rng.normal(size=len(tags)) * STEP * (rng.random(len(tags)) < SOME)).tolist()
            pri = [p + off[k] for p, k in zip(best[2], tag)]
        for _ in range(ROUNDS if best else 10 * ROUNDS):
            end, fin = arrange(ops, rank, into, out, pri, True)
            if best is None or end < best[3] + 1:
                order = sorted(range(n), key=lambda i: (fin[i] - ops[i]["t"] - ops[i]["lag"], i))
                before = ahead(queue, order)
                mean = sum(max(replay(order, before, *c)) for c in cases) / len(cases)
                if best is None or mean <= best[0]:
                    best = (mean, order, pri, end)
            pri = arrange(ops, rank, out, into, fin, False)[1]
    mean, order = best[:2]
    now, tried, before = order, set(), ahead(queue, order)
    fins, ends = [replay(order, before, *c) for c in cases], [i for i in range(n) if not out[i]]
    cur = mean
    for k in range(SWAPS):
        c = int(rng.integers(len(cases)))
        (t, ins), fin = cases[c], fins[c]
        i, pairs = fin.index(max(fin)), []
        while i is not None:
            j, a = None, 0.0
            for x, lat in ins[i]:
                if fin[x] + lat > a:
                    j, a = x, fin[x] + lat
            b = before[i]
            if b is not None and fin[b] - t[b][1] > a + 1e-9:
                j = b
                pairs.append((b, i))
            i = j
        pairs = [p for p in pairs if p not in tried]
        if not pairs:
            tried.clear()
            continue
        b, i = pairs[int(rng.integers(len(pairs)))]
        tried.add((b, i))
        while rng.random() < 0.4 and before[b] is not None:
            b = before[b]
        lo, hi = now.index(b), now.index(i)
        move = {i} | set(x for x, _ in into[i])
        for x in now[hi - 1:lo:-1]:
            if x in move:
                move |= set(y for y, _ in into[x]) | {before[x]}
        if b in move:
            continue
        seg = now[lo:hi + 1]
        new = now[:lo] + [x for x in seg if x in move] + [x for x in seg if x not in move] + now[hi + 1:]
        nb = ahead(queue, new)
        nf = [replay(new[lo:], nb, *c, list(f)) for c, f in zip(cases, fins)]
        m = sum(max(f[x] for x in ends) for f in nf) / len(cases)
        if m < cur + SLACK * (1 - k / SWAPS) * rng.exponential():
            now, before, fins, cur, tried = new, nb, nf, m, {(i, b)}
            if m < mean:
                mean, order = m, new
    return [[i - base[r] for i in order if rank[i] == r] for r in range(N)]


def ahead(queue, order):
    before, last = [None] * len(queue), {}
    for i in order:
        if queue[i]:
            before[i] = last.get(queue[i])
            last[queue[i]] = i
    return before


def replay(order, before, t, into, fin=None):
    fin = fin or [0.0] * len(t)
    for i in order:
        b = before[i]
        s = 0.0 if b is None else fin[b] - t[b][1]
        for j, lat in into[i]:
            if fin[j] + lat > s:
                s = fin[j] + lat
        fin[i] = s + t[i][0] + t[i][1]
    return fin


def arrange(ops, rank, into, out, pri, forward):
    n = len(ops)
    deg, ready, fin, line = [len(l) for l in into], [0.0] * n, [0.0] * n, {}
    pool = sorted((pri[i], -i) for i in range(n) if not deg[i])
    while pool:
        i = -pool.pop()[1]
        o = ops[i]
        s, t = ready[i] + (0.0 if forward else o["lag"]), o["t"]
        if o["k"] != "land":
            l = line.setdefault((rank[i], o["q0"]), [])
            k = len(l)
            while k and l[k - 1][1] > s:
                k -= 1
            while k < len(l) and l[k][0] < s + t:
                s = max(s, l[k][1])
                k += 1
            l.insert(k, (s, s + t))
        fin[i] = s + t + (o["lag"] if forward else 0.0)
        for j, lat in out[i]:
            ready[j] = max(ready[j], fin[i] + lat)
            deg[j] -= 1
            if not deg[j]:
                pool.append((pri[j], -j))
                pool.sort()
    return max(fin), fin


def shares(n):
    return {1: (8,), 2: (4, 4), 3: (4, 2, 2)}[n]


def layout():
    src, dst, home = {}, {}, {r: [] for r in range(N)}
    for r in range(N):
        k = 0
        for call in DOWN[r]:
            for d, u, bl in call:
                for b in bl.split():
                    if (r, u, b) not in src:
                        src[(r, u, b)] = k
                        k += 6
    for q in range(N):
        k = 0
        for _, u, bl, _ in BATCH[q]:
            for b in bl.split():
                for r in range(N - 1, q, -1):
                    for i, call in enumerate(DOWN[r]):
                        for (d, v, bs), w in zip(call, shares(len(call))):
                            if d == q and v == u and b in bs.split() and (q, r, u, b) not in dst:
                                for x in bs.split():
                                    dst[(q, r, u, x)] = (k, i, w)
                                    k += 6
    used = [0] * N
    for r in range(N):
        for i, call in enumerate(HOME[r][1]):
            for (d, a, y), w in zip(call, shares(len(call))):
                home[d].append((r, i, a, y, w, used[d]))
                used[d] += CAP * len(y)
    return src, dst, home


def runs(items, joins):
    out = []
    for x in items:
        if out and joins(out[-1][-1], x):
            out[-1].append(x)
        else:
            out.append([x])
    return out


def program(g, q, T, topo):
    ops, cols, taken, tag, moved = [], {}, {}, ["numbers"], [0, 0]
    core = T.cores[q]
    V, P, S = g.vector, g.tensor, g.scalar
    NA = N - 1 - q
    BASE = -8192.0 * q - 0.4375
    SRC, DST, HOMES = layout()
    WINDOWS = sorted(set(y for h in HOMES[q] for y in h[3]) - {"-"})
    cy = C["cyc"]

    def op(qq, fns, reads, writes, t, **kw):
        o = dict(k="op", q=qq, q0=qq, f=fns, r=reads, w=writes, t=t, tag=tag[0], lag=0.0)
        o.update(kw)
        ops.append(o)

    def B(n, lo=0, hi=None, step=1):
        return (n, lo, SCRATCH[n][1][1] if hi is None else hi, step)

    def new(n, w):
        a = taken.get(n, 0)
        taken[n] = a + (w + 15) // 16 * 16
        assert taken[n] <= SCRATCH[n][1][1], n
        return B(n, a, a + w)

    def sub(r, lo, hi, step=1):
        return (r[0], r[1] + lo * r[3], r[1] + (hi - 1) * r[3] + 1, r[3] * step)

    def ap(r):
        if not isinstance(r, tuple):
            return r
        return T[r[0]][:, r[1]:r[2]] if r[3] == 1 else T[r[0]][:, r[1]:r[2]:r[3]]

    def wd(r):
        return (r[2] - r[1] + r[3] - 1) // r[3]

    def tv(n, f):
        return cy * max(64, n * f)

    def short(*rs):
        return all(SCRATCH[r[0]][2] in ("bfloat16", "uint16") for r in rs)

    def ts(o, i, s1, s2, op0, op1=None, by=None):
        rd = [i] + [s for s in (s1, s2, by) if isinstance(s, tuple)]
        t = 0.05 + cy * C["gg"] * wd(o) if by else tv(wd(o), 0.5 if short(o, i) else 1)
        tail = (op0,) if op1 is None else (op0, op1)
        op("V", [lambda: V.tensor_scalar(ap(o), ap(i).indirect(ap(by)) if by else ap(i), ap(s1), ap(s2), *tail)], rd, [o], t)

    def tt(o, a, b, f):
        op("V", [lambda: V.tensor_tensor(ap(o), ap(a), ap(b), f)], [a, b], [o], tv(wd(o), 1 if a[0] in PS or b[0] in PS else 2))

    def ttg(o, w, l, b, f):
        op("V", [lambda: V.tensor_tensor(ap(o), ap(w).indirect(ap(l)), ap(b), f)], [w, l, b], [o], 0.05 + cy * C["gg"] * wd(o))

    def cp(o, i):
        op("V", [lambda: V.tensor_copy(ap(o), ap(i))], [i], [o], tv(wd(o), 0.5 if short(o, i) else 1))

    def cpg(o, w, l, eng="V", scale=1.0):
        if eng == "V":
            op("V", [lambda: V.tensor_copy(ap(o), ap(w).indirect(ap(l)))], [w, l], [o], 0.05 + cy * C["gg"] * wd(o))
        else:
            op("S", [lambda: S.activation(ap(o), ap(w).indirect(ap(l)), AF.Copy, scale=scale)], [w, l], [o],
               0.065 + cy * C["gg"] * wd(o))

    def sca(w, l, i):
        op("V", [lambda: V.tensor_copy(ap(w).indirect(ap(l)), ap(i))], [l, i], [w], 0.05 + cy * C["sg"] * wd(i), com=w[0])

    def scan(o, a, b, op0, op1, init=0.0):
        op("V", [lambda: V.tensor_tensor_scan(ap(o), ap(a), ap(b), init, op0, op1)], [a, b], [o],
           tv(wd(o), 0.5 if short(o, a, b) else 1))

    def fill(o, c):
        op("V", [lambda: V.memset(ap(o), c)], [], [o], tv(wd(o), 0.5 if short(o) else 1))

    def act(o, i, scale=1.0, bias=None, func=AF.Identity, acc=None):
        t = 0.06 + cy * max(C["smin"], wd(o))
        more = [x for x in (scale, bias) if isinstance(x, tuple)]
        if acc:
            op("S", [lambda: S.activation(ap(o), ap(i), func, bias=ap(bias), scale=scale, accum_out=ap(acc))], [i] + more,
               [o, acc], t + 0.02)
        elif bias:
            op("S", [lambda: S.activation(ap(o), ap(i), func, bias=ap(bias), scale=ap(scale))], [i] + more, [o], t)
        elif more or func != AF.Identity:
            op("S", [lambda: S.activation(ap(o), ap(i), func, scale=ap(scale))], [i] + more, [o], t)
        else:
            op("S", [lambda: S.activation(ap(o), ap(i), AF.Copy, scale=scale)], [i], [o], t)

    def iota(o, pat, base, ch):
        kw = {} if SCRATCH[o[0]][2] == "int32" else {"allow_small_or_imprecise_dtypes": True}
        op("G", [lambda: g.iota(ap(o), pat, base, ch, **kw)], [], [o], 0.13 + 2 * cy * wd(o))

    def const(o, c):
        iota(o, [[0, wd(o)]], c, 0)

    def aff(o, i, pat, cmp, base, ch, other=0.0):
        op("G", [lambda: g.affine_select(ap(o), ap(i), pat, cmp, other, base, ch)], [i], [o], 0.17 + 2 * cy * wd(o))

    def mm(o, lst, a=0, b=None, more=False, last=None):
        n = len(lst)
        last = not more if last is None else last
        part = list(enumerate(lst))[a:b]
        fns = [lambda k=k, l=l, r=r: P.matmul(ap(o), ap(l), ap(r), k == 0 and not more, k == n - 1 and last)
               for k, (l, r) in part]
        t = sum(0.03 + cy * max(64, wd(r)) * (1 if short(r) else 4) for k, (l, r) in part)
        op("P", fns, [x for _, p in part for x in p], [o], t)

    def dma(qq, fns, reads, writes, by):
        moved[bool(reads)] += by
        ahead = 0.0 if reads else C["dissue"] * len([o for o in ops if o["q0"] == qq])
        op(qq, fns, reads, writes, C["dissue"], k="dma", q="D", lag=2 * C["dlat"] + moved[bool(reads)] / C["drate"] - ahead)

    def load(qq, dst, name):
        dma(qq, [lambda: (g.sync if qq == "Y" else g.scalar).dma_start(T[dst[0]][:, dst[1]:dst[2]], T[name][:, :])], [], [dst],
            128 * wd(dst) * (2 if short(dst) else 4))

    def col(name):
        if name not in cols:
            cols[name] = len(cols)
        k = cols[name]
        return B("cc", k, k + 1)

    def M3(n, k):
        return B(n, 128 * k, 128 * k + 128)

    def remote(sem, parts, shared=False, after=[]):
        w = shares(1 if shared else len(parts))

        def go():
            e = topo.engines(core, T.cores[parts[0][0]])
            ids = [DstId(rid=topo.addr(T.cores[d])[0], pnc=topo.addr(T.cores[d])[1]) for d, _, _ in parts]
            masks = [sum(1 << k for k in e[sum(w[:i]):sum(w[:i + 1])]) for i in range(len(w))]
            if shared:
                tr = [RemoteDMATransfer(dst_ids=ids, remote_sem=T.sem[sem], srcs=[ap(parts[0][1])],
                                        dsts=[ap(b) for _, _, b in parts], dma_engine_mask=masks[0])]
            else:
                tr = [RemoteDMATransfer(dst_ids=[i], remote_sem=T.sem[sem], src=ap(a), dst=ap(b), dma_engine_mask=m)
                      for i, m, (_, a, b) in zip(ids, masks, parts)]
            g.remote_dma_fused(tr, local_sem=T.sem.snt)
        op("G", [go], [x[1] for x in parts] + after, [], C["rissue"], k="send", sem=sem,
           to=[(x[0], 16 * len(parts) if shared else 128 // w[i]) for i, x in enumerate(parts)],
           by=sum(128 * wd(x[1]) * (2 if short(x[1]) else 4) for x in parts), val=sum(w))

    def landed(sem, val, regs):
        op("R", [], [], regs, 0.0, k="land", sem=sem, val=val)

    bk, idb = B("bk4"), B("idw", 16, 144)

    def sums(row, lname="lb4"):
        m = wd(row)
        if m >= QUAD:
            return [(M3(lname, r), sub(row, r, m, 4)) for r in range(4)], m // 4
        return [(bk, row)], m

    def lifted(ps, m, w):
        mm(B(ps, 0, w), [(idb, B("nm" if m >= QUAD else "nma", 0, w))], last=False)

    def picked(ps, w, d, n, o=None, lo=0):
        o = o or new("pf", w)
        scan(o, B(ps, lo, lo + w), d, A.max, A.add)
        return sub(o, w // n - 1, w, w // n)

    load("Y", B("es", 0, 16), "en")
    load("S", B("es", 16, 32), "sd")
    load("Y", B("bmr"), "bm")
    load("Y", B("csb", 0, 4096), "cs")
    load("Y", B("lsb", 0, 4096), "ls")
    iota(B("pi", 0, 1), [[0, 1]], 0, 1)
    iota(B("j16"), [[1, 16]], 0, 0)
    iota(B("jm"), [[0, 16], [1, 16]], 0, 0)
    iota(B("mg4"), [[16, 8], [0, 16]], 0, 0)
    iota(B("mi"), [[1, 160]], -16, 0)
    iota(B("m4"), [[0, 16], [1, 4]], 0, 0)
    fill(B("zz"), 0.0)
    ts(B("pi", 1, 2), B("pi", 0, 1), 15, None, A.bitwise_and)
    ts(B("pi", 2, 3), B("pi", 0, 1), 2, 3, A.arith_shift_right, A.bitwise_and)
    ts(B("pi", 3, 4), B("pi", 0, 1), 4, 1, A.arith_shift_right, A.bitwise_and)
    ts(B("pi", 4, 5), B("pi", 0, 1), 1, 7, A.arith_shift_right, A.bitwise_and)
    ts(B("pi", 5, 6), B("pi", 0, 1), 1, None, A.bitwise_and)
    for k, x in enumerate(("p", "o", "o4", "odd", "o8", "o1")):
        assert col(x)[1] == k
    cp(B("cc", 0, 6), B("pi"))
    tt(col("g16"), col("p"), col("o"), A.subtract)
    ts(B("dm"), B("jm"), col("o"), None, A.is_equal)
    cp(B("jcl"), B("j16"))
    ts(bk, B("mg4"), col("g16"), None, A.is_equal)
    ts(B("idw"), B("mi"), col("p"), None, A.is_equal)
    act(col("o32"), col("o"), 1.0, 32.0)
    ts(B("tl", 0, 1), col("odd"), 48.0, col("o"), A.mult, A.add)
    ts(B("tl", 1, 2), col("odd"), -16.0, col("o32"), A.mult, A.add)
    cp(B("ti", 0, 32), B("es"))
    act(B("ti", 32, 48), B("es", 16, 32))
    act(B("ti", 48, 64), B("es", 0, 16))
    op("V", [lambda: V.transpose(ap(B("tr")), ap(B("ti")))], [B("ti")], [B("tr")], tv(64, 1))
    cpg(B("ew", 0, 32), B("tr"), B("tl"))
    enw, sdw = B("ew", 0, 16), B("ew", 16, 32)
    if NA:
        landed("sd%d" % (q + 1), 8, [B("ew", 32, 32 + 16 * NA)])
    if q:
        remote("sd%d" % q, [(q - 1, B("ew", 16, 32 + 16 * NA), B("ew", 32, 48 + 16 * NA))])
    fill(B("lb4"), 0.0)
    for r in range(4):
        cp(B("lb4", 129 * r, 128 * r + 128, 4), B("bk4", r, 128, 4))
    act(B("bkf"), bk)
    iota(B("kt"), [[8, 512]], 0, 0)
    act(col("even"), col("o1"), -1.0, 1.0)
    for k in range(2):
        for j in range(2):
            act(M3("sel", k + 2 * j), B("idw", 16 + k - j, 144 + k - j), col(("even", "o1")[k]))
    ts(B("nm"), B("m4"), col("o4"), OFFS, A.is_equal, A.mult)
    act(B("nma"), B("dm", 0, 144), OFFS)
    tag[0] = "first bins"
    ts(B("wi"), enw, 12, 15, A.arith_shift_right, A.bitwise_and)
    ttg(B("ge"), B("wi"), B("jcl"), B("dm"), A.mult)
    mm(B("X", 0, 256), [(bk, B("ge"))])
    of0, bn = new("pu", 16), new("pu", 16)
    ts(B("iw"), enw, 3, 511, A.arith_shift_right, A.bitwise_and)
    act(of0, B("iw"))
    ts(B("ms"), B("X", 0, 256), col("o"), -0.125, A.is_equal, A.mult)

    def seeds(k, w, ps):
        gv = B("gv", 256 * k, 256 * k + 256)
        ttg(gv, w, B("jcl"), B("dm"), A.mult)
        mm(B(ps, 0, 256), [(B("bkf"), gv)])
        act(B("srow", 256 * k, 256 * k + 256), B(ps, 0, 256))

    tag[0] = "seeds"
    seeds(0, sdw, "W")
    ts(B("v0"), B("srow", 0, 256), 4095, None, A.bitwise_and)
    ts(B("v1"), B("srow", 0, 256), 4, 4095, A.arith_shift_right, A.bitwise_and)
    act(B("v2"), B("srow", 0, 256), 1.0 / 256)
    tag[0] = "table"
    act(col("bb"), col("o"), 4096.0, -8.0)
    act(B("bmh"), B("bmr"), 0.03125)
    act(B("A"), B("bmh"), -40.0, col("bb"))
    tt(B("A"), B("A"), B("bmr"), A.add)
    tt(B("A"), B("A"), B("kt"), A.add)
    act(B("hi"), B("A"))
    const(B("csb", 4096, 4112), 0)
    const(B("lsb", 4096, 4112), 0)
    tt(B("lo"), B("A"), B("hi"), A.subtract)
    tag[0] = "first bins"
    d = new("pd", 64)
    const(d, 0)
    act(sub(d, 3, 64, 4), enw, 0.125, -OFFS - (EMPTY if q else 0))
    w = 64
    lifted("E", 256, w)
    for k, x in enumerate(("hi", "lo")):
        gm = B("gm", 256 * k, 256 * k + 256)
        ttg(gm, B(x), of0, B("ms"), A.mult)
        mm(B("E", 0, w), sums(gm)[0], more=True, last=k == 1)
    ts(bn, picked("E", w, d, RES), BASE + (EMPTY if q else 0), None, A.add)
    tag[0] = "table"
    for k, ps in enumerate("BC"):
        L = [(M3("sel", k), B("hi")), (M3("sel", 2 + k), B("lo"))]
        mm(B(ps), L, 0, 1)
        mm(B(ps), L, 1)
        act(B("bmp", 512 * k, 512 * k + 512), B(ps), -0.125)
    ts(B("oh", 0, 8), B("j16", 0, 8), col("o8"), None, A.is_equal)
    act(B("ohb"), B("oh", 0, 8))
    for k, e in enumerate(ZF[q]):
        w, h = B("win", 16 + 512 * k, 528 + 512 * k), B("bmp", 512 * (k % 2), 512 * (k % 2) + 512)
        if e == "V":
            ts(w, h, B("ohb", k // 2, k // 2 + 1), None, A.mult)
        else:
            act(w, h, B("oh", k // 2, k // 2 + 1))
    for a in (0, 8208):
        const(B("win", a, a + 16), int(OUT) // 16)
    tag[0] = "guests' seeds"
    for r in range(q + 1, N):
        k = r - q
        seeds(k, B("ew", 16 * k + 16, 16 * k + 32), "DYX"[k - 1])
    SW = B("srow", 0, 256 * (NA + 1) + 16)
    if NA:
        const(B("srow", SW[2] - 16, SW[2]), 0)
    tag[0] = "more numbers"
    if q:
        act(B("nb"), bk, -1.0)
        aff(B("nt"), B("nb"), [[-1, 128]], A.is_gt, 0, 1)
        aff(B("nu"), B("nt"), [[-1, 128]], A.not_equal, 0, 1, -2048.0)
        act(B("bko"), bk, col("o"))
        iota(B("j0"), [[-64, 3], [16, 3], [0, 16]], 128, 1)
        act(col("ng"), col("g16"), -1.0)
        act(B("j1"), B("j0"), 1.0, col("ng"))
        iota(B("j2"), [[-64, 3], [1, CAP]], 129 - 2048, 0)
        act(B("r16"), B("jm", 0, 144), func=AF.Sign)
        ts(B("rm"), B("m4", 0, 64), 0.0, 4096.0, A.is_equal, A.mult)
        ts(B("de"), B("jm", 0, 144), 15.0, EMPTY - OFFS, A.is_equal, A.mult)
        const(B("dn"), 0)
        for t in range(2):
            const(B("pe", 48 * q * t, 48 * q * (t + 1)), 0)
        for s in range(q, 4):
            act(B("fx", s, 384, 4), B("dm", 0, 96), 0.0)

    def lift(o, x):
        if q == 0 and x[0] != "ld":
            ts(o, x, 0.0, -OFFS, A.max, A.add)
        else:
            plus(o, x, -OFFS, SMALL[q][1])

    def plus(o, x, c, eng):
        if eng == "V":
            ts(o, x, c, None, A.add)
        else:
            act(o, x, 1.0, c)

    def bins(x, pieces, eng, left=None, parts=None):
        n = sum(wd(p) for p in pieces)
        m = 16 * n
        of, yy = new("pu", n), new("pb", m)
        L, w = sums(yy)
        d = B("pd", 0, 64) if x == "E" else new("pd", w)
        if x != "E":
            const(d, 0)
        last, k = sub(d, w // n - 1, w, w // n), 0
        base = BASE + (EMPTY if x == "E" and q else 0)
        for p in pieces:
            if q:
                ts(sub(of, k, k + wd(p)), p, base + 16, 8208.0, A.add, A.min)
            else:
                ts(sub(of, k, k + wd(p)), p, BASE, 8192.0, A.add, A.min)
            if left:
                up = new("pf", n)
                act(up, left, OUT, -OFFS)
                tt(last, p, up, A.add)
            else:
                lift(sub(last, k, k + wd(p)), p)
            k += wd(p)
        lifted(x, m, w)
        cpg(yy, B("win") if q else B("win", 16), of, eng)
        mm(B(x, 0, w), L, more=True, last=True)
        s, out = picked(x, w, d, n), []
        for lo, hi in parts or [(0, n)]:
            out.append(new("pu", hi - lo))
            ts(out[-1], sub(s, lo, hi), base, 4096.0, A.add, A.min)
        return out, d

    def event(x, bn, d, v, first=False, out=None):
        n = wd(bn)
        m = 16 * n
        hit, row = new("pb", m), new("pb", m)
        L, w = sums(row)
        ks = B(x[-1], 256, 256 + m)
        ttg(hit, B("csb"), bn, v, A.is_le)
        mm(ks, [(bk, hit)])
        mk = ks if len(x) > 1 and not first else new("pb", m)
        ts(mk, ks, col("o"), -0.125, A.is_equal, A.mult)
        lifted(x[0], m, w)
        if first:
            ttg(row, B("lsb"), bn, mk, A.mult)
        else:
            gl = new("pb", m)
            cpg(gl, B("lsb"), bn, "S")
            tt(row, gl, mk, A.mult)
        mm(B(x[0], 0, w), L, more=True, last=True)
        return picked(x[0], w, d, n, out)

    def down(u, b):
        ready.add((u, b))
        for i, call in enumerate(DOWN[q]):
            if i not in sent and all((v, x) in ready for _, v, bs in call for x in bs.split()):
                sent.add(i)
                parts = []
                for d, v, bs in call:
                    x = bs.split()
                    a, z = SRC[(q, v, x[0])], DST[(d, q, v, x[0])][0]
                    parts.append((d, B("dn", a, a + 6 * len(x)), B("ld", z, z + 6 * len(x))))
                remote("dn%d_%d" % (q, i), parts)

    def leavers(t, en):
        def ft(s):
            return B("fx", 128 * t + s, 128 * t + 64, 4)

        def xf(s):
            return B("fx", 128 * t + 64 + s, 128 * t + 128, 4)

        def lt(s):
            return B("lt", 48 * t + 16 * s, 48 * t + 16 * s + 16) if s > 0 else ft(0) if s == 0 else B("zz", 0, 16)
        tag[0] = "flags %d" % t
        for s in range(q - 1, -1, -1):
            ts(lt(s), en, 8192.0 * (s + 1) - EMPTY, None, A.is_lt)
        for s in range(q - 1, -1, -1):
            scan(xf(s), lt(s), lt(s - 1), A.add, A.subtract, 4.0 * s)
        for s in range(1, q):
            tt(ft(s), lt(s), lt(s - 1), A.subtract)
        pl, pw, cs = B("Y", 0, 64), B("pw", 80 * t + 8, 80 * t + 69), "D" if q == N - 1 else "X"
        for c in range(3):
            mm(B(cs, 64 * c, 64 + 64 * c), [(bk, B("fx", 128 * t + 64, 128 * t + 128))])
        mm(pl, [(B("nu"), B("fx", 128 * t, 128 * t + 64)), (bk, B("fx", 128 * t + 64, 128 * t + 128))])
        le = new("pb", CAP * q)
        for s in range(q - 1, -1, -1):
            tt(sub(le, CAP * (q - 1 - s), CAP * (q - s)), B(cs, s, 192, 4), B("j1", CAP * (N - 2 - s), CAP * (N - 1 - s)), A.is_le)
        scan(B("pw", 80 * t + 5, 80 * t + 69), B("rm"), pl, A.add, A.min)
        for ds, ps in PARTS[q][t]:
            m, n, lo = CAP * len(ds), 3 * len(ds), CAP * (N - 2 - ds[0])
            tag[0] = "list %d %d" % (t, ds[0])
            cb, by, sel, gx, d = new("pb", m), new("pu", n), new("pb", m), new("pf", m), new("pe", m)
            lifted(ps, 0, m)
            scan(cb, B("r16", 0, m), sub(le, CAP * (q - 1 - ds[0]), CAP * (q - ds[-1])), A.mult, A.add)
            cb = sub(cb, 15, m, 16)
            ts(by, cb, 15.0, 4.0, A.min, A.mult)
            ttg(sel, pw, by, B("j2", lo, lo + m), A.is_equal)
            ttg(gx, B("xw", 80 * t + 8, 80 * t + 69), by, sel, A.mult)
            if t < 2:
                act(sub(d, 15, m, 16), cb, 16.0, -OFFS)
                lifted("Y", 0, m)
                mm(B("Y", 0, m), [(B("bko"), sel)], more=True, last=True)
                ix = picked("Y", m, d, n)
            mm(B(ps, 0, m), [(B("bkf"), gx)], more=True, last=True)
            x = picked(ps, m, B("de", 0, m), n)
            for r in runs(range(len(ds)), lambda i, j: SRC[(q, t + 1, "%d%d%d" % (q, t, ds[j]))] == SRC[(q, t + 1, "%d%d%d" % (q, t, ds[i]))] + 6):
                a, i, k = SRC[(q, t + 1, "%d%d%d" % (q, t, ds[r[0]]))], 3 * r[0], 3 * len(r)
                ts(B("dn", a, a + 2 * k - 1, 2), sub(x, i, i + k), 0.0, None, A.max)
                if t < 2:
                    act(B("dn", a + 1, a + 2 * k, 2), sub(ix, i, i + k), 1.0, 256.0 * q)
            for s in ds:
                down(t + 1, "%d%d%d" % (q, t, s))
        tag[0] = "windows"
        for y in WINDOWS[t::2] if t < 2 else []:
            for a in (0, YW // 2):
                act(B("ye" + y, a, a + YW // 2), B("bmp", 0, YW // 2), 0.0)
                ops[-1]["r"].append(pw)
        return lt(q - 1)

    ready, sent, seen, local, place, lists, count = set(), set(), set(), {}, {}, {}, [0]
    Y = B("W", 0, 256)

    def add(t):
        tag[0] = "sum"
        if t == 0:
            act(Y, B("sg", 0, 256))
        elif t < EV - 1 or q:
            tt(Y if t < EV - 1 else B("ac"), Y, B("sg", 256 * t, 256 * t + 256), A.add)

    def own(t, bn, d):
        cpg(B("sg", 256 * t, 256 * t + 256), B("csb"), bn, "S")
        en = event("EW", bn, d, B("v%d" % t), t == 0, B("xw", 80 * t + 5, 80 * t + 69)) if t < 3 else None
        left = leavers(t, en) if t < 3 and q else None
        for k in range(EV):
            if k == t == 3 or k <= t == 2:
                add(k)
        return en, left

    def energies(u, b):
        vs = [local[(u, b)]] if (u, b) in local else []
        for r in range(N - 1, q, -1):
            if (q, r, u, b) in DST:
                a, i, w = DST[(q, r, u, b)]
                if (r, i) not in seen:
                    seen.add((r, i))
                    bs = [x for d, _, x in DOWN[r][i] if d == q][0].split()
                    z = DST[(q, r, u, bs[0])][0]
                    landed("dn%d_%d" % (r, i), w, [B("ld", z, z + 6 * len(bs))])
                vs.append(B("ld", a, a + 5, 2))
                place.setdefault(b, B("ld", a + 1, a + 6, 2))
        while len(vs) > 1:
            o = new("pf", 3)
            tt(o, vs[0], vs[1], A.min)
            vs = [o] + vs[2:]
        return vs[0]

    def joined(regs):
        rs = runs(regs, lambda a, b: a[0] == b[0] and a[3] == b[3] and b[1] == a[1] + wd(a) * a[3])
        return [(r[0][0], r[0][1], r[-1][2], r[0][3]) for r in rs]

    tal = TALLY[q].split()

    def batch(x, u, bl, eng):
        bs = bl.split()
        n, m = 3 * len(bs), CAP * len(bs)
        tag[0] = "batch %d %s" % (u, bl)
        one = "!%d" % u
        straight = bs[0] + one in hb
        rs = runs(bs, lambda a, b: hb.index(b + one) == hb.index(a + one) + 1) if straight else [bs]
        bns, d = bins(x[0], joined([energies(u, b) for b in bs]), eng[0], None,
                      [(3 * bs.index(r[0]), 3 * bs.index(r[-1]) + 3) for r in rs])
        bn = bns[0]
        if u < 3:
            if bl not in lists:
                lists[bl], k = new("pu", n), 0
                for p in joined([place[b] for b in bs]):
                    plus(sub(lists[bl], k, k + wd(p)), p, -256.0 * q, SMALL[q][0])
                    k += wd(p)
            if u == 1:
                v = new("pv", m)
                ts(v, SW, 4, 4095, A.arith_shift_right, A.bitwise_and, lists[bl])
            else:
                v = new("pf", m)
                cpg(v, SW, lists[bl], "S", 1.0 / 256)
            en = event(x, bn, d, v)
            for i, b in enumerate(bs):
                local[(u + 1, b)] = sub(en, 3 * i, 3 * i + 3)
            on = [b for b in bs if (q, u + 1, b) in SRC]
            for r in runs(on, lambda a, b: SRC[(q, u + 1, b)] == SRC[(q, u + 1, a)] + 6 and bs.index(b) == bs.index(a) + 1):
                a, i = SRC[(q, u + 1, r[0])], bs.index(r[0])
                ts(B("dn", a, a + 6 * len(r) - 1, 2), sub(en, 3 * i, 3 * (i + len(r))), 0.0, None, A.max)
                if u == 1:
                    for j, b in enumerate(r):
                        act(B("dn", a + 6 * j + 1, a + 6 * j + 6, 2), place[b])
            for b in on:
                down(u + 1, b)
        if straight:
            for r, l in zip(rs, bns):
                a = CAP * hb.index(r[0] + one)
                cpg(B("hs", a, a + CAP * len(r)), B("csb"), l, eng[-1])
            done.update((b + one, u) for b in bs)
        else:
            a = CAP * tal.index(bs[0])
            o = B("tal", a, a + m)
            if any(b in began for b in bs):
                for b in set(bs) - began:
                    const(B("tal", CAP * tal.index(b), CAP * tal.index(b) + CAP), 0)
                ttg(o, B("csb"), bn, o, A.add)
            else:
                cpg(o, B("csb"), bn, "S")
            began.update(bs)
            done.update((b, u) for b in bs)
            full = [b for b in hb if b in bs and end[b] == u]
            for r in runs(full, lambda a, b: hb.index(b) == hb.index(a) + 1 and tal.index(b) == tal.index(a) + 1):
                k, j = CAP * hb.index(r[0]), CAP * tal.index(r[0])
                act(B("hs", k, k + CAP * len(r)), B("tal", j, j + CAP * len(r)))
        for i, call in enumerate(HOME[q][1]):
            if i not in gone and all((b, end[b]) in done for _, f, c in call for b in hb[f:f + len(c)]):
                gone.add(i)
                parts = []
                for h, f, c in call:
                    z = [e[5] for e in HOMES[h] if e[:2] == (q, i)][0]
                    parts.append((h, B("hs", CAP * f, CAP * (f + len(c))), B("hr", z, z + CAP * len(c))))
                remote("hm%d_%d" % (q, i), parts)

    began, done, gone, end, hb = set(), set(), set(), {}, HOME[q][0].split()
    for _, u, bl, _ in BATCH[q]:
        for b in bl.split():
            end["%s!%d" % (b, u) if "%s!%d" % (b, u) in hb else b] = u
    for t in range(EV):
        tag[0] = "own %d" % t
        if t:
            (bn,), d = bins("E", [en], OWN[q][t - 1], left if t < 3 else None)
        en, left = own(t, bn, d)
        for x, u, bl, eng in BATCH[q]:
            if u == t + 1:
                batch(x, u, bl, eng)

    def leave(h):
        lo, hi = 128 * h, 128 * h + 128
        dma("YS"[h], [lambda: (g.scalar if h else g.sync).dma_start(T.y[:, lo:hi], T.yo[:, lo:hi])], [B("yo", lo, hi)], [], 65536)

    tag[0] = "home"
    if q:
        at, where = B("pw", 8, 69, 4), new("pu", 16)
        for t in (1, 2):
            a, b = new("pf", 16), new("pf", 16)
            act(a, B("pw", 80 * t + 8, 80 * t + 69, 4), 1.0, 192.0 * t)
            tt(b, at, a, A.min)
            at = b
        ts(where, at, 2047.0, YW - 16.0, A.add, A.min)
        for r, i, a, ys, val, z in HOMES[q]:
            landed("hm%d_%d" % (r, i), val, [B("hr", z, z + CAP * len(ys))])
            for j, b in enumerate(HOME[r][0].split()[a:a + len(ys)]):
                if ys[j] != "-":
                    k = 192 * int(b[1]) + 64 * int(b[2])
                    o, i = B("ye" + ys[j], k, k + CAP), B("hr", z + CAP * j, z + CAP * j + CAP)
                    if ys[j] == "3" and len(ys) <= 2 or (j + len(ys)) % 2:
                        cp(o, i)
                    else:
                        act(o, i)
        for y in WINDOWS[:-1]:
            ttg(B("ac"), B("ye" + y), where, B("ac"), A.add)
    for h in range(2):
        lo, hi = 128 * h, 128 * h + 128
        if q:
            ttg(B("yo", lo, hi), B("ye3"), sub(where, 8 * h, 8 * h + 8), B("ac", lo, hi), A.add)
        else:
            tt(B("yo", lo, hi), sub(Y, lo, hi), B("sg", 768 + lo, 768 + hi), A.add)
        leave(h)
    return ops


ORDER = []


def rank_program(g, core, T, topo):
    q = T.rank_of(core)
    if q is None:
        return
    if not ORDER:
        ORDER.extend(schedule([program(g, r, T, topo) for r in range(N)]))
    ops = program(g, q, T, topo)
    issue, finish = tracker(g, T)
    for i in ORDER[q]:
        issue(ops[i])
    finish()
